import numpy as np
import ml_dtypes


def mxq(x, axis, fmt="e4m3"):
    dtype, down = {"e4m3": (ml_dtypes.float8_e4m3fn, 7), "e5m2": (ml_dtypes.float8_e5m2, 14)}[fmt]
    v = np.moveaxis(np.asarray(x, np.float32).astype(ml_dtypes.bfloat16).astype(np.float64), axis, -1)
    blocks = v.reshape(v.shape[:-1] + (-1, 32))
    amax = np.abs(blocks).max(-1, keepdims=True)
    byte = np.maximum(np.where(amax > 0, np.frexp(amax)[1] - 1 + 127, 0) - down, 1)
    scale = np.exp2(byte - 127.0)
    codes = (blocks / scale).astype(np.float32).astype(dtype).astype(np.float64)
    return np.moveaxis((codes * scale).reshape(v.shape), -1, axis)


WIDE = False


def mx_kscale(k):
    if not WIDE:
        return np.ones(k)
    levels = np.array([10, -10, 5, -5, 0])
    if k % 512:
        return np.exp2(np.random.permutation(np.resize(levels, k // 32))).repeat(32)
    a = np.empty((k // 512, 16))
    for p in range(k // 512):
        a[p, :8] = np.random.permutation(np.resize(levels, 8))
        for g in range(8):
            far = levels[np.abs(levels - a[p, g]) >= 10]
            a[p, g + 8] = far[np.random.randint(len(far))]
    return np.exp2(a.ravel()).repeat(32)


def f64(x):
    return np.asarray(x).astype(np.float64)


def striped(idx):
    return np.tile(idx.reshape(-1, 16).T, (8, 1)).astype(np.uint16)


def unstriped(offs):
    return offs[:16].T.reshape(-1).astype(np.int64)


E2M1 = np.array([0.0, 0.5, 1.0, 1.5, 2.0, 3.0, 4.0, 6.0, -0.0, -0.5, -1.0, -1.5, -2.0, -3.0, -4.0, -6.0])


def pack_weight(w, fmt):
    k, n = w.shape
    w = f64(np.asarray(w, np.float32).astype(ml_dtypes.bfloat16)).reshape(k // 32, 32, n)
    amax = np.abs(w).max(1)
    if fmt == "e4m3":
        byte = np.frexp(amax)[1] - 1 + 127 - 7
    else:
        mant, ex = np.frexp(amax / 6.0)
        byte = np.where(mant > 0.5, ex, ex - 1) + 127
    byte = np.clip(np.where(amax > 0, byte, 1), 1, 254)
    scaled = (w * np.exp2(127.0 - byte)[:, None, :]).reshape(k, n).astype(np.float32)
    by_word = np.ascontiguousarray(scaled.reshape(k // 512, 128, 4, n).transpose(0, 1, 3, 2))
    if fmt == "e4m3":
        words = by_word.astype(ml_dtypes.float8_e4m3fn).view(np.uint8)
    else:
        c = by_word.astype(ml_dtypes.float4_e2m1fn).view(np.uint8) & 0xF
        words = (c[..., 0::2] | (c[..., 1::2] << 4)).reshape(k // 512, 128, 2 * n)
    return np.ascontiguousarray(words), np.ascontiguousarray(byte.astype(np.uint8).reshape(k // 512, 16, n))


def unpack_weight(words, scales, fmt):
    g, _, n = scales.shape
    words = np.ascontiguousarray(words).reshape(g, 128, n, -1)
    if fmt == "e4m3":
        vals = words.view(ml_dtypes.float8_e4m3fn).astype(np.float64)
    else:
        nib = np.empty((g, 128, n, 4), np.uint8)
        nib[..., 0::2] = words & 0xF
        nib[..., 1::2] = words >> 4
        vals = E2M1[nib]
    vals = vals * np.repeat(np.exp2(scales.astype(np.float64) - 127.0), 8, axis=1)[..., None]
    return vals.transpose(0, 1, 3, 2).reshape(g * 512, n)


def gelu(v):
    return 0.5 * v * (1.0 + np.tanh(np.sqrt(2.0 / np.pi) * (v + 0.044715 * v**3)))


def bf(x):
    return np.asarray(x, np.float32).astype(ml_dtypes.bfloat16)


def planes(Y):
    n, m = Y.shape
    b = f64(bf(Y)).reshape(n // 32, 32, m)
    amax = np.abs(b).max(1)
    byte = np.clip(np.where(amax > 0, np.frexp(amax)[1] - 1 + 127 - 7, 1), 1, 254)
    codes = (b * np.exp2(127.0 - byte)[:, None, :]).reshape(n, m).astype(np.float32).astype(ml_dtypes.float8_e4m3fn).view(np.uint8)
    words = codes.reshape(n // 512, 128, 4, m).transpose(0, 1, 3, 2)
    return np.ascontiguousarray(words), np.ascontiguousarray(byte.astype(np.uint8).reshape(n // 512, 16, m))


K, T, S, H, T2, N = 512, 2048, 1024, 512, 2048, 512

def setup_inputs():
    n = np.random.standard_normal
    s = mx_kscale(K)[:, None]
    u = mx_kscale(H)[:, None]
    tab_words, tab_scales = pack_weight(n((K, T)) * s, "e4m3")
    tab2_words, tab2_scales = pack_weight(n((K, T)) * s, "e4m3")
    wbr_words, wbr_scales = pack_weight(n((K, H)) / np.sqrt(K) / s, "e2m1")
    wbi_words, wbi_scales = pack_weight(n((K, H)) / np.sqrt(K) / s, "e2m1")
    wsp_words, wsp_scales = pack_weight(n((K, H)) / np.sqrt(K) / s * u.T, "e4m3")
    perm = np.random.permutation(T2)
    return {
        "tab_words": tab_words, "tab_scales": tab_scales,
        "tab2_words": tab2_words, "tab2_scales": tab2_scales,
        "offs": striped(np.random.permutation(T)[:S]), "offs2": striped(np.random.permutation(T)[:S]),
        "offs3": striped(perm[:S]), "offs4": striped(perm[S:]),
        "war": (n((K, H)) / np.sqrt(K) / s * u.T).astype(np.float32),
        "wai": (n((K, H)) / np.sqrt(K) / s * u.T).astype(np.float32),
        "wbr_words": wbr_words, "wbr_scales": wbr_scales,
        "wbi_words": wbi_words, "wbi_scales": wbi_scales,
        "wsp_words": wsp_words, "wsp_scales": wsp_scales,
        "wg1": np.exp(0.3 * n((128, S))).astype(np.float32),
        "wg2": np.exp(0.3 * n((128, S))).astype(np.float32),
        "gain": np.exp(0.3 * n(H)).astype(np.float32),
        "wo": (n((H, N)) / np.sqrt(H) / u * np.exp(0.8 * n((1, N)))).astype(np.float32),
    }

def reference(tab_words, tab_scales, tab2_words, tab2_scales, offs, offs2, offs3, offs4, war, wai, wbr_words, wbr_scales, wbi_words, wbi_scales, wsp_words, wsp_scales, wg1, wg2, gain, wo):
    v = unpack_weight(tab_words, tab_scales, "e4m3")[:, unstriped(offs)]
    v2 = unpack_weight(tab2_words, tab2_scales, "e4m3")[:, unstriped(offs2)]
    ar = mxq(f64(war), 0, "e4m3").T @ v
    ai = mxq(f64(wai), 0, "e4m3").T @ v
    br = unpack_weight(wbr_words, wbr_scales, "e2m1").T @ v
    bi = unpack_weight(wbi_words, wbi_scales, "e2m1").T @ v
    h1 = ar * br - ai * bi
    h2 = unpack_weight(wsp_words, wsp_scales, "e4m3").T @ v2
    page = np.zeros((H, T2))
    page[:, unstriped(offs3)] = np.tile(f64(wg1), (H // 128, 1)) * h1
    page[:, unstriped(offs4)] = np.tile(f64(wg2), (H // 128, 1)) * h2
    z = page * f64(gain)[:, None]
    y = mxq(f64(wo), 0, "e4m3").T @ mxq(z, 0, "e4m3")
    words, scales = planes(y)
    return y, words, scales

@@ -1,0 +1,288 @@
+from contextlib import ExitStack
+
+import concourse.mybir as mybir
+from concourse.masks import make_identity
+
+K, T, S, H, T2, N = 512, 2048, 1024, 512, 2048, 512
+FLOPS = 2 * K * H * S * 5 + 2 * H * N * T2
+
+F32 = mybir.dt.float32
+BF16 = mybir.dt.bfloat16
+I32 = mybir.dt.int32
+U32 = mybir.dt.uint32
+U16 = mybir.dt.uint16
+U8 = mybir.dt.uint8
+FP8X4 = mybir.dt.float8_e4m3fn_x4
+FP4X4 = mybir.dt.float4_e2m1fn_x4
+COPY = mybir.ActivationFunctionType.Copy
+MULT = mybir.AluOpType.mult
+
+P = 128
+PACK = 4
+BANK = 512
+LIST_COLS = S // 16
+HALF = S // 2
+JT = HALF // P
+CHUNKS = (256, 256, 512, 512, 256, 256)
+
+
+def tile_list_woven_link_features_kernel(
+    tc, tab_words, tab_scales, tab2_words, tab2_scales, offs, offs2, offs3, offs4, war, wai,
+    wbr_words, wbr_scales, wbi_words, wbi_scales, wsp_words, wsp_scales, wg1, wg2, gain, wo,
+    out_0, out_1, out_2,
+):
+    nc = tc.nc
+    with ExitStack() as ctx:
+        lists = ctx.enter_context(tc.tile_pool(name="lists", bufs=1))
+        keep = ctx.enter_context(tc.tile_pool(name="keep", bufs=1))
+        big = ctx.enter_context(tc.tile_pool(name="big", bufs=7))
+        rows = ctx.enter_context(tc.tile_pool(name="rows", bufs=4))
+        half_prec = ctx.enter_context(tc.tile_pool(name="half_prec", bufs=3))
+        psum = ctx.enter_context(tc.psum_pool(name="psum", bufs=1))
+
+        def load_list(name, src):
+            tile = lists.tile([P, LIST_COLS], U16, name=name)
+            nc.sync.dma_start(tile[:], src)
+            return tile
+
+        def new_plane(name, width, engine):
+            plane = keep.tile([P, width], U8, name=name, align_bytes=64)
+            engine.memset(plane[:].bitcast(I32), 0)
+            return plane
+
+        def load_plane(plane, scales, queue):
+            for q in range(4):
+                queue.dma_start(plane[32 * q : 32 * q + 4, :].bitcast(I32), scales[0, 4 * q : 4 * q + 4, :].bitcast(I32))
+
+        def load_words8(name, words, width):
+            tile = keep.tile([P, width], I32, name=name, align_bytes=64)
+            nc.sync.dma_start(tile[:], words[0].rearrange("p c i -> p (c i)").bitcast(I32))
+            return tile
+
+        def load_words4(name, words):
+            tile = keep.tile([P, 2 * H], U8, name=name, align_bytes=64)
+            nc.sync.dma_start(tile[:].bitcast(I32), words[0].bitcast(I32))
+            return tile
+
+        def load_gate(name, wg, t):
+            tile = keep.tile([P, S], F32, name=name)
+            dealt = wg.rearrange("(p t) j -> t p j", t=PACK)
+            for q in range(4):
+                nc.sync.dma_start(tile[32 * q : 32 * q + 32, :], dealt[t])
+            return tile
+
+        def load_weight(name, w):
+            raw = big.tile([P, PACK, H], F32, name=name, tag="big")
+            nc.sync.dma_start(raw[:], w.rearrange("(p j) c -> p j c", j=PACK))
+            return raw
+
+        def quantise_weight(name, raw):
+            grouped = half_prec.tile([P, PACK * H], BF16, name=name + "_bf", tag="bf", align_bytes=64)
+            dst = grouped[:].rearrange("p (t m j) -> p t m j", t=PACK, j=PACK)
+            src = raw[:].rearrange("p j (m t) -> p t m j", t=PACK)
+            for t in range(PACK):
+                nc.scalar.copy(dst[:, t], src[:, t])
+            codes = keep.tile([P, H], U32, name=name + "_codes", align_bytes=64)
+            plane = keep.tile([P, H], U8, name=name + "_plane", align_bytes=64)
+            nc.vector.quantize_mx(codes[:].bitcast(FP8X4), plane[:], grouped[:])
+            return codes, plane
+
+        tab2_plane = new_plane("tab2_plane", T, nc.vector)
+        tab_plane = new_plane("tab_plane", T, nc.vector)
+        wsp_plane = new_plane("wsp_plane", H, nc.gpsimd)
+        wbr_plane = new_plane("wbr_plane", H, nc.gpsimd)
+        wbi_plane = new_plane("wbi_plane", H, nc.gpsimd)
+
+        list2 = load_list("list2", offs2)
+        tab2 = load_words8("tab2", tab2_words, T)
+        list1 = load_list("list1", offs)
+        list4 = load_list("list4", offs4)
+        list3 = load_list("list3", offs3)
+        wsp = load_words8("wsp", wsp_words, H)
+        wbr = load_words4("wbr", wbr_words)
+        wbi = load_words4("wbi", wbi_words)
+        load_plane(wsp_plane, wsp_scales, nc.gpsimd)
+        load_plane(tab2_plane, tab2_scales, nc.sync)
+        tab1 = load_words8("tab1", tab_words, T)
+        load_plane(tab_plane, tab_scales, nc.sync)
+        gates2 = [load_gate("gate2_%d" % t, wg2, t) for t in range(2)]
+        war_raw = load_weight("war_raw", war)
+        wai_raw = load_weight("wai_raw", wai)
+        load_plane(wbr_plane, wbr_scales, nc.sync)
+        load_plane(wbi_plane, wbi_scales, nc.sync)
+        for t in range(2, PACK):
+            gates2.append(load_gate("gate2_%d" % t, wg2, t))
+        gates1 = [load_gate("gate1_%d" % t, wg1, t) for t in range(PACK)]
+        banks = [psum.tile([P, BANK], F32, name="bank%d" % b) for b in range(8)]
+        product_banks = banks[:6]
+        turn_banks = banks[6:]
+
+        def take(ring):
+            bank = ring.pop(0)
+            ring.append(bank)
+            return bank
+
+        ident = keep.tile([P, P], F32)
+        make_identity(nc, ident[:])
+
+        def gather(name, table, plane, offsets, pieces):
+            words = keep.tile([P, S], U32, name=name + "_words", align_bytes=64)
+            scale = keep.tile([P, S], U8, name=name + "_scale", align_bytes=64)
+            nc.vector.tensor_copy(words[:], table[:].bitcast(U32).indirect(offsets[:]))
+            n, c = S // pieces, LIST_COLS // pieces
+            for i in range(pieces):
+                nc.vector.tensor_copy(scale[:, i * n : (i + 1) * n], plane[:].indirect(offsets[:, i * c : (i + 1) * c]))
+            return words, scale
+
+        def first_product(picked, jt, moving, plane):
+            bank = take(product_banks)
+            cols = slice(jt * P, (jt + 1) * P)
+            nc.tensor.matmul_mx(
+                bank[:], lhsT=picked[0][:, cols].bitcast(FP8X4), lhsT_scale=picked[1][:, cols],
+                rhs=moving, rhs_scale=plane[:], start=True, stop=True,
+            )
+            return bank
+
+        def deal_out(dst, bank, scale):
+            nc.scalar.activation(
+                dst.rearrange("p (t m) -> p t m", t=PACK), bank[:].rearrange("p (m t) -> p t m", t=PACK), COPY, scale=scale
+            )
+
+        def turn(terms, t, dst, ring=turn_banks):
+            bank = take(ring)
+            for jt in range(JT):
+                for i, term in enumerate(terms):
+                    nc.tensor.matmul(
+                        bank[:, jt * P : (jt + 1) * P], lhsT=term[:, jt, t * P : (t + 1) * P], rhs=ident[:],
+                        start=(i == 0), stop=(i == len(terms) - 1), is_transpose=True,
+                    )
+            nc.scalar.copy(dst, bank[:])
+
+        pages = [keep.tile([P, T2], F32, name="page%d" % t) for t in range(PACK)]
+
+        def scatter(t, offsets, stream, gate, pieces):
+            n, c = S // pieces, LIST_COLS // pieces
+            for i in range(pieces):
+                cols = slice(i * n, (i + 1) * n)
+                nc.vector.tensor_tensor(
+                    pages[t][:].indirect(offsets[:, i * c : (i + 1) * c]), stream[:, cols], gate[:, cols], MULT
+                )
+
+        picked2 = gather("picked2", tab2, tab2_plane, list2, 2)
+        picked1 = gather("picked1", tab1, tab_plane, list1, 1)
+        h2 = [rows.tile([P, S], F32, name="h2_%d" % t, tag="stream") for t in range(PACK)]
+        h2_turned = []
+        for half in range(2):
+            tile = big.tile([P, JT, H], F32, name="h2t_%d" % half, tag="big")
+            for jt in range(JT):
+                bank = first_product(picked2, half * JT + jt, wsp[:].bitcast(FP8X4), wsp_plane)
+                deal_out(tile[:, jt, :], bank, 1.0)
+            h2_turned.append(tile)
+            turn([tile], 0, h2[0][:, half * HALF : (half + 1) * HALF])
+        for t in range(1, PACK - 1):
+            if t == PACK - 2:
+                war_q = quantise_weight("war", war_raw)
+                wai_q = quantise_weight("wai", wai_raw)
+            for half in range(2):
+                turn([h2_turned[half]], t, h2[t][:, half * HALF : (half + 1) * HALF])
+
+        terms = []
+        for half in range(2):
+            real = big.tile([P, JT, H], F32, name="real_%d" % half, tag="big")
+            imag = big.tile([P, JT, H], F32, name="imag_%d" % half, tag="big")
+            for jt in range(JT):
+                bank = first_product(picked1, half * JT + jt, wbr[:].bitcast(FP4X4), wbr_plane)
+                deal_out(real[:, jt, :], bank, 1.0)
+                bank = first_product(picked1, half * JT + jt, wbi[:].bitcast(FP4X4), wbi_plane)
+                deal_out(imag[:, jt, :], bank, -1.0)
+            terms.append((real, imag))
+
+        for t in range(PACK - 1):
+            scatter(t, list4, h2[t], gates2[t], 2 if t == 0 else 1)
+
+        h1 = [rows.tile([P, S], F32, name="h1_%d" % t, tag="stream") for t in range(PACK)]
+        for half in range(2):
+            for jt in range(JT):
+                for (codes, plane), term in zip((war_q, wai_q), terms[half]):
+                    bank = first_product(picked1, half * JT + jt, codes[:].bitcast(FP8X4), plane)
+                    nc.vector.tensor_tensor(term[:, jt, :], bank[:], term[:, jt, :], MULT)
+            if half == 1:
+                for i in range(2):
+                    turn([h2_turned[i]], PACK - 1, h2[PACK - 1][:, i * HALF : (i + 1) * HALF], product_banks)
+                scatter(PACK - 1, list4, h2[PACK - 1], gates2[PACK - 1], 1)
+            turn(terms[half], 0, h1[0][:, half * HALF : (half + 1) * HALF])
+        for t in range(1, PACK):
+            for half in range(2):
+                turn(terms[half], t, h1[t][:, half * HALF : (half + 1) * HALF])
+
+        gains = terms[1][1][:, JT - 1, 2 * P : 2 * P + PACK]
+        nc.sync.dma_start(gains, gain.rearrange("(p t) -> p t", t=PACK))
+        wo_raw = h2_turned[0]
+        nc.sync.dma_start(wo_raw[:], wo.rearrange("(p j) c -> p j c", j=PACK))
+        wo_codes, wo_plane = quantise_weight("wo", wo_raw)
+
+        starts = [sum(CHUNKS[:c]) for c in range(len(CHUNKS))]
+        z = [keep.tile([P, w, PACK], BF16, name="z%d" % c, align_bytes=64) for c, w in enumerate(CHUNKS)]
+
+        def round_page(t, c):
+            cols = slice(starts[c], starts[c] + CHUNKS[c])
+            if t == PACK - 1:
+                nc.vector.tensor_scalar(z[c][:, :, t], pages[t][:, cols], gains[:, t : t + 1], None, MULT)
+            elif t == PACK - 2:
+                both = pages[t][:, cols].unsqueeze(2).to_broadcast([P, CHUNKS[c], 2])
+                nc.scalar.activation(z[c][:, :, t : t + 2], both, COPY, scale=gains[:, t : t + 1])
+            else:
+                nc.scalar.activation(z[c][:, :, t], pages[t][:, cols], COPY, scale=gains[:, t : t + 1])
+
+        for t in range(PACK):
+            scatter(t, list3, h1[t], gates1[t], 1)
+            if t < PACK - 1:
+                for c in range(len(CHUNKS)):
+                    round_page(t, c)
+
+        z_codes = keep.tile([P, T2], U32, align_bytes=64)
+        z_plane = keep.tile([P, T2], U8, align_bytes=64)
+        y_codes = keep.tile([P, T2], U32, align_bytes=64)
+        y_plane = keep.tile([P, T2], U8, align_bytes=64)
+        out_rows = out_0.rearrange("(p t) m -> p t m", t=PACK)
+        out_words = out_1[0].rearrange("p m t -> p (m t)").bitcast(I32)
+        last_banks = list(banks)
+        ys = {}
+
+        def last_product(c):
+            w = CHUNKS[c]
+            cols = slice(starts[c], starts[c] + w)
+            round_page(PACK - 1, c)
+            nc.vector.quantize_mx(z_codes[:, cols].bitcast(FP8X4), z_plane[:, cols], z[c][:].rearrange("p m t -> p (m t)"))
+            y = big.tile([P, PACK, w], F32, name="y%d" % c, tag="big")
+            per_bank = BANK // w
+            for b in range(PACK // per_bank):
+                bank = take(last_banks)[:].rearrange("p (i m) -> p i m", m=w)
+                for i in range(per_bank):
+                    t = b * per_bank + i
+                    nc.tensor.matmul_mx(
+                        bank[:, i, :], lhsT=wo_codes[:, t * P : (t + 1) * P].bitcast(FP8X4), lhsT_scale=wo_plane[:, t * P : (t + 1) * P],
+                        rhs=z_codes[:, cols].bitcast(FP8X4), rhs_scale=z_plane[:, cols], start=True, stop=True,
+                    )
+                dst = y[:, b * per_bank : (b + 1) * per_bank, :]
+                nc.scalar.copy(dst, bank)
+            nc.sync.dma_start(out_rows[:, :, cols], y[:])
+            ys[c] = y
+
+        def planes(c):
+            w = CHUNKS[c]
+            cols = slice(starts[c], starts[c] + w)
+            grouped = half_prec.tile([P, w, PACK], BF16, name="y_bf%d" % c, tag="bf", align_bytes=64)
+            if c == len(CHUNKS) - 1:
+                nc.scalar.copy(grouped[:], ys[c][:].rearrange("p t m -> p m t"))
+            else:
+                nc.vector.tensor_copy(grouped[:], ys[c][:].rearrange("p t m -> p m t"))
+            nc.vector.quantize_mx(y_codes[:, cols].bitcast(FP8X4), y_plane[:, cols], grouped[:].rearrange("p m t -> p (m t)"))
+            nc.sync.dma_start(out_words[:, cols], y_codes[:, cols].bitcast(I32))
+
+        for c in range(len(CHUNKS)):
+            last_product(c)
+        for c in range(len(CHUNKS)):
+            planes(c)
+        for q in range(4):
+            (nc.scalar, nc.sync)[q % 2].dma_start(out_2[0, 4 * q : 4 * q + 4, :].bitcast(I32), y_plane[32 * q : 32 * q + 4, :].bitcast(I32))

@@ -19,11 +19,17 @@ MULT = mybir.AluOpType.mult
 
 P = 128
 PACK = 4
+LAST = PACK - 1
+QUADRANTS = 4
+QUADRANT = P // QUADRANTS
+SCALE_ROWS = 4
 BANK = 512
 LIST_COLS = S // 16
 HALF = S // 2
-JT = HALF // P
+LINK_TILES = HALF // P
+PRODUCT_BANKS = 6
 CHUNKS = (256, 256, 512, 512, 256, 256)
+CODE_STORE = 512
 
 
 def tile_list_woven_link_features_kernel(
@@ -36,50 +42,59 @@ def tile_list_woven_link_features_kernel(
         lists = ctx.enter_context(tc.tile_pool(name="lists", bufs=1))
         keep = ctx.enter_context(tc.tile_pool(name="keep", bufs=1))
         big = ctx.enter_context(tc.tile_pool(name="big", bufs=7))
-        rows = ctx.enter_context(tc.tile_pool(name="rows", bufs=4))
-        half_prec = ctx.enter_context(tc.tile_pool(name="half_prec", bufs=3))
+        streams = ctx.enter_context(tc.tile_pool(name="streams", bufs=PACK))
+        rounded = ctx.enter_context(tc.tile_pool(name="rounded", bufs=3))
         psum = ctx.enter_context(tc.psum_pool(name="psum", bufs=1))
 
-        def load_list(name, src):
+        def load_list(name, offsets):
             tile = lists.tile([P, LIST_COLS], U16, name=name)
-            nc.sync.dma_start(tile[:], src)
+            nc.sync.dma_start(tile[:], offsets)
             return tile
 
-        def new_plane(name, width, engine):
+        def zeroed_plane(name, width, engine):
             plane = keep.tile([P, width], U8, name=name, align_bytes=64)
             engine.memset(plane[:].bitcast(I32), 0)
             return plane
 
-        def load_plane(plane, scales, queue):
-            for q in range(4):
-                queue.dma_start(plane[32 * q : 32 * q + 4, :].bitcast(I32), scales[0, 4 * q : 4 * q + 4, :].bitcast(I32))
+        def plane_rows(plane, q):
+            return plane[QUADRANT * q : QUADRANT * q + SCALE_ROWS, :].bitcast(I32)
 
-        def load_words8(name, words, width):
+        def scale_rows(scales, q):
+            return scales[0, SCALE_ROWS * q : SCALE_ROWS * (q + 1), :].bitcast(I32)
+
+        def load_plane(plane, scales, queue):
+            for q in range(QUADRANTS):
+                queue.dma_start(plane_rows(plane, q), scale_rows(scales, q))
+
+        def load_e4m3_words(name, words, width):
             tile = keep.tile([P, width], I32, name=name, align_bytes=64)
             nc.sync.dma_start(tile[:], words[0].rearrange("p c i -> p (c i)").bitcast(I32))
             return tile
 
-        def load_words4(name, words):
+        def load_e2m1_words(name, words):
             tile = keep.tile([P, 2 * H], U8, name=name, align_bytes=64)
             nc.sync.dma_start(tile[:].bitcast(I32), words[0].bitcast(I32))
             return tile
 
         def load_gate(name, wg, t):
             tile = keep.tile([P, S], F32, name=name)
-            dealt = wg.rearrange("(p t) j -> t p j", t=PACK)
-            for q in range(4):
-                nc.sync.dma_start(tile[32 * q : 32 * q + 32, :], dealt[t])
+            rows_of_slice = wg.rearrange("(p t) j -> t p j", t=PACK)[t]
+            for q in range(QUADRANTS):
+                nc.sync.dma_start(tile[QUADRANT * q : QUADRANT * (q + 1), :], rows_of_slice)
             return tile
+
+        def fill_weight(raw, w):
+            nc.sync.dma_start(raw[:], w.rearrange("(p i) c -> p i c", i=PACK))
 
         def load_weight(name, w):
             raw = big.tile([P, PACK, H], F32, name=name, tag="big")
-            nc.sync.dma_start(raw[:], w.rearrange("(p j) c -> p j c", j=PACK))
+            fill_weight(raw, w)
             return raw
 
         def quantise_weight(name, raw):
-            grouped = half_prec.tile([P, PACK * H], BF16, name=name + "_bf", tag="bf", align_bytes=64)
-            dst = grouped[:].rearrange("p (t m j) -> p t m j", t=PACK, j=PACK)
-            src = raw[:].rearrange("p j (m t) -> p t m j", t=PACK)
+            grouped = rounded.tile([P, PACK * H], BF16, name=name + "_bf", tag="bf", align_bytes=64)
+            dst = grouped[:].rearrange("p (t m i) -> p t m i", t=PACK, i=PACK)
+            src = raw[:].rearrange("p i (m t) -> p t m i", t=PACK)
             for t in range(PACK):
                 nc.scalar.copy(dst[:, t], src[:, t])
             codes = keep.tile([P, H], U32, name=name + "_codes", align_bytes=64)
@@ -87,35 +102,35 @@ def tile_list_woven_link_features_kernel(
             nc.vector.quantize_mx(codes[:].bitcast(FP8X4), plane[:], grouped[:])
             return codes, plane
 
-        tab2_plane = new_plane("tab2_plane", T, nc.vector)
-        tab_plane = new_plane("tab_plane", T, nc.vector)
-        wsp_plane = new_plane("wsp_plane", H, nc.gpsimd)
-        wbr_plane = new_plane("wbr_plane", H, nc.gpsimd)
-        wbi_plane = new_plane("wbi_plane", H, nc.gpsimd)
+        tab2_plane = zeroed_plane("tab2_plane", T, nc.vector)
+        tab_plane = zeroed_plane("tab_plane", T, nc.vector)
+        wsp_plane = zeroed_plane("wsp_plane", H, nc.gpsimd)
+        wbr_plane = zeroed_plane("wbr_plane", H, nc.gpsimd)
+        wbi_plane = zeroed_plane("wbi_plane", H, nc.gpsimd)
 
         list2 = load_list("list2", offs2)
-        tab2 = load_words8("tab2", tab2_words, T)
         list1 = load_list("list1", offs)
         list4 = load_list("list4", offs4)
         list3 = load_list("list3", offs3)
-        wsp = load_words8("wsp", wsp_words, H)
-        wbr = load_words4("wbr", wbr_words)
-        wbi = load_words4("wbi", wbi_words)
+        tab2 = load_e4m3_words("tab2", tab2_words, T)
+        wsp = load_e4m3_words("wsp", wsp_words, H)
+        wbr = load_e2m1_words("wbr", wbr_words)
+        wbi = load_e2m1_words("wbi", wbi_words)
         load_plane(wsp_plane, wsp_scales, nc.gpsimd)
         load_plane(tab2_plane, tab2_scales, nc.sync)
-        tab1 = load_words8("tab1", tab_words, T)
+        tab1 = load_e4m3_words("tab1", tab_words, T)
         load_plane(tab_plane, tab_scales, nc.sync)
-        gates2 = [load_gate("gate2_%d" % t, wg2, t) for t in range(2)]
+        gates2 = [load_gate("gate2_%d" % t, wg2, t) for t in range(PACK // 2)]
         war_raw = load_weight("war_raw", war)
         wai_raw = load_weight("wai_raw", wai)
         load_plane(wbr_plane, wbr_scales, nc.sync)
         load_plane(wbi_plane, wbi_scales, nc.sync)
-        for t in range(2, PACK):
-            gates2.append(load_gate("gate2_%d" % t, wg2, t))
+        gates2.extend(load_gate("gate2_%d" % t, wg2, t) for t in range(PACK // 2, PACK))
         gates1 = [load_gate("gate1_%d" % t, wg1, t) for t in range(PACK)]
+
         banks = [psum.tile([P, BANK], F32, name="bank%d" % b) for b in range(8)]
-        product_banks = banks[:6]
-        turn_banks = banks[6:]
+        product_banks = banks[:PRODUCT_BANKS]
+        turn_banks = banks[PRODUCT_BANKS:]
 
         def take(ring):
             bank = ring.pop(0)
@@ -125,38 +140,39 @@ def tile_list_woven_link_features_kernel(
         ident = keep.tile([P, P], F32)
         make_identity(nc, ident[:])
 
-        def gather(name, table, plane, offsets, pieces):
+        def gather(name, table, plane, offsets, scale_pieces):
             words = keep.tile([P, S], U32, name=name + "_words", align_bytes=64)
             scale = keep.tile([P, S], U8, name=name + "_scale", align_bytes=64)
             nc.vector.tensor_copy(words[:], table[:].bitcast(U32).indirect(offsets[:]))
-            n, c = S // pieces, LIST_COLS // pieces
-            for i in range(pieces):
+            n, c = S // scale_pieces, LIST_COLS // scale_pieces
+            for i in range(scale_pieces):
                 nc.vector.tensor_copy(scale[:, i * n : (i + 1) * n], plane[:].indirect(offsets[:, i * c : (i + 1) * c]))
             return words, scale
 
-        def first_product(picked, jt, moving, plane):
+        def first_product(picked, half, lt, moving, plane):
             bank = take(product_banks)
-            cols = slice(jt * P, (jt + 1) * P)
+            first = half * HALF + lt * P
+            words, scale = picked
             nc.tensor.matmul_mx(
-                bank[:], lhsT=picked[0][:, cols].bitcast(FP8X4), lhsT_scale=picked[1][:, cols],
+                bank[:], lhsT=words[:, first : first + P].bitcast(FP8X4), lhsT_scale=scale[:, first : first + P],
                 rhs=moving, rhs_scale=plane[:], start=True, stop=True,
             )
             return bank
 
-        def deal_out(dst, bank, scale):
+        def deal_out(dst, bank, sign):
             nc.scalar.activation(
-                dst.rearrange("p (t m) -> p t m", t=PACK), bank[:].rearrange("p (m t) -> p t m", t=PACK), COPY, scale=scale
+                dst.rearrange("p (t m) -> p t m", t=PACK), bank[:].rearrange("p (m t) -> p t m", t=PACK), COPY, scale=sign
             )
 
-        def turn(terms, t, dst, ring=turn_banks):
+        def turn(terms, t, stream, half, ring):
             bank = take(ring)
-            for jt in range(JT):
+            for lt in range(LINK_TILES):
                 for i, term in enumerate(terms):
                     nc.tensor.matmul(
-                        bank[:, jt * P : (jt + 1) * P], lhsT=term[:, jt, t * P : (t + 1) * P], rhs=ident[:],
+                        bank[:, lt * P : (lt + 1) * P], lhsT=term[:, lt, t * P : (t + 1) * P], rhs=ident[:],
                         start=(i == 0), stop=(i == len(terms) - 1), is_transpose=True,
                     )
-            nc.scalar.copy(dst, bank[:])
+            nc.scalar.copy(stream[:, half * HALF : (half + 1) * HALF], bank[:])
 
         pages = [keep.tile([P, T2], F32, name="page%d" % t) for t in range(PACK)]
 
@@ -170,73 +186,74 @@ def tile_list_woven_link_features_kernel(
 
         picked2 = gather("picked2", tab2, tab2_plane, list2, 2)
         picked1 = gather("picked1", tab1, tab_plane, list1, 1)
-        h2 = [rows.tile([P, S], F32, name="h2_%d" % t, tag="stream") for t in range(PACK)]
-        h2_turned = []
+
+        h2 = [streams.tile([P, S], F32, name="h2_%d" % t, tag="stream") for t in range(PACK)]
+        h2_by_link = []
         for half in range(2):
-            tile = big.tile([P, JT, H], F32, name="h2t_%d" % half, tag="big")
-            for jt in range(JT):
-                bank = first_product(picked2, half * JT + jt, wsp[:].bitcast(FP8X4), wsp_plane)
-                deal_out(tile[:, jt, :], bank, 1.0)
-            h2_turned.append(tile)
-            turn([tile], 0, h2[0][:, half * HALF : (half + 1) * HALF])
-        for t in range(1, PACK - 1):
-            if t == PACK - 2:
-                war_q = quantise_weight("war", war_raw)
-                wai_q = quantise_weight("wai", wai_raw)
-            for half in range(2):
-                turn([h2_turned[half]], t, h2[t][:, half * HALF : (half + 1) * HALF])
+            tile = big.tile([P, LINK_TILES, H], F32, name="h2_by_link%d" % half, tag="big")
+            for lt in range(LINK_TILES):
+                deal_out(tile[:, lt, :], first_product(picked2, half, lt, wsp[:].bitcast(FP8X4), wsp_plane), 1.0)
+            h2_by_link.append(tile)
+            turn([tile], 0, h2[0], half, turn_banks)
+        for half in range(2):
+            turn([h2_by_link[half]], 1, h2[1], half, turn_banks)
+        war_q = quantise_weight("war", war_raw)
+        wai_q = quantise_weight("wai", wai_raw)
+        for half in range(2):
+            turn([h2_by_link[half]], 2, h2[2], half, turn_banks)
 
         terms = []
         for half in range(2):
-            real = big.tile([P, JT, H], F32, name="real_%d" % half, tag="big")
-            imag = big.tile([P, JT, H], F32, name="imag_%d" % half, tag="big")
-            for jt in range(JT):
-                bank = first_product(picked1, half * JT + jt, wbr[:].bitcast(FP4X4), wbr_plane)
-                deal_out(real[:, jt, :], bank, 1.0)
-                bank = first_product(picked1, half * JT + jt, wbi[:].bitcast(FP4X4), wbi_plane)
-                deal_out(imag[:, jt, :], bank, -1.0)
+            real = big.tile([P, LINK_TILES, H], F32, name="real_%d" % half, tag="big")
+            imag = big.tile([P, LINK_TILES, H], F32, name="imag_%d" % half, tag="big")
+            for lt in range(LINK_TILES):
+                deal_out(real[:, lt, :], first_product(picked1, half, lt, wbr[:].bitcast(FP4X4), wbr_plane), 1.0)
+                deal_out(imag[:, lt, :], first_product(picked1, half, lt, wbi[:].bitcast(FP4X4), wbi_plane), -1.0)
             terms.append((real, imag))
 
-        for t in range(PACK - 1):
+        for t in range(LAST):
             scatter(t, list4, h2[t], gates2[t], 2 if t == 0 else 1)
 
-        h1 = [rows.tile([P, S], F32, name="h1_%d" % t, tag="stream") for t in range(PACK)]
-        for half in range(2):
-            for jt in range(JT):
+        def multiply_terms(half):
+            for lt in range(LINK_TILES):
                 for (codes, plane), term in zip((war_q, wai_q), terms[half]):
-                    bank = first_product(picked1, half * JT + jt, codes[:].bitcast(FP8X4), plane)
-                    nc.vector.tensor_tensor(term[:, jt, :], bank[:], term[:, jt, :], MULT)
-            if half == 1:
-                for i in range(2):
-                    turn([h2_turned[i]], PACK - 1, h2[PACK - 1][:, i * HALF : (i + 1) * HALF], product_banks)
-                scatter(PACK - 1, list4, h2[PACK - 1], gates2[PACK - 1], 1)
-            turn(terms[half], 0, h1[0][:, half * HALF : (half + 1) * HALF])
+                    bank = first_product(picked1, half, lt, codes[:].bitcast(FP8X4), plane)
+                    nc.vector.tensor_tensor(term[:, lt, :], bank[:], term[:, lt, :], MULT)
+
+        h1 = [streams.tile([P, S], F32, name="h1_%d" % t, tag="stream") for t in range(PACK)]
+        multiply_terms(0)
+        turn(terms[0], 0, h1[0], 0, turn_banks)
+        multiply_terms(1)
+        for half in range(2):
+            turn([h2_by_link[half]], LAST, h2[LAST], half, product_banks)
+        scatter(LAST, list4, h2[LAST], gates2[LAST], 1)
+        turn(terms[1], 0, h1[0], 1, turn_banks)
         for t in range(1, PACK):
             for half in range(2):
-                turn(terms[half], t, h1[t][:, half * HALF : (half + 1) * HALF])
+                turn(terms[half], t, h1[t], half, turn_banks)
 
-        gains = terms[1][1][:, JT - 1, 2 * P : 2 * P + PACK]
+        gains = terms[1][1][:, LINK_TILES - 1, 2 * P : 2 * P + PACK]
         nc.sync.dma_start(gains, gain.rearrange("(p t) -> p t", t=PACK))
-        wo_raw = h2_turned[0]
-        nc.sync.dma_start(wo_raw[:], wo.rearrange("(p j) c -> p j c", j=PACK))
+        wo_raw = h2_by_link[0]
+        fill_weight(wo_raw, wo)
         wo_codes, wo_plane = quantise_weight("wo", wo_raw)
 
-        starts = [sum(CHUNKS[:c]) for c in range(len(CHUNKS))]
+        chunk_cols = [slice(sum(CHUNKS[:c]), sum(CHUNKS[: c + 1])) for c in range(len(CHUNKS))]
         z = [keep.tile([P, w, PACK], BF16, name="z%d" % c, align_bytes=64) for c, w in enumerate(CHUNKS)]
 
         def round_page(t, c):
-            cols = slice(starts[c], starts[c] + CHUNKS[c])
-            if t == PACK - 1:
-                nc.vector.tensor_scalar(z[c][:, :, t], pages[t][:, cols], gains[:, t : t + 1], None, MULT)
-            elif t == PACK - 2:
-                both = pages[t][:, cols].unsqueeze(2).to_broadcast([P, CHUNKS[c], 2])
-                nc.scalar.activation(z[c][:, :, t : t + 2], both, COPY, scale=gains[:, t : t + 1])
+            page, factor = pages[t][:, chunk_cols[c]], gains[:, t : t + 1]
+            if t == LAST:
+                nc.vector.tensor_scalar(z[c][:, :, t], page, factor, None, MULT)
+            elif t == LAST - 1:
+                twice = page.unsqueeze(2).to_broadcast([P, CHUNKS[c], 2])
+                nc.scalar.activation(z[c][:, :, t : t + 2], twice, COPY, scale=factor)
             else:
-                nc.scalar.activation(z[c][:, :, t], pages[t][:, cols], COPY, scale=gains[:, t : t + 1])
+                nc.scalar.activation(z[c][:, :, t], page, COPY, scale=factor)
 
         for t in range(PACK):
             scatter(t, list3, h1[t], gates1[t], 1)
-            if t < PACK - 1:
+            if t < LAST:
                 for c in range(len(CHUNKS)):
                     round_page(t, c)
 
@@ -246,43 +263,39 @@ def tile_list_woven_link_features_kernel(
         y_plane = keep.tile([P, T2], U8, align_bytes=64)
         out_rows = out_0.rearrange("(p t) m -> p t m", t=PACK)
         out_words = out_1[0].rearrange("p m t -> p (m t)").bitcast(I32)
-        last_banks = list(banks)
-        ys = {}
 
         def last_product(c):
-            w = CHUNKS[c]
-            cols = slice(starts[c], starts[c] + w)
-            round_page(PACK - 1, c)
+            w, cols = CHUNKS[c], chunk_cols[c]
+            round_page(LAST, c)
             nc.vector.quantize_mx(z_codes[:, cols].bitcast(FP8X4), z_plane[:, cols], z[c][:].rearrange("p m t -> p (m t)"))
             y = big.tile([P, PACK, w], F32, name="y%d" % c, tag="big")
             per_bank = BANK // w
-            for b in range(PACK // per_bank):
-                bank = take(last_banks)[:].rearrange("p (i m) -> p i m", m=w)
+            for first in range(0, PACK, per_bank):
+                bank = take(banks)[:].rearrange("p (i m) -> p i m", m=w)
                 for i in range(per_bank):
-                    t = b * per_bank + i
+                    rows = slice((first + i) * P, (first + i + 1) * P)
                     nc.tensor.matmul_mx(
-                        bank[:, i, :], lhsT=wo_codes[:, t * P : (t + 1) * P].bitcast(FP8X4), lhsT_scale=wo_plane[:, t * P : (t + 1) * P],
+                        bank[:, i, :], lhsT=wo_codes[:, rows].bitcast(FP8X4), lhsT_scale=wo_plane[:, rows],
                         rhs=z_codes[:, cols].bitcast(FP8X4), rhs_scale=z_plane[:, cols], start=True, stop=True,
                     )
-                dst = y[:, b * per_bank : (b + 1) * per_bank, :]
-                nc.scalar.copy(dst, bank)
-            nc.sync.dma_start(out_rows[:, :, cols], y[:])
-            ys[c] = y
+                nc.scalar.copy(y[:, first : first + per_bank, :], bank)
+            nc.scalar.dma_start(out_rows[:, :, cols], y[:])
+            return y
 
-        def planes(c):
-            w = CHUNKS[c]
-            cols = slice(starts[c], starts[c] + w)
-            grouped = half_prec.tile([P, w, PACK], BF16, name="y_bf%d" % c, tag="bf", align_bytes=64)
+        def store_codes(c, y):
+            w, cols = CHUNKS[c], chunk_cols[c]
+            grouped = rounded.tile([P, w, PACK], BF16, name="y_bf%d" % c, tag="bf", align_bytes=64)
             if c == len(CHUNKS) - 1:
-                nc.scalar.copy(grouped[:], ys[c][:].rearrange("p t m -> p m t"))
+                nc.scalar.copy(grouped[:], y[:].rearrange("p t m -> p m t"))
             else:
-                nc.vector.tensor_copy(grouped[:], ys[c][:].rearrange("p t m -> p m t"))
+                nc.vector.tensor_copy(grouped[:], y[:].rearrange("p t m -> p m t"))
             nc.vector.quantize_mx(y_codes[:, cols].bitcast(FP8X4), y_plane[:, cols], grouped[:].rearrange("p m t -> p (m t)"))
-            nc.sync.dma_start(out_words[:, cols], y_codes[:, cols].bitcast(I32))
+            if cols.stop % CODE_STORE == 0:
+                stored = slice(cols.stop - CODE_STORE, cols.stop)
+                nc.sync.dma_start(out_words[:, stored], y_codes[:, stored].bitcast(I32))
 
-        for c in range(len(CHUNKS)):
-            last_product(c)
-        for c in range(len(CHUNKS)):
-            planes(c)
-        for q in range(4):
-            (nc.scalar, nc.sync)[q % 2].dma_start(out_2[0, 4 * q : 4 * q + 4, :].bitcast(I32), y_plane[32 * q : 32 * q + 4, :].bitcast(I32))
+        ys = [last_product(c) for c in range(len(CHUNKS))]
+        for c, y in enumerate(ys):
+            store_codes(c, y)
+        for q in range(QUADRANTS):
+            (nc.scalar, nc.sync)[q % 2].dma_start(scale_rows(out_2, q), plane_rows(y_plane, q))

@@ -1,7 +1,6 @@
 from contextlib import ExitStack
 
 import concourse.mybir as mybir
-from concourse.masks import make_identity
 
 K, T, S, H, T2, N = 512, 2048, 1024, 512, 2048, 512
 FLOPS = 2 * K * H * S * 5 + 2 * H * N * T2
@@ -16,6 +15,7 @@ FP8X4 = mybir.dt.float8_e4m3fn_x4
 FP4X4 = mybir.dt.float4_e2m1fn_x4
 COPY = mybir.ActivationFunctionType.Copy
 MULT = mybir.AluOpType.mult
+SUB = mybir.AluOpType.subtract
 
 P = 128
 PACK = 4
@@ -26,10 +26,14 @@ SCALE_ROWS = 4
 BANK = 512
 LIST_COLS = S // 16
 HALF = S // 2
-LINK_TILES = HALF // P
-PRODUCT_BANKS = 6
 CHUNKS = (256, 256, 512, 512, 256, 256)
 CODE_STORE = 512
+SCALAR_LAST_PAGE_CHUNKS = 1
+KIB = 1024
+FACTORS = 0
+PAGES = 64 * KIB
+H2 = 96 * KIB
+Z = 112 * KIB
 
 
 def tile_list_woven_link_features_kernel(
@@ -41,10 +45,17 @@ def tile_list_woven_link_features_kernel(
     with ExitStack() as ctx:
         lists = ctx.enter_context(tc.tile_pool(name="lists", bufs=1))
         keep = ctx.enter_context(tc.tile_pool(name="keep", bufs=1))
-        big = ctx.enter_context(tc.tile_pool(name="big", bufs=7))
-        streams = ctx.enter_context(tc.tile_pool(name="streams", bufs=PACK))
-        rounded = ctx.enter_context(tc.tile_pool(name="rounded", bufs=3))
+        shared = ctx.enter_context(tc.tile_pool(name="shared", bufs=1))
         psum = ctx.enter_context(tc.psum_pool(name="psum", bufs=1))
+
+        def placed(name, shape, dtype, offset):
+            return shared.tile(shape, dtype, name=name, align_bytes=64, offset=offset)
+
+        def a_bytes(t):
+            return FACTORS + 16 * KIB * t
+
+        def b_bytes(t):
+            return a_bytes(t) + 8 * KIB
 
         def load_list(name, offsets):
             tile = lists.tile([P, LIST_COLS], U16, name=name)
@@ -66,8 +77,7 @@ def tile_list_woven_link_features_kernel(
             for q in range(QUADRANTS):
                 queue.dma_start(plane_rows(plane, q), scale_rows(scales, q))
 
-        def load_e4m3_words(name, words, width):
-            tile = keep.tile([P, width], I32, name=name, align_bytes=64)
+        def load_e4m3_words(tile, words):
             nc.sync.dma_start(tile[:], words[0].rearrange("p c i -> p (c i)").bitcast(I32))
             return tile
 
@@ -76,31 +86,32 @@ def tile_list_woven_link_features_kernel(
             nc.sync.dma_start(tile[:].bitcast(I32), words[0].bitcast(I32))
             return tile
 
-        def load_gate(name, wg, t):
-            tile = keep.tile([P, S], F32, name=name)
-            rows_of_slice = wg.rearrange("(p t) j -> t p j", t=PACK)[t]
+        def load_gates(name, wg, first, count):
+            tile = keep.tile([P, count, S], F32, name=name)
+            rows = wg.rearrange("(p t) j -> p t j", t=PACK)[:, first : first + count, :]
             for q in range(QUADRANTS):
-                nc.sync.dma_start(tile[QUADRANT * q : QUADRANT * (q + 1), :], rows_of_slice)
-            return tile
+                nc.sync.dma_start(tile[QUADRANT * q : QUADRANT * (q + 1)], rows)
+            return [tile[:, i, :] for i in range(count)]
 
-        def fill_weight(raw, w):
+        def load_weight(name, w, offset):
+            raw = placed(name, [P, PACK, H], F32, offset)
             nc.sync.dma_start(raw[:], w.rearrange("(p i) c -> p i c", i=PACK))
-
-        def load_weight(name, w):
-            raw = big.tile([P, PACK, H], F32, name=name, tag="big")
-            fill_weight(raw, w)
             return raw
 
-        def quantise_weight(name, raw):
-            grouped = rounded.tile([P, PACK * H], BF16, name=name + "_bf", tag="bf", align_bytes=64)
-            dst = grouped[:].rearrange("p (t m i) -> p t m i", t=PACK, i=PACK)
-            src = raw[:].rearrange("p i (m t) -> p t m i", t=PACK)
-            for t in range(PACK):
-                nc.scalar.copy(dst[:, t], src[:, t])
-            codes = keep.tile([P, H], U32, name=name + "_codes", align_bytes=64)
-            plane = keep.tile([P, H], U8, name=name + "_plane", align_bytes=64)
-            nc.vector.quantize_mx(codes[:].bitcast(FP8X4), plane[:], grouped[:])
-            return codes, plane
+        def round_weight(grouped, raw):
+            dst = grouped.rearrange("p (t m i) -> p m t i", t=PACK, i=PACK)
+            src = raw[:].rearrange("p i (m t) -> p m t i", t=PACK)
+            for half in range(2):
+                ms = slice(half * P // 2, (half + 1) * P // 2)
+                nc.scalar.copy(dst[:, ms], src[:, ms])
+
+        def deal(name, raw, dtype, per_column):
+            dealt = keep.tile([P, H * per_column], dtype, name=name, align_bytes=64)
+            nc.gpsimd.tensor_copy(
+                dealt[:].rearrange("p (t m b) -> p t m b", t=PACK, b=per_column),
+                raw[:].rearrange("p (m t b) -> p t m b", t=PACK, b=per_column),
+            )
+            return dealt
 
         tab2_plane = zeroed_plane("tab2_plane", T, nc.vector)
         tab_plane = zeroed_plane("tab_plane", T, nc.vector)
@@ -109,153 +120,139 @@ def tile_list_woven_link_features_kernel(
         wbi_plane = zeroed_plane("wbi_plane", H, nc.gpsimd)
 
         list2 = load_list("list2", offs2)
+        tab2 = load_e4m3_words(placed("tab2", [P, T], I32, a_bytes(LAST)), tab2_words)
+        load_plane(tab2_plane, tab2_scales, nc.sync)
+        wsp = load_e4m3_words(keep.tile([P, H], I32, name="wsp", align_bytes=64), wsp_words)
+        load_plane(wsp_plane, wsp_scales, nc.gpsimd)
         list1 = load_list("list1", offs)
+        tab1 = load_e4m3_words(placed("tab1", [P, T], I32, b_bytes(LAST)), tab_words)
+        load_plane(tab_plane, tab_scales, nc.sync)
         list4 = load_list("list4", offs4)
-        list3 = load_list("list3", offs3)
-        tab2 = load_e4m3_words("tab2", tab2_words, T)
-        wsp = load_e4m3_words("wsp", wsp_words, H)
+        gates2 = load_gates("gate2_first", wg2, 0, 1)
+        war_raw = load_weight("war_raw", war, a_bytes(0))
+        wai_raw = load_weight("wai_raw", wai, b_bytes(0))
         wbr = load_e2m1_words("wbr", wbr_words)
         wbi = load_e2m1_words("wbi", wbi_words)
-        load_plane(wsp_plane, wsp_scales, nc.gpsimd)
-        load_plane(tab2_plane, tab2_scales, nc.sync)
-        tab1 = load_e4m3_words("tab1", tab_words, T)
-        load_plane(tab_plane, tab_scales, nc.sync)
-        gates2 = [load_gate("gate2_%d" % t, wg2, t) for t in range(PACK // 2)]
-        war_raw = load_weight("war_raw", war)
-        wai_raw = load_weight("wai_raw", wai)
         load_plane(wbr_plane, wbr_scales, nc.sync)
         load_plane(wbi_plane, wbi_scales, nc.sync)
-        gates2.extend(load_gate("gate2_%d" % t, wg2, t) for t in range(PACK // 2, PACK))
-        gates1 = [load_gate("gate1_%d" % t, wg1, t) for t in range(PACK)]
+        gates2.extend(load_gates("gate2_rest", wg2, 1, LAST))
+        list3 = load_list("list3", offs3)
+        gates1 = load_gates("gate1", wg1, 0, PACK)
+        wo_raw = load_weight("wo_raw", wo, Z)
+        gains = keep.tile([P, PACK], F32, name="gains")
+        nc.sync.dma_start(gains[:], gain.rearrange("(p t) -> p t", t=PACK))
 
         banks = [psum.tile([P, BANK], F32, name="bank%d" % b) for b in range(8)]
-        product_banks = banks[:PRODUCT_BANKS]
-        turn_banks = banks[PRODUCT_BANKS:]
 
-        def take(ring):
-            bank = ring.pop(0)
-            ring.append(bank)
+        def take():
+            bank = banks.pop(0)
+            banks.append(bank)
             return bank
 
-        ident = keep.tile([P, P], F32)
-        make_identity(nc, ident[:])
-
-        def gather(name, table, plane, offsets, scale_pieces):
+        def gather(name, table, plane, offsets, word_pieces):
             words = keep.tile([P, S], U32, name=name + "_words", align_bytes=64)
             scale = keep.tile([P, S], U8, name=name + "_scale", align_bytes=64)
-            nc.vector.tensor_copy(words[:], table[:].bitcast(U32).indirect(offsets[:]))
-            n, c = S // scale_pieces, LIST_COLS // scale_pieces
-            for i in range(scale_pieces):
-                nc.vector.tensor_copy(scale[:, i * n : (i + 1) * n], plane[:].indirect(offsets[:, i * c : (i + 1) * c]))
+            nc.vector.tensor_copy(scale[:], plane[:].indirect(offsets[:]))
+            n, c = S // word_pieces, LIST_COLS // word_pieces
+            for i in range(word_pieces):
+                nc.vector.tensor_copy(words[:, i * n : (i + 1) * n], table[:].bitcast(U32).indirect(offsets[:, i * c : (i + 1) * c]))
             return words, scale
 
-        def first_product(picked, half, lt, moving, plane):
-            bank = take(product_banks)
-            first = half * HALF + lt * P
+        def first_product(dst, weight, plane, picked):
             words, scale = picked
-            nc.tensor.matmul_mx(
-                bank[:], lhsT=words[:, first : first + P].bitcast(FP8X4), lhsT_scale=scale[:, first : first + P],
-                rhs=moving, rhs_scale=plane[:], start=True, stop=True,
-            )
-            return bank
+            for half in range(2):
+                cols = slice(half * HALF, (half + 1) * HALF)
+                bank = take()
+                nc.tensor.matmul_mx(
+                    bank[:], lhsT=weight, lhsT_scale=plane,
+                    rhs=words[:, cols].bitcast(FP8X4), rhs_scale=scale[:, cols], start=True, stop=True,
+                )
+                nc.scalar.copy(dst[:, cols], bank[:])
 
-        def deal_out(dst, bank, sign):
-            nc.scalar.activation(
-                dst.rearrange("p (t m) -> p t m", t=PACK), bank[:].rearrange("p (m t) -> p t m", t=PACK), COPY, scale=sign
-            )
+        def rows(t, first=0, width=1):
+            return slice((first + t * P) * width, (first + (t + 1) * P) * width)
 
-        def turn(terms, t, stream, half, ring):
-            bank = take(ring)
-            for lt in range(LINK_TILES):
-                for i, term in enumerate(terms):
-                    nc.tensor.matmul(
-                        bank[:, lt * P : (lt + 1) * P], lhsT=term[:, lt, t * P : (t + 1) * P], rhs=ident[:],
-                        start=(i == 0), stop=(i == len(terms) - 1), is_transpose=True,
-                    )
-            nc.scalar.copy(stream[:, half * HALF : (half + 1) * HALF], bank[:])
+        picked2 = gather("picked2", tab2, tab2_plane, list2, 2)
+        wsp_d = deal("wsp_d", wsp, I32, 1)
+        wsp_plane_d = deal("wsp_plane_d", wsp_plane, U8, 1)
+        picked1 = gather("picked1", tab1, tab_plane, list1, 1)
 
-        pages = [keep.tile([P, T2], F32, name="page%d" % t) for t in range(PACK)]
+        h2 = [placed("h2_%d" % t, [P, S], F32, H2 + 4 * KIB * t) for t in range(PACK)]
+        for t in range(PACK):
+            first_product(h2[t], wsp_d[:, rows(t)].bitcast(FP8X4), wsp_plane_d[:, rows(t)], picked2)
 
-        def scatter(t, offsets, stream, gate, pieces):
+        wa_bf = placed("wa_bf", [P, 2 * PACK * H], BF16, PAGES + 8 * KIB)
+        round_weight(wa_bf[:, : PACK * H], war_raw)
+        round_weight(wa_bf[:, PACK * H :], wai_raw)
+
+        def new_page(t):
+            return placed("page%d" % t, [P, T2], F32, PAGES + 8 * KIB * t)
+
+        def gate_and_scatter(page, offsets, gated, stream, gate, pieces):
             n, c = S // pieces, LIST_COLS // pieces
             for i in range(pieces):
                 cols = slice(i * n, (i + 1) * n)
-                nc.vector.tensor_tensor(
-                    pages[t][:].indirect(offsets[:, i * c : (i + 1) * c]), stream[:, cols], gate[:, cols], MULT
-                )
+                nc.gpsimd.tensor_tensor(gated[:, cols], stream[:, cols], gate[:, cols], MULT)
+                nc.vector.tensor_copy(page[:].indirect(offsets[:, i * c : (i + 1) * c]), gated[:, cols])
 
-        picked2 = gather("picked2", tab2, tab2_plane, list2, 2)
-        picked1 = gather("picked1", tab1, tab_plane, list1, 1)
-
-        h2 = [streams.tile([P, S], F32, name="h2_%d" % t, tag="stream") for t in range(PACK)]
-        h2_by_link = []
-        for half in range(2):
-            tile = big.tile([P, LINK_TILES, H], F32, name="h2_by_link%d" % half, tag="big")
-            for lt in range(LINK_TILES):
-                deal_out(tile[:, lt, :], first_product(picked2, half, lt, wsp[:].bitcast(FP8X4), wsp_plane), 1.0)
-            h2_by_link.append(tile)
-            turn([tile], 0, h2[0], half, turn_banks)
-        for half in range(2):
-            turn([h2_by_link[half]], 1, h2[1], half, turn_banks)
-        war_q = quantise_weight("war", war_raw)
-        wai_q = quantise_weight("wai", wai_raw)
-        for half in range(2):
-            turn([h2_by_link[half]], 2, h2[2], half, turn_banks)
-
-        terms = []
-        for half in range(2):
-            real = big.tile([P, LINK_TILES, H], F32, name="real_%d" % half, tag="big")
-            imag = big.tile([P, LINK_TILES, H], F32, name="imag_%d" % half, tag="big")
-            for lt in range(LINK_TILES):
-                deal_out(real[:, lt, :], first_product(picked1, half, lt, wbr[:].bitcast(FP4X4), wbr_plane), 1.0)
-                deal_out(imag[:, lt, :], first_product(picked1, half, lt, wbi[:].bitcast(FP4X4), wbi_plane), -1.0)
-            terms.append((real, imag))
-
-        for t in range(LAST):
-            scatter(t, list4, h2[t], gates2[t], 2 if t == 0 else 1)
-
-        def multiply_terms(half):
-            for lt in range(LINK_TILES):
-                for (codes, plane), term in zip((war_q, wai_q), terms[half]):
-                    bank = first_product(picked1, half, lt, codes[:].bitcast(FP8X4), plane)
-                    nc.vector.tensor_tensor(term[:, lt, :], bank[:], term[:, lt, :], MULT)
-
-        h1 = [streams.tile([P, S], F32, name="h1_%d" % t, tag="stream") for t in range(PACK)]
-        multiply_terms(0)
-        turn(terms[0], 0, h1[0], 0, turn_banks)
-        multiply_terms(1)
-        for half in range(2):
-            turn([h2_by_link[half]], LAST, h2[LAST], half, product_banks)
-        scatter(LAST, list4, h2[LAST], gates2[LAST], 1)
-        turn(terms[1], 0, h1[0], 1, turn_banks)
+        pages = [new_page(0)]
+        gate_and_scatter(pages[0], list4, gates2[0], h2[0], gates2[0], 2)
+        wa_codes = keep.tile([P, 2 * H], U32, name="wa_codes", align_bytes=64)
+        wa_plane = keep.tile([P, 2 * H], U8, name="wa_plane", align_bytes=64)
+        nc.vector.quantize_mx(wa_codes[:].bitcast(FP8X4), wa_plane[:], wa_bf[:])
+        wbr_d = deal("wbr_d", wbr, U8, 2)
+        wbr_plane_d = deal("wbr_plane_d", wbr_plane, U8, 1)
+        wbi_d = deal("wbi_d", wbi, U8, 2)
+        wbi_plane_d = deal("wbi_plane_d", wbi_plane, U8, 1)
         for t in range(1, PACK):
-            for half in range(2):
-                turn(terms[half], t, h1[t], half, turn_banks)
+            pages.append(new_page(t))
+            gate_and_scatter(pages[t], list4, gates2[t], h2[t], gates2[t], 1)
 
-        gains = terms[1][1][:, LINK_TILES - 1, 2 * P : 2 * P + PACK]
-        nc.sync.dma_start(gains, gain.rearrange("(p t) -> p t", t=PACK))
-        wo_raw = h2_by_link[0]
-        fill_weight(wo_raw, wo)
-        wo_codes, wo_plane = quantise_weight("wo", wo_raw)
+        a_parts, b_parts = [], []
+        for t in range(PACK):
+            a = placed("a_%d" % t, [P, 2, S], F32, a_bytes(t))
+            b = placed("b_%d" % t, [P, 2, S], F32, b_bytes(t))
+            first_product(b[:, 0, :], wbr_d[:, rows(t, 0, 2)].bitcast(FP4X4), wbr_plane_d[:, rows(t)], picked1)
+            first_product(b[:, 1, :], wbi_d[:, rows(t, 0, 2)].bitcast(FP4X4), wbi_plane_d[:, rows(t)], picked1)
+            for i in range(2):
+                first_product(a[:, i, :], wa_codes[:, rows(t, i * H)].bitcast(FP8X4), wa_plane[:, rows(t, i * H)], picked1)
+            a_parts.append(a)
+            b_parts.append(b)
+
+        wo_bf = placed("wo_bf", [P, PACK * N], BF16, H2)
+        round_weight(wo_bf[:], wo_raw)
 
         chunk_cols = [slice(sum(CHUNKS[:c]), sum(CHUNKS[: c + 1])) for c in range(len(CHUNKS))]
-        z = [keep.tile([P, w, PACK], BF16, name="z%d" % c, align_bytes=64) for c, w in enumerate(CHUNKS)]
+        z = [placed("z%d" % c, [P, w, PACK], BF16, Z + 2 * PACK * chunk_cols[c].start) for c, w in enumerate(CHUNKS)]
+        on_scalar = range(len(CHUNKS) - SCALAR_LAST_PAGE_CHUNKS, len(CHUNKS))
 
         def round_page(t, c):
             page, factor = pages[t][:, chunk_cols[c]], gains[:, t : t + 1]
-            if t == LAST:
+            if t == LAST and c not in on_scalar:
                 nc.vector.tensor_scalar(z[c][:, :, t], page, factor, None, MULT)
-            elif t == LAST - 1:
+            elif t == LAST - 1 and c not in on_scalar:
                 twice = page.unsqueeze(2).to_broadcast([P, CHUNKS[c], 2])
                 nc.scalar.activation(z[c][:, :, t : t + 2], twice, COPY, scale=factor)
             else:
                 nc.scalar.activation(z[c][:, :, t], page, COPY, scale=factor)
 
         for t in range(PACK):
-            scatter(t, list3, h1[t], gates1[t], 1)
+            a, b = a_parts[t], b_parts[t]
+            products = placed("products%d" % t, [P, 2, S], F32, H2 + 8 * KIB)
+            nc.gpsimd.tensor_tensor(products[:], a[:], b[:], MULT)
+            h1 = products[:, 0, :]
+            nc.gpsimd.tensor_tensor(h1, h1, products[:, 1, :], SUB)
             if t < LAST:
+                gate_and_scatter(pages[t], list3, b[:, 0, :], h1, gates1[t], 1)
                 for c in range(len(CHUNKS)):
                     round_page(t, c)
+            else:
+                wo_codes = placed("wo_codes", [P, N], U32, b_bytes(LAST - 1))
+                wo_plane = placed("wo_plane", [P, N], U8, b_bytes(LAST - 1) + 4 * N)
+                nc.vector.quantize_mx(wo_codes[:].bitcast(FP8X4), wo_plane[:], wo_bf[:])
+                nc.vector.tensor_tensor(pages[t][:].indirect(list3[:]), h1, gates1[t], MULT)
+        for c in on_scalar:
+            round_page(LAST, c)
 
         z_codes = keep.tile([P, T2], U32, align_bytes=64)
         z_plane = keep.tile([P, T2], U8, align_bytes=64)
@@ -266,16 +263,16 @@ def tile_list_woven_link_features_kernel(
 
         def last_product(c):
             w, cols = CHUNKS[c], chunk_cols[c]
-            round_page(LAST, c)
+            if c not in on_scalar:
+                round_page(LAST, c)
             nc.vector.quantize_mx(z_codes[:, cols].bitcast(FP8X4), z_plane[:, cols], z[c][:].rearrange("p m t -> p (m t)"))
-            y = big.tile([P, PACK, w], F32, name="y%d" % c, tag="big")
+            y = placed("y%d" % c, [P, PACK, w], F32, a_bytes(0) + 4 * PACK * cols.start)
             per_bank = BANK // w
             for first in range(0, PACK, per_bank):
-                bank = take(banks)[:].rearrange("p (i m) -> p i m", m=w)
+                bank = take()[:].rearrange("p (i m) -> p i m", m=w)
                 for i in range(per_bank):
-                    rows = slice((first + i) * P, (first + i + 1) * P)
                     nc.tensor.matmul_mx(
-                        bank[:, i, :], lhsT=wo_codes[:, rows].bitcast(FP8X4), lhsT_scale=wo_plane[:, rows],
+                        bank[:, i, :], lhsT=wo_codes[:, rows(first + i)].bitcast(FP8X4), lhsT_scale=wo_plane[:, rows(first + i)],
                         rhs=z_codes[:, cols].bitcast(FP8X4), rhs_scale=z_plane[:, cols], start=True, stop=True,
                     )
                 nc.scalar.copy(y[:, first : first + per_bank, :], bank)
@@ -284,11 +281,13 @@ def tile_list_woven_link_features_kernel(
 
         def store_codes(c, y):
             w, cols = CHUNKS[c], chunk_cols[c]
-            grouped = rounded.tile([P, w, PACK], BF16, name="y_bf%d" % c, tag="bf", align_bytes=64)
+            grouped = placed("y_bf%d" % c, [P, w, PACK], BF16, a_bytes(LAST) + 2 * PACK * cols.start)
+            dst = grouped[:].rearrange("p (c i) t -> p c t i", i=PACK)
+            src = y[:].rearrange("p t (c i) -> p c t i", i=PACK)
             if c == len(CHUNKS) - 1:
-                nc.scalar.copy(grouped[:], y[:].rearrange("p t m -> p m t"))
+                nc.scalar.copy(dst, src)
             else:
-                nc.vector.tensor_copy(grouped[:], y[:].rearrange("p t m -> p m t"))
+                nc.vector.tensor_copy(dst, src)
             nc.vector.quantize_mx(y_codes[:, cols].bitcast(FP8X4), y_plane[:, cols], grouped[:].rearrange("p m t -> p (m t)"))
             if cols.stop % CODE_STORE == 0:
                 stored = slice(cols.stop - CODE_STORE, cols.stop)

@@ -34,6 +34,9 @@ FACTORS = 0
 PAGES = 64 * KIB
 H2 = 96 * KIB
 Z = 112 * KIB
+PICKED1 = 128 * KIB
+WA_CODES = 133 * KIB
+OVERHANG = 64
 
 
 def tile_list_woven_link_features_kernel(
@@ -51,6 +54,9 @@ def tile_list_woven_link_features_kernel(
         def placed(name, shape, dtype, offset):
             return shared.tile(shape, dtype, name=name, align_bytes=64, offset=offset)
 
+        def kept(name, shape, dtype):
+            return keep.tile(shape, dtype, name=name, align_bytes=64)
+
         def a_bytes(t):
             return FACTORS + 16 * KIB * t
 
@@ -62,8 +68,7 @@ def tile_list_woven_link_features_kernel(
             nc.sync.dma_start(tile[:], offsets)
             return tile
 
-        def zeroed_plane(name, width, engine):
-            plane = keep.tile([P, width], U8, name=name, align_bytes=64)
+        def zeroed_plane(plane, engine):
             engine.memset(plane[:].bitcast(I32), 0)
             return plane
 
@@ -81,10 +86,6 @@ def tile_list_woven_link_features_kernel(
             nc.sync.dma_start(tile[:], words[0].rearrange("p c i -> p (c i)").bitcast(I32))
             return tile
 
-        def load_e2m1_words(name, words):
-            tile = keep.tile([P, 2 * H], U8, name=name, align_bytes=64)
-            nc.sync.dma_start(tile[:].bitcast(I32), words[0].bitcast(I32))
-            return tile
 
         def load_gates(name, wg, first, count):
             tile = keep.tile([P, count, S], F32, name=name)
@@ -105,37 +106,37 @@ def tile_list_woven_link_features_kernel(
                 ms = slice(half * P // 2, (half + 1) * P // 2)
                 nc.scalar.copy(dst[:, ms], src[:, ms])
 
-        def deal(name, raw, dtype, per_column):
-            dealt = keep.tile([P, H * per_column], dtype, name=name, align_bytes=64)
-            nc.gpsimd.tensor_copy(
-                dealt[:].rearrange("p (t m b) -> p t m b", t=PACK, b=per_column),
-                raw[:].rearrange("p (m t b) -> p t m b", t=PACK, b=per_column),
+        def deal(name, raw, dtype, weights):
+            dealt = keep.tile([P, H * weights], dtype, name=name, align_bytes=64)
+            nc.vector.tensor_copy(
+                dealt[:].rearrange("p (w t m) -> p w t m", t=PACK, w=weights),
+                raw.rearrange("p (w m t) -> p w t m", t=PACK, w=weights),
             )
             return dealt
 
-        tab2_plane = zeroed_plane("tab2_plane", T, nc.vector)
-        tab_plane = zeroed_plane("tab_plane", T, nc.vector)
-        wsp_plane = zeroed_plane("wsp_plane", H, nc.gpsimd)
-        wbr_plane = zeroed_plane("wbr_plane", H, nc.gpsimd)
-        wbi_plane = zeroed_plane("wbi_plane", H, nc.gpsimd)
+        tab2_plane = zeroed_plane(kept("tab2_plane", [P, T], U8), nc.gpsimd)
+        tab_plane = zeroed_plane(kept("tab_plane", [P, T], U8), nc.vector)
+        wsp_plane = zeroed_plane(placed("wsp_plane", [P, H], U8, PICKED1 + 4 * S), nc.gpsimd)
+        wb_plane = zeroed_plane(placed("wb_plane", [P, 2 * H], U8, WA_CODES + 4 * H), nc.gpsimd)
 
         list2 = load_list("list2", offs2)
-        tab2 = load_e4m3_words(placed("tab2", [P, T], I32, a_bytes(LAST)), tab2_words)
         load_plane(tab2_plane, tab2_scales, nc.sync)
-        wsp = load_e4m3_words(keep.tile([P, H], I32, name="wsp", align_bytes=64), wsp_words)
-        load_plane(wsp_plane, wsp_scales, nc.gpsimd)
+        tab2 = load_e4m3_words(placed("tab2", [P, T], I32, a_bytes(LAST)), tab2_words)
+        wsp = load_e4m3_words(placed("wsp", [P, H], I32, PICKED1), wsp_words)
+        load_plane(wsp_plane, wsp_scales, nc.sync)
         list1 = load_list("list1", offs)
         tab1 = load_e4m3_words(placed("tab1", [P, T], I32, b_bytes(LAST)), tab_words)
         load_plane(tab_plane, tab_scales, nc.sync)
         list4 = load_list("list4", offs4)
-        gates2 = load_gates("gate2_first", wg2, 0, 1)
+        gates2 = load_gates("gate2_first", wg2, 0, 2)
+        gates2.extend(load_gates("gate2_rest", wg2, 2, 2))
         war_raw = load_weight("war_raw", war, a_bytes(0))
         wai_raw = load_weight("wai_raw", wai, b_bytes(0))
-        wbr = load_e2m1_words("wbr", wbr_words)
-        wbi = load_e2m1_words("wbi", wbi_words)
-        load_plane(wbr_plane, wbr_scales, nc.sync)
-        load_plane(wbi_plane, wbi_scales, nc.sync)
-        gates2.extend(load_gates("gate2_rest", wg2, 1, LAST))
+        wb = placed("wb", [P, 2 * H], U16, WA_CODES)
+        for i, words in enumerate((wbr_words, wbi_words)):
+            nc.sync.dma_start(wb[:, i * H : (i + 1) * H].bitcast(I32), words[0].bitcast(I32))
+        for i, scales in enumerate((wbr_scales, wbi_scales)):
+            load_plane(wb_plane[:, i * H : (i + 1) * H], scales, nc.sync)
         list3 = load_list("list3", offs3)
         gates1 = load_gates("gate1", wg1, 0, PACK)
         wo_raw = load_weight("wo_raw", wo, Z)
@@ -149,39 +150,38 @@ def tile_list_woven_link_features_kernel(
             banks.append(bank)
             return bank
 
-        def gather(name, table, plane, offsets, word_pieces):
-            words = keep.tile([P, S], U32, name=name + "_words", align_bytes=64)
-            scale = keep.tile([P, S], U8, name=name + "_scale", align_bytes=64)
+        def gather(words, scale, table, plane, offsets, word_pieces):
             nc.vector.tensor_copy(scale[:], plane[:].indirect(offsets[:]))
             n, c = S // word_pieces, LIST_COLS // word_pieces
             for i in range(word_pieces):
                 nc.vector.tensor_copy(words[:, i * n : (i + 1) * n], table[:].bitcast(U32).indirect(offsets[:, i * c : (i + 1) * c]))
             return words, scale
 
-        def first_product(dst, weight, plane, picked):
+        halves = [slice(half * HALF, (half + 1) * HALF) for half in range(2)]
+
+        def first_product(dst, weight, plane, picked, cols):
             words, scale = picked
-            for half in range(2):
-                cols = slice(half * HALF, (half + 1) * HALF)
-                bank = take()
-                nc.tensor.matmul_mx(
-                    bank[:], lhsT=weight, lhsT_scale=plane,
-                    rhs=words[:, cols].bitcast(FP8X4), rhs_scale=scale[:, cols], start=True, stop=True,
-                )
-                nc.scalar.copy(dst[:, cols], bank[:])
+            bank = take()
+            nc.tensor.matmul_mx(
+                bank[:], lhsT=weight, lhsT_scale=plane,
+                rhs=words[:, cols].bitcast(FP8X4), rhs_scale=scale[:, cols], start=True, stop=True,
+            )
+            nc.scalar.copy(dst[:, cols], bank[:])
 
-        def rows(t, first=0, width=1):
-            return slice((first + t * P) * width, (first + (t + 1) * P) * width)
+        def rows(t, first=0):
+            return slice(first + t * P, first + (t + 1) * P)
 
-        picked2 = gather("picked2", tab2, tab2_plane, list2, 2)
-        wsp_d = deal("wsp_d", wsp, I32, 1)
-        wsp_plane_d = deal("wsp_plane_d", wsp_plane, U8, 1)
-        picked1 = gather("picked1", tab1, tab_plane, list1, 1)
+        picked2 = gather(kept("words2", [P, S], U32), kept("scale2", [P, S], U8), tab2, tab2_plane, list2, 2)
+        wsp_d = deal("wsp_d", wsp[:], I32, 1)
+        wsp_plane_d = deal("wsp_plane_d", wsp_plane[:], U8, 1)
+        picked1 = gather(placed("words1", [P, S], U32, PICKED1), placed("scale1", [P, S], U8, PICKED1 + 4 * S), tab1, tab_plane, list1, 1)
 
         h2 = [placed("h2_%d" % t, [P, S], F32, H2 + 4 * KIB * t) for t in range(PACK)]
         for t in range(PACK):
-            first_product(h2[t], wsp_d[:, rows(t)].bitcast(FP8X4), wsp_plane_d[:, rows(t)], picked2)
+            for cols in halves:
+                first_product(h2[t], wsp_d[:, rows(t)].bitcast(FP8X4), wsp_plane_d[:, rows(t)], picked2, cols)
 
-        wa_bf = placed("wa_bf", [P, 2 * PACK * H], BF16, PAGES + 8 * KIB)
+        wa_bf = placed("wa_bf", [P, 2 * PACK * H + OVERHANG], BF16, PAGES + 16 * KIB - OVERHANG)[:, : 2 * PACK * H]
         round_weight(wa_bf[:, : PACK * H], war_raw)
         round_weight(wa_bf[:, PACK * H :], wai_raw)
 
@@ -197,13 +197,11 @@ def tile_list_woven_link_features_kernel(
 
         pages = [new_page(0)]
         gate_and_scatter(pages[0], list4, gates2[0], h2[0], gates2[0], 2)
-        wa_codes = keep.tile([P, 2 * H], U32, name="wa_codes", align_bytes=64)
+        wb_d = deal("wb_d", wb[:], U16, 2)
+        wb_plane_d = deal("wb_plane_d", wb_plane[:], U8, 2)
+        wa_codes = placed("wa_codes", [P, 2 * H], U32, WA_CODES)
         wa_plane = keep.tile([P, 2 * H], U8, name="wa_plane", align_bytes=64)
-        nc.vector.quantize_mx(wa_codes[:].bitcast(FP8X4), wa_plane[:], wa_bf[:])
-        wbr_d = deal("wbr_d", wbr, U8, 2)
-        wbr_plane_d = deal("wbr_plane_d", wbr_plane, U8, 1)
-        wbi_d = deal("wbi_d", wbi, U8, 2)
-        wbi_plane_d = deal("wbi_plane_d", wbi_plane, U8, 1)
+        nc.vector.quantize_mx(wa_codes[:].bitcast(FP8X4), wa_plane[:], wa_bf)
         for t in range(1, PACK):
             pages.append(new_page(t))
             gate_and_scatter(pages[t], list4, gates2[t], h2[t], gates2[t], 1)
@@ -212,10 +210,11 @@ def tile_list_woven_link_features_kernel(
         for t in range(PACK):
             a = placed("a_%d" % t, [P, 2, S], F32, a_bytes(t))
             b = placed("b_%d" % t, [P, 2, S], F32, b_bytes(t))
-            first_product(b[:, 0, :], wbr_d[:, rows(t, 0, 2)].bitcast(FP4X4), wbr_plane_d[:, rows(t)], picked1)
-            first_product(b[:, 1, :], wbi_d[:, rows(t, 0, 2)].bitcast(FP4X4), wbi_plane_d[:, rows(t)], picked1)
-            for i in range(2):
-                first_product(a[:, i, :], wa_codes[:, rows(t, i * H)].bitcast(FP8X4), wa_plane[:, rows(t, i * H)], picked1)
+            for cols in halves:
+                for i in range(2):
+                    first_product(b[:, i, :], wb_d[:, rows(t, i * H)].bitcast(FP4X4), wb_plane_d[:, rows(t, i * H)], picked1, cols)
+                for i in range(2):
+                    first_product(a[:, i, :], wa_codes[:, rows(t, i * H)].bitcast(FP8X4), wa_plane[:, rows(t, i * H)], picked1, cols)
             a_parts.append(a)
             b_parts.append(b)
 
@@ -239,7 +238,8 @@ def tile_list_woven_link_features_kernel(
         for t in range(PACK):
             a, b = a_parts[t], b_parts[t]
             products = placed("products%d" % t, [P, 2, S], F32, H2 + 8 * KIB)
-            nc.gpsimd.tensor_tensor(products[:], a[:], b[:], MULT)
+            for cols in halves if t == 0 else [slice(0, S)]:
+                nc.gpsimd.tensor_tensor(products[:, :, cols], a[:, :, cols], b[:, :, cols], MULT)
             h1 = products[:, 0, :]
             nc.gpsimd.tensor_tensor(h1, h1, products[:, 1, :], SUB)
             if t < LAST:

@@ -31,12 +31,15 @@ CODE_STORE = 512
 SCALAR_LAST_PAGE_CHUNKS = 1
 KIB = 1024
 FACTORS = 0
-PAGES = 64 * KIB
-H2 = 96 * KIB
-Z = 112 * KIB
-PICKED1 = 128 * KIB
-WA_CODES = 133 * KIB
-OVERHANG = 64
+GATED = 64 * KIB
+PAGES = 72 * KIB
+PAGE_ORDER = (1, 0, 2, 3)
+H2 = 104 * KIB
+Z = 120 * KIB
+PICKED1 = 136 * KIB
+WA_CODES = 141 * KIB
+VECTOR_SLICES = (2, 3)
+VECTOR_PRODUCT_BYTES = {2: GATED, 3: FACTORS + 8 * KIB}
 
 
 def tile_list_woven_link_features_kernel(
@@ -129,7 +132,6 @@ def tile_list_woven_link_features_kernel(
         load_plane(tab_plane, tab_scales, nc.sync)
         list4 = load_list("list4", offs4)
         gates2 = load_gates("gate2_first", wg2, 0, 2)
-        gates2.extend(load_gates("gate2_rest", wg2, 2, 2))
         war_raw = load_weight("war_raw", war, a_bytes(0))
         wai_raw = load_weight("wai_raw", wai, b_bytes(0))
         wb = placed("wb", [P, 2 * H], U16, WA_CODES)
@@ -137,6 +139,7 @@ def tile_list_woven_link_features_kernel(
             nc.sync.dma_start(wb[:, i * H : (i + 1) * H].bitcast(I32), words[0].bitcast(I32))
         for i, scales in enumerate((wbr_scales, wbi_scales)):
             load_plane(wb_plane[:, i * H : (i + 1) * H], scales, nc.sync)
+        gates2.extend(load_gates("gate2_rest", wg2, 2, 2))
         list3 = load_list("list3", offs3)
         gates1 = load_gates("gate1", wg1, 0, PACK)
         wo_raw = load_weight("wo_raw", wo, Z)
@@ -145,9 +148,11 @@ def tile_list_woven_link_features_kernel(
 
         banks = [psum.tile([P, BANK], F32, name="bank%d" % b) for b in range(8)]
 
-        def take():
-            bank = banks.pop(0)
-            banks.append(bank)
+        scalar_banks, vector_banks = banks[:4], banks[4:]
+
+        def take(ring):
+            bank = ring.pop(0)
+            ring.append(bank)
             return bank
 
         def gather(words, scale, table, plane, offsets, word_pieces):
@@ -159,14 +164,17 @@ def tile_list_woven_link_features_kernel(
 
         halves = [slice(half * HALF, (half + 1) * HALF) for half in range(2)]
 
-        def first_product(dst, weight, plane, picked, cols):
+        def first_sums(ring, weight, plane, picked, cols):
             words, scale = picked
-            bank = take()
+            bank = take(ring)
             nc.tensor.matmul_mx(
                 bank[:], lhsT=weight, lhsT_scale=plane,
                 rhs=words[:, cols].bitcast(FP8X4), rhs_scale=scale[:, cols], start=True, stop=True,
             )
-            nc.scalar.copy(dst[:, cols], bank[:])
+            return bank
+
+        def first_product(dst, weight, plane, picked, cols):
+            nc.scalar.copy(dst[:, cols], first_sums(scalar_banks, weight, plane, picked, cols)[:])
 
         def rows(t, first=0):
             return slice(first + t * P, first + (t + 1) * P)
@@ -181,12 +189,12 @@ def tile_list_woven_link_features_kernel(
             for cols in halves:
                 first_product(h2[t], wsp_d[:, rows(t)].bitcast(FP8X4), wsp_plane_d[:, rows(t)], picked2, cols)
 
-        wa_bf = placed("wa_bf", [P, 2 * PACK * H + OVERHANG], BF16, PAGES + 16 * KIB - OVERHANG)[:, : 2 * PACK * H]
+        wa_bf = placed("wa_bf", [P, 2 * PACK * H], BF16, GATED + 4 * KIB)
         round_weight(wa_bf[:, : PACK * H], war_raw)
         round_weight(wa_bf[:, PACK * H :], wai_raw)
 
         def new_page(t):
-            return placed("page%d" % t, [P, T2], F32, PAGES + 8 * KIB * t)
+            return placed("page%d" % t, [P, T2], F32, PAGES + 8 * KIB * PAGE_ORDER.index(t))
 
         def gate_and_scatter(page, offsets, gated, stream, gate, pieces):
             n, c = S // pieces, LIST_COLS // pieces
@@ -201,20 +209,26 @@ def tile_list_woven_link_features_kernel(
         wb_plane_d = deal("wb_plane_d", wb_plane[:], U8, 2)
         wa_codes = placed("wa_codes", [P, 2 * H], U32, WA_CODES)
         wa_plane = keep.tile([P, 2 * H], U8, name="wa_plane", align_bytes=64)
-        nc.vector.quantize_mx(wa_codes[:].bitcast(FP8X4), wa_plane[:], wa_bf)
+        nc.vector.quantize_mx(wa_codes[:].bitcast(FP8X4), wa_plane[:], wa_bf[:])
+        gated_rest = placed("gated_rest", [P, 2, S], F32, GATED)
         for t in range(1, PACK):
             pages.append(new_page(t))
-            gate_and_scatter(pages[t], list4, gates2[t], h2[t], gates2[t], 1)
+            gated = gates2[t] if t == 1 else gated_rest[:, t - 2, :]
+            gate_and_scatter(pages[t], list4, gated, h2[t], gates2[t], 1)
 
-        a_parts, b_parts = [], []
+        a_parts, b_parts, ai_banks = [], [], {}
         for t in range(PACK):
             a = placed("a_%d" % t, [P, 2, S], F32, a_bytes(t))
             b = placed("b_%d" % t, [P, 2, S], F32, b_bytes(t))
             for cols in halves:
                 for i in range(2):
                     first_product(b[:, i, :], wb_d[:, rows(t, i * H)].bitcast(FP4X4), wb_plane_d[:, rows(t, i * H)], picked1, cols)
-                for i in range(2):
-                    first_product(a[:, i, :], wa_codes[:, rows(t, i * H)].bitcast(FP8X4), wa_plane[:, rows(t, i * H)], picked1, cols)
+                first_product(a[:, 0, :], wa_codes[:, rows(t)].bitcast(FP8X4), wa_plane[:, rows(t)], picked1, cols)
+                wai_slice = wa_codes[:, rows(t, H)].bitcast(FP8X4), wa_plane[:, rows(t, H)]
+                if t in VECTOR_SLICES:
+                    ai_banks.setdefault(t, []).append(first_sums(vector_banks, *wai_slice, picked1, cols))
+                else:
+                    first_product(a[:, 1, :], *wai_slice, picked1, cols)
             a_parts.append(a)
             b_parts.append(b)
 
@@ -238,10 +252,16 @@ def tile_list_woven_link_features_kernel(
         for t in range(PACK):
             a, b = a_parts[t], b_parts[t]
             products = placed("products%d" % t, [P, 2, S], F32, H2 + 8 * KIB)
-            for cols in halves if t == 0 else [slice(0, S)]:
-                nc.gpsimd.tensor_tensor(products[:, :, cols], a[:, :, cols], b[:, :, cols], MULT)
             h1 = products[:, 0, :]
-            nc.gpsimd.tensor_tensor(h1, h1, products[:, 1, :], SUB)
+            if t in VECTOR_SLICES:
+                imag = placed("imag%d" % t, [P, S], F32, VECTOR_PRODUCT_BYTES[t])
+                for cols, bank in zip(halves, ai_banks[t]):
+                    nc.vector.tensor_tensor(imag[:, cols], bank[:], b[:, 1, cols], MULT)
+                nc.gpsimd.tensor_tensor(h1, a[:, 0, :], b[:, 0, :], MULT)
+                nc.gpsimd.tensor_tensor(h1, h1, imag[:], SUB)
+            else:
+                nc.gpsimd.tensor_tensor(products[:], a[:], b[:], MULT)
+                nc.gpsimd.tensor_tensor(h1, h1, products[:, 1, :], SUB)
             if t < LAST:
                 gate_and_scatter(pages[t], list3, b[:, 0, :], h1, gates1[t], 1)
                 for c in range(len(CHUNKS)):
@@ -269,7 +289,7 @@ def tile_list_woven_link_features_kernel(
             y = placed("y%d" % c, [P, PACK, w], F32, a_bytes(0) + 4 * PACK * cols.start)
             per_bank = BANK // w
             for first in range(0, PACK, per_bank):
-                bank = take()[:].rearrange("p (i m) -> p i m", m=w)
+                bank = take(banks)[:].rearrange("p (i m) -> p i m", m=w)
                 for i in range(per_bank):
                     nc.tensor.matmul_mx(
                         bank[:, i, :], lhsT=wo_codes[:, rows(first + i)].bitcast(FP8X4), lhsT_scale=wo_plane[:, rows(first + i)],

@@ -1,6 +1,7 @@
 from contextlib import ExitStack
 
 import concourse.mybir as mybir
+from concourse.masks import make_identity
 
 K, T, S, H, T2, N = 512, 2048, 1024, 512, 2048, 512
 FLOPS = 2 * K * H * S * 5 + 2 * H * N * T2
@@ -32,14 +33,14 @@ SCALAR_LAST_PAGE_CHUNKS = 1
 KIB = 1024
 FACTORS = 0
 GATED = 64 * KIB
-PAGES = 72 * KIB
-PAGE_ORDER = (1, 0, 2, 3)
-H2 = 104 * KIB
-Z = 120 * KIB
-PICKED1 = 136 * KIB
-WA_CODES = 141 * KIB
-VECTOR_SLICES = (2, 3)
-VECTOR_PRODUCT_BYTES = {2: GATED, 3: FACTORS + 8 * KIB}
+PAGES = 68 * KIB
+PAGE_ORDER = (1, 2, 0, 3)
+H2 = 100 * KIB
+Z = 116 * KIB
+PICKED1 = 132 * KIB
+WA_CODES = 137 * KIB
+OVERHANG = 64
+LINK_TILES = HALF // P
 
 
 def tile_list_woven_link_features_kernel(
@@ -131,7 +132,7 @@ def tile_list_woven_link_features_kernel(
         tab1 = load_e4m3_words(placed("tab1", [P, T], I32, b_bytes(LAST)), tab_words)
         load_plane(tab_plane, tab_scales, nc.sync)
         list4 = load_list("list4", offs4)
-        gates2 = load_gates("gate2_first", wg2, 0, 2)
+        gates2 = load_gates("gate2_first", wg2, 0, 1) + load_gates("gate2_next", wg2, 1, 2)
         war_raw = load_weight("war_raw", war, a_bytes(0))
         wai_raw = load_weight("wai_raw", wai, b_bytes(0))
         wb = placed("wb", [P, 2 * H], U16, WA_CODES)
@@ -139,16 +140,16 @@ def tile_list_woven_link_features_kernel(
             nc.sync.dma_start(wb[:, i * H : (i + 1) * H].bitcast(I32), words[0].bitcast(I32))
         for i, scales in enumerate((wbr_scales, wbi_scales)):
             load_plane(wb_plane[:, i * H : (i + 1) * H], scales, nc.sync)
-        gates2.extend(load_gates("gate2_rest", wg2, 2, 2))
+        gates2.extend(load_gates("gate2_last", wg2, LAST, 1))
         list3 = load_list("list3", offs3)
         gates1 = load_gates("gate1", wg1, 0, PACK)
         wo_raw = load_weight("wo_raw", wo, Z)
-        gains = keep.tile([P, PACK], F32, name="gains")
-        nc.sync.dma_start(gains[:], gain.rearrange("(p t) -> p t", t=PACK))
 
         banks = [psum.tile([P, BANK], F32, name="bank%d" % b) for b in range(8)]
 
-        scalar_banks, vector_banks = banks[:4], banks[4:]
+        scalar_banks, turn_banks = banks[:6], banks[6:]
+        ident = keep.tile([P, P], F32)
+        make_identity(nc, ident[:])
 
         def take(ring):
             bank = ring.pop(0)
@@ -189,7 +190,7 @@ def tile_list_woven_link_features_kernel(
             for cols in halves:
                 first_product(h2[t], wsp_d[:, rows(t)].bitcast(FP8X4), wsp_plane_d[:, rows(t)], picked2, cols)
 
-        wa_bf = placed("wa_bf", [P, 2 * PACK * H], BF16, GATED + 4 * KIB)
+        wa_bf = placed("wa_bf", [P, 2 * PACK * H + OVERHANG], BF16, PAGES - OVERHANG)[:, : 2 * PACK * H]
         round_weight(wa_bf[:, : PACK * H], war_raw)
         round_weight(wa_bf[:, PACK * H :], wai_raw)
 
@@ -209,34 +210,72 @@ def tile_list_woven_link_features_kernel(
         wb_plane_d = deal("wb_plane_d", wb_plane[:], U8, 2)
         wa_codes = placed("wa_codes", [P, 2 * H], U32, WA_CODES)
         wa_plane = keep.tile([P, 2 * H], U8, name="wa_plane", align_bytes=64)
-        nc.vector.quantize_mx(wa_codes[:].bitcast(FP8X4), wa_plane[:], wa_bf[:])
-        gated_rest = placed("gated_rest", [P, 2, S], F32, GATED)
+        nc.vector.quantize_mx(wa_codes[:].bitcast(FP8X4), wa_plane[:], wa_bf)
+        gated_last = placed("gated_last", [P, S], F32, GATED)
         for t in range(1, PACK):
             pages.append(new_page(t))
-            gated = gates2[t] if t == 1 else gated_rest[:, t - 2, :]
+            gated = gated_last if t == LAST else gates2[t]
             gate_and_scatter(pages[t], list4, gated, h2[t], gates2[t], 1)
 
-        a_parts, b_parts, ai_banks = [], [], {}
-        for t in range(PACK):
+        def factor_by_link(dst, weight, plane, half, sign):
+            words, scale = picked1
+            bank = take(scalar_banks)
+            for lt in range(LINK_TILES):
+                links = slice(half * HALF + lt * P, half * HALF + (lt + 1) * P)
+                nc.tensor.matmul_mx(
+                    bank[:, lt * P : (lt + 1) * P], lhsT=words[:, links].bitcast(FP8X4), lhsT_scale=scale[:, links],
+                    rhs=weight, rhs_scale=plane, start=True, stop=True,
+                )
+            nc.scalar.activation(dst[:, halves[half]], bank[:], COPY, scale=sign)
+
+        def factors(t):
             a = placed("a_%d" % t, [P, 2, S], F32, a_bytes(t))
             b = placed("b_%d" % t, [P, 2, S], F32, b_bytes(t))
+            for half in range(2):
+                for dst, codes, plane, dtype in ((b, wb_d, wb_plane_d, FP4X4), (a, wa_codes, wa_plane, FP8X4)):
+                    for i in range(2):
+                        weight = codes[:, rows(t, i * H)].bitcast(dtype), plane[:, rows(t, i * H)]
+                        if t == LAST:
+                            first_product(dst[:, i, :], *weight, picked1, halves[half])
+                        else:
+                            factor_by_link(dst[:, i, :], *weight, half, -1.0 if dst is b and i == 1 else 1.0)
+            return a, b
+
+        def multiply(products, a, b):
             for cols in halves:
-                for i in range(2):
-                    first_product(b[:, i, :], wb_d[:, rows(t, i * H)].bitcast(FP4X4), wb_plane_d[:, rows(t, i * H)], picked1, cols)
-                first_product(a[:, 0, :], wa_codes[:, rows(t)].bitcast(FP8X4), wa_plane[:, rows(t)], picked1, cols)
-                wai_slice = wa_codes[:, rows(t, H)].bitcast(FP8X4), wa_plane[:, rows(t, H)]
-                if t in VECTOR_SLICES:
-                    ai_banks.setdefault(t, []).append(first_sums(vector_banks, *wai_slice, picked1, cols))
-                else:
-                    first_product(a[:, 1, :], *wai_slice, picked1, cols)
-            a_parts.append(a)
-            b_parts.append(b)
+                nc.gpsimd.tensor_tensor(products[:, :, cols], a[:, :, cols], b[:, :, cols], MULT)
+
+        def turn(t, products):
+            h1 = placed("h1_%d" % t, [P, S], F32, a_bytes(t))
+            for half in range(2):
+                bank = take(turn_banks)
+                for lt in range(LINK_TILES):
+                    first = half * HALF + lt * P
+                    for i in range(2):
+                        nc.tensor.matmul(
+                            bank[:, lt * P : (lt + 1) * P], lhsT=products[:, i, first : first + P], rhs=ident[:],
+                            start=(i == 0), stop=(i == 1), is_transpose=True,
+                        )
+                nc.scalar.copy(h1[:, halves[half]], bank[:])
+            return h1
+
+        a0, b0 = factors(0)
+        a1, b1 = factors(1)
+        products0 = placed("products0", [P, 2, S], F32, H2 + 8 * KIB)
+        multiply(products0, a0, b0)
+        h1 = [turn(0, products0)]
+        multiply(b1, a1, b1)
+        h1.append(turn(1, b1))
+        a2, b2 = factors(2)
+        a3, b3 = factors(3)
 
         wo_bf = placed("wo_bf", [P, PACK * N], BF16, H2)
         round_weight(wo_bf[:], wo_raw)
 
         chunk_cols = [slice(sum(CHUNKS[:c]), sum(CHUNKS[: c + 1])) for c in range(len(CHUNKS))]
-        z = [placed("z%d" % c, [P, w, PACK], BF16, Z + 2 * PACK * chunk_cols[c].start) for c, w in enumerate(CHUNKS)]
+        z_all = placed("z", [P, T2 * PACK], BF16, Z)
+        z_flat = [z_all[:, PACK * cols.start : PACK * cols.stop] for cols in chunk_cols]
+        z = [flat.rearrange("p (m t) -> p m t", t=PACK) for flat in z_flat]
         on_scalar = range(len(CHUNKS) - SCALAR_LAST_PAGE_CHUNKS, len(CHUNKS))
 
         def round_page(t, c):
@@ -249,28 +288,34 @@ def tile_list_woven_link_features_kernel(
             else:
                 nc.scalar.activation(z[c][:, :, t], page, COPY, scale=factor)
 
-        for t in range(PACK):
-            a, b = a_parts[t], b_parts[t]
-            products = placed("products%d" % t, [P, 2, S], F32, H2 + 8 * KIB)
-            h1 = products[:, 0, :]
-            if t in VECTOR_SLICES:
-                imag = placed("imag%d" % t, [P, S], F32, VECTOR_PRODUCT_BYTES[t])
-                for cols, bank in zip(halves, ai_banks[t]):
-                    nc.vector.tensor_tensor(imag[:, cols], bank[:], b[:, 1, cols], MULT)
-                nc.gpsimd.tensor_tensor(h1, a[:, 0, :], b[:, 0, :], MULT)
-                nc.gpsimd.tensor_tensor(h1, h1, imag[:], SUB)
-            else:
-                nc.gpsimd.tensor_tensor(products[:], a[:], b[:], MULT)
-                nc.gpsimd.tensor_tensor(h1, h1, products[:, 1, :], SUB)
-            if t < LAST:
-                gate_and_scatter(pages[t], list3, b[:, 0, :], h1, gates1[t], 1)
-                for c in range(len(CHUNKS)):
-                    round_page(t, c)
-            else:
-                wo_codes = placed("wo_codes", [P, N], U32, b_bytes(LAST - 1))
-                wo_plane = placed("wo_plane", [P, N], U8, b_bytes(LAST - 1) + 4 * N)
-                nc.vector.quantize_mx(wo_codes[:].bitcast(FP8X4), wo_plane[:], wo_bf[:])
-                nc.vector.tensor_tensor(pages[t][:].indirect(list3[:]), h1, gates1[t], MULT)
+        def round_whole_page(t):
+            for c in range(len(CHUNKS)):
+                round_page(t, c)
+
+        def place_h1(t, offset):
+            gated = placed("gated1_%d" % t, [P, S], F32, offset)
+            gate_and_scatter(pages[t], list3, gated, h1[t], gates1[t], 1)
+
+        place_h1(0, b_bytes(0))
+        products2 = placed("products2", [P, 2, S], F32, a_bytes(0))
+        multiply(products2, a2, b2)
+        h1.append(turn(2, products2))
+        gains = placed("gains", [P, PACK], F32, b_bytes(2))
+        nc.sync.dma_start(gains[:], gain.rearrange("(p t) -> p t", t=PACK))
+        round_whole_page(0)
+        place_h1(1, b_bytes(1))
+        round_whole_page(1)
+        place_h1(2, H2 + 4 * KIB)
+        round_whole_page(2)
+        h1_last = placed("h1_last", [P, S], F32, a_bytes(1) + 4 * KIB)
+        for half, cols in enumerate(halves):
+            products = placed("products3_%d" % half, [P, 2, HALF], F32, a_bytes(1 + half))
+            nc.gpsimd.tensor_tensor(products[:], a3[:, :, cols], b3[:, :, cols], MULT)
+            nc.gpsimd.tensor_tensor(h1_last[:, cols], products[:, 0, :], products[:, 1, :], SUB)
+        wo_codes = placed("wo_codes", [P, N], U32, H2 + 4 * KIB)
+        wo_plane = placed("wo_plane", [P, N], U8, H2 + 4 * KIB + 4 * N)
+        nc.vector.quantize_mx(wo_codes[:].bitcast(FP8X4), wo_plane[:], wo_bf[:])
+        nc.vector.tensor_tensor(pages[LAST][:].indirect(list3[:]), h1_last[:], gates1[LAST], MULT)
         for c in on_scalar:
             round_page(LAST, c)
 
@@ -285,7 +330,7 @@ def tile_list_woven_link_features_kernel(
             w, cols = CHUNKS[c], chunk_cols[c]
             if c not in on_scalar:
                 round_page(LAST, c)
-            nc.vector.quantize_mx(z_codes[:, cols].bitcast(FP8X4), z_plane[:, cols], z[c][:].rearrange("p m t -> p (m t)"))
+            nc.vector.quantize_mx(z_codes[:, cols].bitcast(FP8X4), z_plane[:, cols], z_flat[c])
             y = placed("y%d" % c, [P, PACK, w], F32, a_bytes(0) + 4 * PACK * cols.start)
             per_bank = BANK // w
             for first in range(0, PACK, per_bank):

@@ -32,14 +32,17 @@ CODE_STORE = 512
 SCALAR_LAST_PAGE_CHUNKS = 1
 KIB = 1024
 FACTORS = 0
-GATED = 64 * KIB
-PAGES = 68 * KIB
-PAGE_ORDER = (1, 2, 0, 3)
-H2 = 100 * KIB
-Z = 116 * KIB
-PICKED1 = 132 * KIB
-WA_CODES = 137 * KIB
 OVERHANG = 64
+PRODUCTS1 = 64 * KIB
+GATES_NEXT = PRODUCTS1 + 4 * KIB + OVERHANG
+GATED = 72 * KIB
+PAGES = 76 * KIB
+PAGE_ORDER = (1, 2, 0, 3)
+H2 = 108 * KIB
+Z = 124 * KIB
+PICKED1 = 140 * KIB
+WA_CODES = 145 * KIB
+GATE_LAST = FACTORS + 40 * KIB
 LINK_TILES = HALF // P
 
 
@@ -91,8 +94,7 @@ def tile_list_woven_link_features_kernel(
             return tile
 
 
-        def load_gates(name, wg, first, count):
-            tile = keep.tile([P, count, S], F32, name=name)
+        def load_gates(tile, wg, first, count):
             rows = wg.rearrange("(p t) j -> p t j", t=PACK)[:, first : first + count, :]
             for q in range(QUADRANTS):
                 nc.sync.dma_start(tile[QUADRANT * q : QUADRANT * (q + 1)], rows)
@@ -110,8 +112,7 @@ def tile_list_woven_link_features_kernel(
                 ms = slice(half * P // 2, (half + 1) * P // 2)
                 nc.scalar.copy(dst[:, ms], src[:, ms])
 
-        def deal(name, raw, dtype, weights):
-            dealt = keep.tile([P, H * weights], dtype, name=name, align_bytes=64)
+        def deal(dealt, raw, weights):
             nc.vector.tensor_copy(
                 dealt[:].rearrange("p (w t m) -> p w t m", t=PACK, w=weights),
                 raw.rearrange("p (w m t) -> p w t m", t=PACK, w=weights),
@@ -124,25 +125,26 @@ def tile_list_woven_link_features_kernel(
         wb_plane = zeroed_plane(placed("wb_plane", [P, 2 * H], U8, WA_CODES + 4 * H), nc.gpsimd)
 
         list2 = load_list("list2", offs2)
-        load_plane(tab2_plane, tab2_scales, nc.sync)
         tab2 = load_e4m3_words(placed("tab2", [P, T], I32, a_bytes(LAST)), tab2_words)
+        load_plane(tab2_plane, tab2_scales, nc.sync)
         wsp = load_e4m3_words(placed("wsp", [P, H], I32, PICKED1), wsp_words)
         load_plane(wsp_plane, wsp_scales, nc.sync)
         list1 = load_list("list1", offs)
         tab1 = load_e4m3_words(placed("tab1", [P, T], I32, b_bytes(LAST)), tab_words)
         load_plane(tab_plane, tab_scales, nc.sync)
         list4 = load_list("list4", offs4)
-        gates2 = load_gates("gate2_first", wg2, 0, 1) + load_gates("gate2_next", wg2, 1, 2)
+        gates2 = load_gates(kept("gate2_first", [P, 2, S], F32), wg2, 0, 2)
         war_raw = load_weight("war_raw", war, a_bytes(0))
         wai_raw = load_weight("wai_raw", wai, b_bytes(0))
         wb = placed("wb", [P, 2 * H], U16, WA_CODES)
         for i, words in enumerate((wbr_words, wbi_words)):
             nc.sync.dma_start(wb[:, i * H : (i + 1) * H].bitcast(I32), words[0].bitcast(I32))
         for i, scales in enumerate((wbr_scales, wbi_scales)):
-            load_plane(wb_plane[:, i * H : (i + 1) * H], scales, nc.sync)
-        gates2.extend(load_gates("gate2_last", wg2, LAST, 1))
+            load_plane(wb_plane[:, i * H : (i + 1) * H], scales, nc.gpsimd)
+        gates2.extend(load_gates(placed("gate2_next", [P, 1, S], F32, GATES_NEXT), wg2, 2, 1))
+        gates2.extend(load_gates(placed("gate2_last", [P, 1, S], F32, GATE_LAST), wg2, LAST, 1))
         list3 = load_list("list3", offs3)
-        gates1 = load_gates("gate1", wg1, 0, PACK)
+        gates1 = load_gates(kept("gate1", [P, PACK, S], F32), wg1, 0, PACK)
         wo_raw = load_weight("wo_raw", wo, Z)
 
         banks = [psum.tile([P, BANK], F32, name="bank%d" % b) for b in range(8)]
@@ -181,8 +183,8 @@ def tile_list_woven_link_features_kernel(
             return slice(first + t * P, first + (t + 1) * P)
 
         picked2 = gather(kept("words2", [P, S], U32), kept("scale2", [P, S], U8), tab2, tab2_plane, list2, 2)
-        wsp_d = deal("wsp_d", wsp[:], I32, 1)
-        wsp_plane_d = deal("wsp_plane_d", wsp_plane[:], U8, 1)
+        wsp_d = deal(kept("wsp_d", [P, H], I32), wsp[:], 1)
+        wsp_plane_d = deal(kept("wsp_plane_d", [P, H], U8), wsp_plane[:], 1)
         picked1 = gather(placed("words1", [P, S], U32, PICKED1), placed("scale1", [P, S], U8, PICKED1 + 4 * S), tab1, tab_plane, list1, 1)
 
         h2 = [placed("h2_%d" % t, [P, S], F32, H2 + 4 * KIB * t) for t in range(PACK)]
@@ -205,16 +207,16 @@ def tile_list_woven_link_features_kernel(
                 nc.vector.tensor_copy(page[:].indirect(offsets[:, i * c : (i + 1) * c]), gated[:, cols])
 
         pages = [new_page(0)]
-        gate_and_scatter(pages[0], list4, gates2[0], h2[0], gates2[0], 2)
-        wb_d = deal("wb_d", wb[:], U16, 2)
-        wb_plane_d = deal("wb_plane_d", wb_plane[:], U8, 2)
+        gate_and_scatter(pages[0], list4, h2[0], h2[0], gates2[0], 2)
+        wb_d = deal(placed("wb_d", [P, 2 * H], U16, H2), wb[:], 2)
+        wb_plane_d = deal(placed("wb_plane_d", [P, 2 * H], U8, H2 + 4 * H), wb_plane[:], 2)
         wa_codes = placed("wa_codes", [P, 2 * H], U32, WA_CODES)
         wa_plane = keep.tile([P, 2 * H], U8, name="wa_plane", align_bytes=64)
         nc.vector.quantize_mx(wa_codes[:].bitcast(FP8X4), wa_plane[:], wa_bf)
         gated_last = placed("gated_last", [P, S], F32, GATED)
         for t in range(1, PACK):
             pages.append(new_page(t))
-            gated = gated_last if t == LAST else gates2[t]
+            gated = gated_last if t == LAST else h2[t]
             gate_and_scatter(pages[t], list4, gated, h2[t], gates2[t], 1)
 
         def factor_by_link(dst, weight, plane, half, sign):
@@ -261,15 +263,16 @@ def tile_list_woven_link_features_kernel(
 
         a0, b0 = factors(0)
         a1, b1 = factors(1)
-        products0 = placed("products0", [P, 2, S], F32, H2 + 8 * KIB)
+        products0 = placed("products0", [P, 2, S], F32, GATE_LAST)
         multiply(products0, a0, b0)
         h1 = [turn(0, products0)]
-        multiply(b1, a1, b1)
-        h1.append(turn(1, b1))
+        products1 = placed("products1", [P, 2, S], F32, b_bytes(0))
+        multiply(products1, a1, b1)
+        h1.append(turn(1, products1))
         a2, b2 = factors(2)
         a3, b3 = factors(3)
 
-        wo_bf = placed("wo_bf", [P, PACK * N], BF16, H2)
+        wo_bf = placed("wo_bf", [P, PACK * N], BF16, b_bytes(0))
         round_weight(wo_bf[:], wo_raw)
 
         chunk_cols = [slice(sum(CHUNKS[:c]), sum(CHUNKS[: c + 1])) for c in range(len(CHUNKS))]
@@ -296,24 +299,24 @@ def tile_list_woven_link_features_kernel(
             gated = placed("gated1_%d" % t, [P, S], F32, offset)
             gate_and_scatter(pages[t], list3, gated, h1[t], gates1[t], 1)
 
-        place_h1(0, b_bytes(0))
+        place_h1(0, PRODUCTS1)
         products2 = placed("products2", [P, 2, S], F32, a_bytes(0))
         multiply(products2, a2, b2)
         h1.append(turn(2, products2))
-        gains = placed("gains", [P, PACK], F32, b_bytes(2))
+        gains = placed("gains", [P, PACK], F32, a_bytes(0))
         nc.sync.dma_start(gains[:], gain.rearrange("(p t) -> p t", t=PACK))
         round_whole_page(0)
         place_h1(1, b_bytes(1))
         round_whole_page(1)
-        place_h1(2, H2 + 4 * KIB)
+        place_h1(2, H2 + 8 * KIB)
         round_whole_page(2)
         h1_last = placed("h1_last", [P, S], F32, a_bytes(1) + 4 * KIB)
         for half, cols in enumerate(halves):
             products = placed("products3_%d" % half, [P, 2, HALF], F32, a_bytes(1 + half))
             nc.gpsimd.tensor_tensor(products[:], a3[:, :, cols], b3[:, :, cols], MULT)
             nc.gpsimd.tensor_tensor(h1_last[:, cols], products[:, 0, :], products[:, 1, :], SUB)
-        wo_codes = placed("wo_codes", [P, N], U32, H2 + 4 * KIB)
-        wo_plane = placed("wo_plane", [P, N], U8, H2 + 4 * KIB + 4 * N)
+        wo_codes = placed("wo_codes", [P, N], U32, H2 + 8 * KIB)
+        wo_plane = placed("wo_plane", [P, N], U8, H2 + 8 * KIB + 4 * N)
         nc.vector.quantize_mx(wo_codes[:].bitcast(FP8X4), wo_plane[:], wo_bf[:])
         nc.vector.tensor_tensor(pages[LAST][:].indirect(list3[:]), h1_last[:], gates1[LAST], MULT)
         for c in on_scalar:
@@ -331,7 +334,7 @@ def tile_list_woven_link_features_kernel(
             if c not in on_scalar:
                 round_page(LAST, c)
             nc.vector.quantize_mx(z_codes[:, cols].bitcast(FP8X4), z_plane[:, cols], z_flat[c])
-            y = placed("y%d" % c, [P, PACK, w], F32, a_bytes(0) + 4 * PACK * cols.start)
+            y = placed("y%d" % c, [P, PACK, w], F32, a_bytes(1) + 4 * PACK * cols.start)
             per_bank = BANK // w
             for first in range(0, PACK, per_bank):
                 bank = take(banks)[:].rearrange("p (i m) -> p i m", m=w)

@@ -16,7 +16,7 @@ FP8X4 = mybir.dt.float8_e4m3fn_x4
 FP4X4 = mybir.dt.float4_e2m1fn_x4
 COPY = mybir.ActivationFunctionType.Copy
 MULT = mybir.AluOpType.mult
-SUB = mybir.AluOpType.subtract
+ADD = mybir.AluOpType.add
 
 P = 128
 PACK = 4
@@ -34,15 +34,16 @@ KIB = 1024
 FACTORS = 0
 OVERHANG = 64
 PRODUCTS1 = 64 * KIB
-GATES_NEXT = PRODUCTS1 + 4 * KIB + OVERHANG
+GATES_NEXT = PRODUCTS1 + OVERHANG
 GATED = 72 * KIB
 PAGES = 76 * KIB
 PAGE_ORDER = (1, 2, 0, 3)
 H2 = 108 * KIB
 Z = 124 * KIB
-PICKED1 = 140 * KIB
-WA_CODES = 145 * KIB
-GATE_LAST = FACTORS + 40 * KIB
+H1_FIRST = Z + 16 * KIB
+PICKED1 = 144 * KIB
+WA_CODES = 149 * KIB
+GATE_LAST = 153 * KIB
 LINK_TILES = HALF // P
 
 
@@ -105,16 +106,16 @@ def tile_list_woven_link_features_kernel(
             nc.sync.dma_start(raw[:], w.rearrange("(p i) c -> p i c", i=PACK))
             return raw
 
-        def round_weight(grouped, raw):
-            dst = grouped.rearrange("p (t m i) -> p m t i", t=PACK, i=PACK)
+        def round_weight(dealt, raw, sign):
+            dst = dealt.rearrange("p t (m i) -> p m t i", i=PACK)
             src = raw[:].rearrange("p i (m t) -> p m t i", t=PACK)
             for half in range(2):
                 ms = slice(half * P // 2, (half + 1) * P // 2)
-                nc.scalar.copy(dst[:, ms], src[:, ms])
+                nc.scalar.activation(dst[:, ms], src[:, ms], COPY, scale=sign)
 
         def deal(dealt, raw, weights):
             nc.vector.tensor_copy(
-                dealt[:].rearrange("p (w t m) -> p w t m", t=PACK, w=weights),
+                dealt[:].rearrange("p (t w m) -> p w t m", t=PACK, w=weights),
                 raw.rearrange("p (w m t) -> p w t m", t=PACK, w=weights),
             )
             return dealt
@@ -133,19 +134,22 @@ def tile_list_woven_link_features_kernel(
         tab1 = load_e4m3_words(placed("tab1", [P, T], I32, b_bytes(LAST)), tab_words)
         load_plane(tab_plane, tab_scales, nc.sync)
         list4 = load_list("list4", offs4)
-        gates2 = load_gates(kept("gate2_first", [P, 2, S], F32), wg2, 0, 2)
+        gate2_next = placed("gate2_next", [P, 2, S], F32, GATES_NEXT)
+        gates2 = load_gates(kept("gate2_0", [P, 1, S], F32), wg2, 0, 1) + load_gates(gate2_next, wg2, 1, 2)
         war_raw = load_weight("war_raw", war, a_bytes(0))
         wai_raw = load_weight("wai_raw", wai, b_bytes(0))
         wb = placed("wb", [P, 2 * H], U16, WA_CODES)
         for i, words in enumerate((wbr_words, wbi_words)):
             nc.sync.dma_start(wb[:, i * H : (i + 1) * H].bitcast(I32), words[0].bitcast(I32))
         for i, scales in enumerate((wbr_scales, wbi_scales)):
-            load_plane(wb_plane[:, i * H : (i + 1) * H], scales, nc.gpsimd)
-        gates2.extend(load_gates(placed("gate2_next", [P, 1, S], F32, GATES_NEXT), wg2, 2, 1))
+            load_plane(wb_plane[:, i * H : (i + 1) * H], scales, nc.sync)
         gates2.extend(load_gates(placed("gate2_last", [P, 1, S], F32, GATE_LAST), wg2, LAST, 1))
         list3 = load_list("list3", offs3)
         gates1 = load_gates(kept("gate1", [P, PACK, S], F32), wg1, 0, PACK)
         wo_raw = load_weight("wo_raw", wo, Z)
+
+        gains = keep.tile([P, PACK], F32, name="gains")
+        nc.sync.dma_start(gains[:], gain.rearrange("(p t) -> p t", t=PACK))
 
         banks = [psum.tile([P, BANK], F32, name="bank%d" % b) for b in range(8)]
 
@@ -187,14 +191,16 @@ def tile_list_woven_link_features_kernel(
         wsp_plane_d = deal(kept("wsp_plane_d", [P, H], U8), wsp_plane[:], 1)
         picked1 = gather(placed("words1", [P, S], U32, PICKED1), placed("scale1", [P, S], U8, PICKED1 + 4 * S), tab1, tab_plane, list1, 1)
 
-        h2 = [placed("h2_%d" % t, [P, S], F32, H2 + 4 * KIB * t) for t in range(PACK)]
+        h2_next = placed("h2_next", [P, 2, S], F32, H2 + 4 * KIB)
+        h2 = [placed("h2_0", [P, S], F32, H2), h2_next[:, 0, :], h2_next[:, 1, :], placed("h2_last", [P, S], F32, H2 + 12 * KIB)]
         for t in range(PACK):
             for cols in halves:
                 first_product(h2[t], wsp_d[:, rows(t)].bitcast(FP8X4), wsp_plane_d[:, rows(t)], picked2, cols)
 
         wa_bf = placed("wa_bf", [P, 2 * PACK * H + OVERHANG], BF16, PAGES - OVERHANG)[:, : 2 * PACK * H]
-        round_weight(wa_bf[:, : PACK * H], war_raw)
-        round_weight(wa_bf[:, PACK * H :], wai_raw)
+        wa_by_weight = wa_bf.rearrange("p (t w c) -> p w t c", t=PACK, w=2)
+        round_weight(wa_by_weight[:, 0], war_raw, 1.0)
+        round_weight(wa_by_weight[:, 1], wai_raw, -1.0)
 
         def new_page(t):
             return placed("page%d" % t, [P, T2], F32, PAGES + 8 * KIB * PAGE_ORDER.index(t))
@@ -213,22 +219,24 @@ def tile_list_woven_link_features_kernel(
         wa_codes = placed("wa_codes", [P, 2 * H], U32, WA_CODES)
         wa_plane = keep.tile([P, 2 * H], U8, name="wa_plane", align_bytes=64)
         nc.vector.quantize_mx(wa_codes[:].bitcast(FP8X4), wa_plane[:], wa_bf)
+        pages.extend(new_page(t) for t in range(1, PACK))
+        nc.gpsimd.tensor_tensor(h2_next[:], h2_next[:], gate2_next[:], MULT)
+        for t in range(1, LAST):
+            nc.vector.tensor_copy(pages[t][:].indirect(list4[:]), h2[t])
         gated_last = placed("gated_last", [P, S], F32, GATED)
-        for t in range(1, PACK):
-            pages.append(new_page(t))
-            gated = gated_last if t == LAST else h2[t]
-            gate_and_scatter(pages[t], list4, gated, h2[t], gates2[t], 1)
+        gate_and_scatter(pages[LAST], list4, gated_last, h2[LAST], gates2[LAST], 1)
 
-        def factor_by_link(dst, weight, plane, half, sign):
+        def factors_by_link(dst, weights, plane, pair):
             words, scale = picked1
             bank = take(scalar_banks)
-            for lt in range(LINK_TILES):
-                links = slice(half * HALF + lt * P, half * HALF + (lt + 1) * P)
+            for lt in range(2):
+                links = slice((2 * pair + lt) * P, (2 * pair + lt + 1) * P)
                 nc.tensor.matmul_mx(
-                    bank[:, lt * P : (lt + 1) * P], lhsT=words[:, links].bitcast(FP8X4), lhsT_scale=scale[:, links],
-                    rhs=weight, rhs_scale=plane, start=True, stop=True,
+                    bank[:, 2 * P * lt : 2 * P * (lt + 1)], lhsT=words[:, links].bitcast(FP8X4), lhsT_scale=scale[:, links],
+                    rhs=weights, rhs_scale=plane, start=True, stop=True,
                 )
-            nc.scalar.activation(dst[:, halves[half]], bank[:], COPY, scale=sign)
+            places = dst[:, :, 2 * P * pair : 2 * P * (pair + 1)].rearrange("p i (lt m) -> p lt i m", lt=2)
+            nc.scalar.copy(places, bank[:].rearrange("p (lt i m) -> p lt i m", lt=2, i=2))
 
         def factors(t):
             a = placed("a_%d" % t, [P, 2, S], F32, a_bytes(t))
@@ -236,44 +244,48 @@ def tile_list_woven_link_features_kernel(
             for half in range(2):
                 for dst, codes, plane, dtype in ((b, wb_d, wb_plane_d, FP4X4), (a, wa_codes, wa_plane, FP8X4)):
                     for i in range(2):
-                        weight = codes[:, rows(t, i * H)].bitcast(dtype), plane[:, rows(t, i * H)]
                         if t == LAST:
-                            first_product(dst[:, i, :], *weight, picked1, halves[half])
+                            cols = rows(2 * t + i)
+                            first_product(dst[:, i, :], codes[:, cols].bitcast(dtype), plane[:, cols], picked1, halves[half])
                         else:
-                            factor_by_link(dst[:, i, :], *weight, half, -1.0 if dst is b and i == 1 else 1.0)
+                            cols = slice(2 * P * t, 2 * P * (t + 1))
+                            factors_by_link(dst, codes[:, cols].bitcast(dtype), plane[:, cols], 2 * half + i)
             return a, b
 
-        def multiply(products, a, b):
-            for cols in halves:
+        def multiply(t, offset, pieces):
+            a, b = factor_tiles[t]
+            products = placed("products%d" % t, [P, 2, S], F32, offset)
+            for cols in pieces:
                 nc.gpsimd.tensor_tensor(products[:, :, cols], a[:, :, cols], b[:, :, cols], MULT)
+            return products
 
-        def turn(t, products):
-            h1 = placed("h1_%d" % t, [P, S], F32, a_bytes(t))
+        def turn(t, products, offset):
+            h1 = placed("h1_%d" % t, [P, S], F32, offset)
             for half in range(2):
                 bank = take(turn_banks)
                 for lt in range(LINK_TILES):
-                    first = half * HALF + lt * P
                     for i in range(2):
                         nc.tensor.matmul(
-                            bank[:, lt * P : (lt + 1) * P], lhsT=products[:, i, first : first + P], rhs=ident[:],
+                            bank[:, lt * P : (lt + 1) * P], lhsT=products[:, i, half * HALF + lt * P : half * HALF + (lt + 1) * P], rhs=ident[:],
                             start=(i == 0), stop=(i == 1), is_transpose=True,
                         )
                 nc.scalar.copy(h1[:, halves[half]], bank[:])
             return h1
 
-        a0, b0 = factors(0)
-        a1, b1 = factors(1)
-        products0 = placed("products0", [P, 2, S], F32, GATE_LAST)
-        multiply(products0, a0, b0)
-        h1 = [turn(0, products0)]
-        products1 = placed("products1", [P, 2, S], F32, b_bytes(0))
-        multiply(products1, a1, b1)
-        h1.append(turn(1, products1))
-        a2, b2 = factors(2)
-        a3, b3 = factors(3)
+        def gate_h1(t, offset):
+            gated = placed("gated1_%d" % t, [P, S], F32, offset)
+            gate_and_scatter(pages[t], list3, gated, h1[t], gates1[t], 1)
 
+        factor_tiles = [factors(0), factors(1)]
+        whole = [slice(0, S)]
+        h1 = [turn(0, multiply(0, GATE_LAST, halves), H1_FIRST)]
+        h1.append(turn(1, multiply(1, b_bytes(0), whole), a_bytes(1)))
+        gate_h1(0, PRODUCTS1)
+        factor_tiles.extend([factors(2), factors(3)])
+
+        h1.append(turn(2, multiply(2, H1_FIRST - 4 * KIB, whole), a_bytes(2)))
         wo_bf = placed("wo_bf", [P, PACK * N], BF16, b_bytes(0))
-        round_weight(wo_bf[:], wo_raw)
+        round_weight(wo_bf[:].rearrange("p (t c) -> p t c", t=PACK), wo_raw, 1.0)
 
         chunk_cols = [slice(sum(CHUNKS[:c]), sum(CHUNKS[: c + 1])) for c in range(len(CHUNKS))]
         z_all = placed("z", [P, T2 * PACK], BF16, Z)
@@ -295,26 +307,13 @@ def tile_list_woven_link_features_kernel(
             for c in range(len(CHUNKS)):
                 round_page(t, c)
 
-        def place_h1(t, offset):
-            gated = placed("gated1_%d" % t, [P, S], F32, offset)
-            gate_and_scatter(pages[t], list3, gated, h1[t], gates1[t], 1)
-
-        place_h1(0, PRODUCTS1)
-        products2 = placed("products2", [P, 2, S], F32, a_bytes(0))
-        multiply(products2, a2, b2)
-        h1.append(turn(2, products2))
-        gains = placed("gains", [P, PACK], F32, a_bytes(0))
-        nc.sync.dma_start(gains[:], gain.rearrange("(p t) -> p t", t=PACK))
-        round_whole_page(0)
-        place_h1(1, b_bytes(1))
-        round_whole_page(1)
-        place_h1(2, H2 + 8 * KIB)
-        round_whole_page(2)
-        h1_last = placed("h1_last", [P, S], F32, a_bytes(1) + 4 * KIB)
-        for half, cols in enumerate(halves):
-            products = placed("products3_%d" % half, [P, 2, HALF], F32, a_bytes(1 + half))
-            nc.gpsimd.tensor_tensor(products[:], a3[:, :, cols], b3[:, :, cols], MULT)
-            nc.gpsimd.tensor_tensor(h1_last[:, cols], products[:, 0, :], products[:, 1, :], SUB)
+        gate_h1(1, b_bytes(2))
+        gate_h1(2, H2 + 8 * KIB)
+        products = multiply(LAST, a_bytes(2), whole)
+        h1_last = placed("h1_last", [P, S], F32, a_bytes(1))
+        nc.gpsimd.tensor_tensor(h1_last[:], products[:, 0, :], products[:, 1, :], ADD)
+        for t in range(LAST):
+            round_whole_page(t)
         wo_codes = placed("wo_codes", [P, N], U32, H2 + 8 * KIB)
         wo_plane = placed("wo_plane", [P, N], U8, H2 + 8 * KIB + 4 * N)
         nc.vector.quantize_mx(wo_codes[:].bitcast(FP8X4), wo_plane[:], wo_bf[:])
@@ -334,7 +333,7 @@ def tile_list_woven_link_features_kernel(
             if c not in on_scalar:
                 round_page(LAST, c)
             nc.vector.quantize_mx(z_codes[:, cols].bitcast(FP8X4), z_plane[:, cols], z_flat[c])
-            y = placed("y%d" % c, [P, PACK, w], F32, a_bytes(1) + 4 * PACK * cols.start)
+            y = placed("y%d" % c, [P, PACK, w], F32, a_bytes(2) + 4 * PACK * cols.start)
             per_bank = BANK // w
             for first in range(0, PACK, per_bank):
                 bank = take(banks)[:].rearrange("p (i m) -> p i m", m=w)
@@ -349,7 +348,7 @@ def tile_list_woven_link_features_kernel(
 
         def store_codes(c, y):
             w, cols = CHUNKS[c], chunk_cols[c]
-            grouped = placed("y_bf%d" % c, [P, w, PACK], BF16, a_bytes(LAST) + 2 * PACK * cols.start)
+            grouped = placed("y_bf%d" % c, [P, w, PACK], BF16, a_bytes(0) + 2 * PACK * cols.start)
             dst = grouped[:].rearrange("p (c i) t -> p c t i", i=PACK)
             src = y[:].rearrange("p t (c i) -> p c t i", i=PACK)
             if c == len(CHUNKS) - 1:

@@ -28,8 +28,8 @@ BANK = 512
 LIST_COLS = S // 16
 HALF = S // 2
 CHUNKS = (256, 256, 512, 512, 256, 256)
-CODE_STORE = 512
-SCALAR_LAST_PAGE_CHUNKS = 1
+CODE_STORES = (0, 512, 1024, 1536, 2048)
+SCALAR_LAST_PAGE_CHUNKS = 2
 KIB = 1024
 FACTORS = 0
 OVERHANG = 64
@@ -42,8 +42,8 @@ H2 = 108 * KIB
 Z = 124 * KIB
 H1_FIRST = Z + 16 * KIB
 PICKED1 = 144 * KIB
-WA_CODES = 149 * KIB
-GATE_LAST = 153 * KIB
+WA_CODES = 150 * KIB
+GATE_LAST = 154 * KIB
 LINK_TILES = HALF // P
 
 
@@ -120,16 +120,16 @@ def tile_list_woven_link_features_kernel(
             )
             return dealt
 
-        tab2_plane = zeroed_plane(kept("tab2_plane", [P, T], U8), nc.gpsimd)
-        tab_plane = zeroed_plane(kept("tab_plane", [P, T], U8), nc.vector)
         wsp_plane = zeroed_plane(placed("wsp_plane", [P, H], U8, PICKED1 + 4 * S), nc.gpsimd)
+        tab2_plane = zeroed_plane(kept("tab2_plane", [P, T], U8), nc.vector)
+        tab_plane = zeroed_plane(kept("tab_plane", [P, T], U8), nc.vector)
         wb_plane = zeroed_plane(placed("wb_plane", [P, 2 * H], U8, WA_CODES + 4 * H), nc.gpsimd)
 
         list2 = load_list("list2", offs2)
         tab2 = load_e4m3_words(placed("tab2", [P, T], I32, a_bytes(LAST)), tab2_words)
-        load_plane(tab2_plane, tab2_scales, nc.sync)
         wsp = load_e4m3_words(placed("wsp", [P, H], I32, PICKED1), wsp_words)
         load_plane(wsp_plane, wsp_scales, nc.sync)
+        load_plane(tab2_plane, tab2_scales, nc.sync)
         list1 = load_list("list1", offs)
         tab1 = load_e4m3_words(placed("tab1", [P, T], I32, b_bytes(LAST)), tab_words)
         load_plane(tab_plane, tab_scales, nc.sync)
@@ -162,12 +162,15 @@ def tile_list_woven_link_features_kernel(
             ring.append(bank)
             return bank
 
-        def gather(words, scale, table, plane, offsets, word_pieces):
-            nc.vector.tensor_copy(scale[:], plane[:].indirect(offsets[:]))
-            n, c = S // word_pieces, LIST_COLS // word_pieces
-            for i in range(word_pieces):
-                nc.vector.tensor_copy(words[:, i * n : (i + 1) * n], table[:].bitcast(U32).indirect(offsets[:, i * c : (i + 1) * c]))
-            return words, scale
+        def gather_words(words, table, offsets):
+            nc.vector.tensor_copy(words[:], table[:].bitcast(U32).indirect(offsets[:]))
+            return words
+
+        def gather_scales(scale, plane, offsets, pieces):
+            n, c = S // pieces, LIST_COLS // pieces
+            for i in range(pieces):
+                nc.vector.tensor_copy(scale[:, i * n : (i + 1) * n], plane[:].indirect(offsets[:, i * c : (i + 1) * c]))
+            return scale
 
         halves = [slice(half * HALF, (half + 1) * HALF) for half in range(2)]
 
@@ -186,21 +189,28 @@ def tile_list_woven_link_features_kernel(
         def rows(t, first=0):
             return slice(first + t * P, first + (t + 1) * P)
 
-        picked2 = gather(kept("words2", [P, S], U32), kept("scale2", [P, S], U8), tab2, tab2_plane, list2, 2)
+        words2 = gather_words(kept("words2", [P, S], U32), tab2, list2)
         wsp_d = deal(kept("wsp_d", [P, H], I32), wsp[:], 1)
         wsp_plane_d = deal(kept("wsp_plane_d", [P, H], U8), wsp_plane[:], 1)
-        picked1 = gather(placed("words1", [P, S], U32, PICKED1), placed("scale1", [P, S], U8, PICKED1 + 4 * S), tab1, tab_plane, list1, 1)
+        picked2 = words2, gather_scales(placed("scale2", [P, S], U8, PICKED1 + 4 * S), tab2_plane, list2, 2)
+        scale1 = gather_scales(placed("scale1", [P, S], U8, PICKED1 + 4 * S + S), tab_plane, list1, 1)
+        picked1 = gather_words(placed("words1", [P, S], U32, PICKED1), tab1, list1), scale1
 
         h2_next = placed("h2_next", [P, 2, S], F32, H2 + 4 * KIB)
         h2 = [placed("h2_0", [P, S], F32, H2), h2_next[:, 0, :], h2_next[:, 1, :], placed("h2_last", [P, S], F32, H2 + 12 * KIB)]
-        for t in range(PACK):
+
+        def spatial_sums(t):
             for cols in halves:
                 first_product(h2[t], wsp_d[:, rows(t)].bitcast(FP8X4), wsp_plane_d[:, rows(t)], picked2, cols)
+
+        for t in range(LAST):
+            spatial_sums(t)
 
         wa_bf = placed("wa_bf", [P, 2 * PACK * H + OVERHANG], BF16, PAGES - OVERHANG)[:, : 2 * PACK * H]
         wa_by_weight = wa_bf.rearrange("p (t w c) -> p w t c", t=PACK, w=2)
         round_weight(wa_by_weight[:, 0], war_raw, 1.0)
         round_weight(wa_by_weight[:, 1], wai_raw, -1.0)
+        spatial_sums(LAST)
 
         def new_page(t):
             return placed("page%d" % t, [P, T2], F32, PAGES + 8 * KIB * PAGE_ORDER.index(t))
@@ -213,7 +223,7 @@ def tile_list_woven_link_features_kernel(
                 nc.vector.tensor_copy(page[:].indirect(offsets[:, i * c : (i + 1) * c]), gated[:, cols])
 
         pages = [new_page(0)]
-        gate_and_scatter(pages[0], list4, h2[0], h2[0], gates2[0], 2)
+        gate_and_scatter(pages[0], list4, h2[0], h2[0], gates2[0], 1)
         wb_d = deal(placed("wb_d", [P, 2 * H], U16, H2), wb[:], 2)
         wb_plane_d = deal(placed("wb_plane_d", [P, 2 * H], U8, H2 + 4 * H), wb_plane[:], 2)
         wa_codes = placed("wa_codes", [P, 2 * H], U32, WA_CODES)
@@ -356,8 +366,8 @@ def tile_list_woven_link_features_kernel(
             else:
                 nc.vector.tensor_copy(dst, src)
             nc.vector.quantize_mx(y_codes[:, cols].bitcast(FP8X4), y_plane[:, cols], grouped[:].rearrange("p m t -> p (m t)"))
-            if cols.stop % CODE_STORE == 0:
-                stored = slice(cols.stop - CODE_STORE, cols.stop)
+            if cols.stop in CODE_STORES:
+                stored = slice(CODE_STORES[CODE_STORES.index(cols.stop) - 1], cols.stop)
                 nc.sync.dma_start(out_words[:, stored], y_codes[:, stored].bitcast(I32))
 
         ys = [last_product(c) for c in range(len(CHUNKS))]

@@ -29,15 +29,13 @@ LIST_COLS = S // 16
 HALF = S // 2
 CHUNKS = (256, 256, 512, 512, 256, 256)
 CODE_STORES = (0, 512, 1024, 1536, 2048)
-SCALAR_LAST_PAGE_CHUNKS = 2
+SCALAR_LAST_PAGE_CHUNKS = 1
 KIB = 1024
 FACTORS = 0
-OVERHANG = 64
 PRODUCTS1 = 64 * KIB
-GATES_NEXT = PRODUCTS1 + OVERHANG
-GATED = 72 * KIB
+GATED = 68 * KIB
 PAGES = 76 * KIB
-PAGE_ORDER = (1, 2, 0, 3)
+PAGE_ORDER = (1, 0, 2, 3)
 H2 = 108 * KIB
 Z = 124 * KIB
 H1_FIRST = Z + 16 * KIB
@@ -129,20 +127,21 @@ def tile_list_woven_link_features_kernel(
         tab2 = load_e4m3_words(placed("tab2", [P, T], I32, a_bytes(LAST)), tab2_words)
         wsp = load_e4m3_words(placed("wsp", [P, H], I32, PICKED1), wsp_words)
         load_plane(wsp_plane, wsp_scales, nc.sync)
+        tab1 = load_e4m3_words(placed("tab1", [P, T], I32, b_bytes(LAST)), tab_words)
         load_plane(tab2_plane, tab2_scales, nc.sync)
         list1 = load_list("list1", offs)
-        tab1 = load_e4m3_words(placed("tab1", [P, T], I32, b_bytes(LAST)), tab_words)
         load_plane(tab_plane, tab_scales, nc.sync)
         list4 = load_list("list4", offs4)
-        gate2_next = placed("gate2_next", [P, 2, S], F32, GATES_NEXT)
-        gates2 = load_gates(kept("gate2_0", [P, 1, S], F32), wg2, 0, 1) + load_gates(gate2_next, wg2, 1, 2)
+        gates2 = load_gates(kept("gate2_0", [P, 1, S], F32), wg2, 0, 1)
         war_raw = load_weight("war_raw", war, a_bytes(0))
+        gates2.extend(load_gates(kept("gate2_1", [P, 1, S], F32), wg2, 1, 1))
         wai_raw = load_weight("wai_raw", wai, b_bytes(0))
         wb = placed("wb", [P, 2 * H], U16, WA_CODES)
         for i, words in enumerate((wbr_words, wbi_words)):
             nc.sync.dma_start(wb[:, i * H : (i + 1) * H].bitcast(I32), words[0].bitcast(I32))
         for i, scales in enumerate((wbr_scales, wbi_scales)):
             load_plane(wb_plane[:, i * H : (i + 1) * H], scales, nc.sync)
+        gates2.extend(load_gates(kept("gate2_2", [P, 1, S], F32), wg2, 2, 1))
         gates2.extend(load_gates(placed("gate2_last", [P, 1, S], F32, GATE_LAST), wg2, LAST, 1))
         list3 = load_list("list3", offs3)
         gates1 = load_gates(kept("gate1", [P, PACK, S], F32), wg1, 0, PACK)
@@ -196,8 +195,7 @@ def tile_list_woven_link_features_kernel(
         scale1 = gather_scales(placed("scale1", [P, S], U8, PICKED1 + 4 * S + S), tab_plane, list1, 1)
         picked1 = gather_words(placed("words1", [P, S], U32, PICKED1), tab1, list1), scale1
 
-        h2_next = placed("h2_next", [P, 2, S], F32, H2 + 4 * KIB)
-        h2 = [placed("h2_0", [P, S], F32, H2), h2_next[:, 0, :], h2_next[:, 1, :], placed("h2_last", [P, S], F32, H2 + 12 * KIB)]
+        h2 = [placed("h2_%d" % t, [P, S], F32, H2 + 4 * KIB * t) for t in range(PACK)]
 
         def spatial_sums(t):
             for cols in halves:
@@ -206,7 +204,7 @@ def tile_list_woven_link_features_kernel(
         for t in range(LAST):
             spatial_sums(t)
 
-        wa_bf = placed("wa_bf", [P, 2 * PACK * H + OVERHANG], BF16, PAGES - OVERHANG)[:, : 2 * PACK * H]
+        wa_bf = placed("wa_bf", [P, 2 * PACK * H], BF16, PAGES - 4 * KIB)[:]
         wa_by_weight = wa_bf.rearrange("p (t w c) -> p w t c", t=PACK, w=2)
         round_weight(wa_by_weight[:, 0], war_raw, 1.0)
         round_weight(wa_by_weight[:, 1], wai_raw, -1.0)
@@ -229,12 +227,11 @@ def tile_list_woven_link_features_kernel(
         wa_codes = placed("wa_codes", [P, 2 * H], U32, WA_CODES)
         wa_plane = keep.tile([P, 2 * H], U8, name="wa_plane", align_bytes=64)
         nc.vector.quantize_mx(wa_codes[:].bitcast(FP8X4), wa_plane[:], wa_bf)
-        pages.extend(new_page(t) for t in range(1, PACK))
-        nc.gpsimd.tensor_tensor(h2_next[:], h2_next[:], gate2_next[:], MULT)
-        for t in range(1, LAST):
-            nc.vector.tensor_copy(pages[t][:].indirect(list4[:]), h2[t])
-        gated_last = placed("gated_last", [P, S], F32, GATED)
-        gate_and_scatter(pages[LAST], list4, gated_last, h2[LAST], gates2[LAST], 1)
+        gated_rest = placed("gated_rest", [P, 2, S], F32, GATED)
+        for t in range(1, PACK):
+            pages.append(new_page(t))
+            gated = h2[t] if t == 1 else gated_rest[:, t - 2, :]
+            gate_and_scatter(pages[t], list4, gated, h2[t], gates2[t], 1)
 
         def factors_by_link(dst, weights, plane, pair):
             words, scale = picked1

@@ -27,7 +27,8 @@ SCALE_ROWS = 4
 BANK = 512
 LIST_COLS = S // 16
 HALF = S // 2
-CHUNKS = (256, 256, 512, 512, 256, 256)
+CHUNKS = (256, 256, 512, 512, 512)
+STORE_ROWS = (2, 2, 2, 2, 2)
 CODE_STORES = (0, 512, 1024, 1536, 2048)
 SCALAR_LAST_PAGE_CHUNKS = 1
 KIB = 1024
@@ -350,15 +351,18 @@ def tile_list_woven_link_features_kernel(
                         rhs=z_codes[:, cols].bitcast(FP8X4), rhs_scale=z_plane[:, cols], start=True, stop=True,
                     )
                 nc.scalar.copy(y[:, first : first + per_bank, :], bank)
-            nc.scalar.dma_start(out_rows[:, :, cols], y[:])
+                done = first + per_bank
+                if done % STORE_ROWS[c] == 0:
+                    stored = slice(done - STORE_ROWS[c], done)
+                    nc.sync.dma_start(out_rows[:, stored, cols], y[:, stored, :])
             return y
 
-        def store_codes(c, y):
-            w, cols = CHUNKS[c], chunk_cols[c]
-            grouped = placed("y_bf%d" % c, [P, w, PACK], BF16, a_bytes(0) + 2 * PACK * cols.start)
+        def store_codes(c, y, first, w, on_scalar):
+            cols = slice(chunk_cols[c].start + first, chunk_cols[c].start + first + w)
+            grouped = placed("y_bf%d_%d" % (c, first), [P, w, PACK], BF16, a_bytes(0) + 2 * PACK * cols.start)
             dst = grouped[:].rearrange("p (c i) t -> p c t i", i=PACK)
-            src = y[:].rearrange("p t (c i) -> p c t i", i=PACK)
-            if c == len(CHUNKS) - 1:
+            src = y[:, :, first : first + w].rearrange("p t (c i) -> p c t i", i=PACK)
+            if on_scalar:
                 nc.scalar.copy(dst, src)
             else:
                 nc.vector.tensor_copy(dst, src)
@@ -368,7 +372,10 @@ def tile_list_woven_link_features_kernel(
                 nc.sync.dma_start(out_words[:, stored], y_codes[:, stored].bitcast(I32))
 
         ys = [last_product(c) for c in range(len(CHUNKS))]
-        for c, y in enumerate(ys):
-            store_codes(c, y)
+        for c, y in enumerate(ys[:-1]):
+            store_codes(c, y, 0, CHUNKS[c], False)
+        half = CHUNKS[-1] // 2
+        store_codes(len(CHUNKS) - 1, ys[-1], 0, half, False)
+        store_codes(len(CHUNKS) - 1, ys[-1], half, half, True)
         for q in range(QUADRANTS):
             (nc.scalar, nc.sync)[q % 2].dma_start(scale_rows(out_2, q), plane_rows(y_plane, q))

@@ -21,29 +21,29 @@ ADD = mybir.AluOpType.add
 P = 128
 PACK = 4
 LAST = PACK - 1
+RUN = 4
 QUADRANTS = 4
 QUADRANT = P // QUADRANTS
+QUADRANT_ORDER = (0, 2, 1, 3)
 SCALE_ROWS = 4
 BANK = 512
 LIST_COLS = S // 16
 HALF = S // 2
-CHUNKS = (256, 256, 512, 512, 512)
-STORE_ROWS = (2, 2, 2, 2, 2)
-CODE_STORES = (0, 512, 1024, 1536, 2048)
-SCALAR_LAST_PAGE_CHUNKS = 1
-KIB = 1024
-FACTORS = 0
-PRODUCTS1 = 64 * KIB
-GATED = 68 * KIB
-PAGES = 76 * KIB
-PAGE_ORDER = (1, 0, 2, 3)
-H2 = 108 * KIB
-Z = 124 * KIB
-H1_FIRST = Z + 16 * KIB
-PICKED1 = 144 * KIB
-WA_CODES = 150 * KIB
-GATE_LAST = 154 * KIB
 LINK_TILES = HALF // P
+CHUNKS = (256, 256, 512, 512, 512)
+STORE_ROWS = 2
+CODE_STORE = 512
+KIB = 1024
+B_FACTORS = 0
+A_FACTORS = 32 * KIB
+FACTOR_PLACES = (0, 1, 2, 0, 1, 5, 6, 7)
+STREAMS = 64 * KIB
+PAGES = 80 * KIB
+GATES2 = 112 * KIB
+GATES1 = 128 * KIB
+GATE1_ORDER = (1, 0, 2, 3)
+WA_ROUNDED = 144 * KIB
+WORDS1 = 152 * KIB
 
 
 def tile_list_woven_link_features_kernel(
@@ -64,11 +64,17 @@ def tile_list_woven_link_features_kernel(
         def kept(name, shape, dtype):
             return keep.tile(shape, dtype, name=name, align_bytes=64)
 
-        def a_bytes(t):
-            return FACTORS + 16 * KIB * t
+        def page_bytes(t):
+            return PAGES + 8 * KIB * t
 
-        def b_bytes(t):
-            return a_bytes(t) + 8 * KIB
+        def a_bytes(t, half):
+            return A_FACTORS + 8 * KIB * t + 4 * KIB * half
+
+        def gate2_bytes(t):
+            return GATES2 + 4 * KIB * t
+
+        def gate1_bytes(t):
+            return GATES1 + 4 * KIB * GATE1_ORDER.index(t)
 
         def load_list(name, offsets):
             tile = lists.tile([P, LIST_COLS], U16, name=name)
@@ -85,75 +91,65 @@ def tile_list_woven_link_features_kernel(
         def scale_rows(scales, q):
             return scales[0, SCALE_ROWS * q : SCALE_ROWS * (q + 1), :].bitcast(I32)
 
-        def load_plane(plane, scales, queue):
-            for q in range(QUADRANTS):
-                queue.dma_start(plane_rows(plane, q), scale_rows(scales, q))
+        def load_plane(plane, scales):
+            for q in QUADRANT_ORDER:
+                nc.sync.dma_start(plane_rows(plane, q), scale_rows(scales, q))
 
         def load_e4m3_words(tile, words):
             nc.sync.dma_start(tile[:], words[0].rearrange("p c i -> p (c i)").bitcast(I32))
             return tile
 
-
-        def load_gates(tile, wg, first, count):
-            rows = wg.rearrange("(p t) j -> p t j", t=PACK)[:, first : first + count, :]
-            for q in range(QUADRANTS):
+        def load_gate(name, wg, t, offset):
+            tile = placed(name, [P, S], F32, offset)
+            rows = wg.rearrange("(a t b) j -> t a b j", t=PACK, b=RUN)[t]
+            for q in QUADRANT_ORDER:
                 nc.sync.dma_start(tile[QUADRANT * q : QUADRANT * (q + 1)], rows)
-            return [tile[:, i, :] for i in range(count)]
+            return tile
 
-        def load_weight(name, w, offset):
-            raw = placed(name, [P, PACK, H], F32, offset)
-            nc.sync.dma_start(raw[:], w.rearrange("(p i) c -> p i c", i=PACK))
+        def load_gain(t, tile):
+            nc.sync.dma_start(tile[:], gain.rearrange("(a t b o) -> t a b o", t=PACK, b=RUN, o=1)[t])
+            return tile
+
+        def load_weight(name, w, offset, first, width):
+            raw = placed(name, [P, PACK, width], F32, offset)
+            nc.sync.dma_start(raw[:], w.rearrange("(p i) c -> p i c", i=PACK)[:, :, first : first + width])
             return raw
 
-        def round_weight(dealt, raw, sign):
-            dst = dealt.rearrange("p t (m i) -> p m t i", i=PACK)
-            src = raw[:].rearrange("p i (m t) -> p m t i", t=PACK)
-            for half in range(2):
-                ms = slice(half * P // 2, (half + 1) * P // 2)
-                nc.scalar.activation(dst[:, ms], src[:, ms], COPY, scale=sign)
-
-        def deal(dealt, raw, weights):
-            nc.vector.tensor_copy(
-                dealt[:].rearrange("p (t w m) -> p w t m", t=PACK, w=weights),
-                raw.rearrange("p (w m t) -> p w t m", t=PACK, w=weights),
-            )
-            return dealt
-
-        wsp_plane = zeroed_plane(placed("wsp_plane", [P, H], U8, PICKED1 + 4 * S), nc.gpsimd)
-        tab2_plane = zeroed_plane(kept("tab2_plane", [P, T], U8), nc.vector)
+        tab2_plane = zeroed_plane(kept("tab2_plane", [P, T], U8), nc.gpsimd)
+        wsp_plane = zeroed_plane(kept("wsp_plane", [P, H], U8), nc.vector)
         tab_plane = zeroed_plane(kept("tab_plane", [P, T], U8), nc.vector)
-        wb_plane = zeroed_plane(placed("wb_plane", [P, 2 * H], U8, WA_CODES + 4 * H), nc.gpsimd)
+        wb_plane = zeroed_plane(placed("wb_plane", [P, 2 * H], U8, page_bytes(1) + 2 * KIB), nc.vector)
 
         list2 = load_list("list2", offs2)
-        tab2 = load_e4m3_words(placed("tab2", [P, T], I32, a_bytes(LAST)), tab2_words)
-        wsp = load_e4m3_words(placed("wsp", [P, H], I32, PICKED1), wsp_words)
-        load_plane(wsp_plane, wsp_scales, nc.sync)
-        tab1 = load_e4m3_words(placed("tab1", [P, T], I32, b_bytes(LAST)), tab_words)
-        load_plane(tab2_plane, tab2_scales, nc.sync)
         list1 = load_list("list1", offs)
-        load_plane(tab_plane, tab_scales, nc.sync)
         list4 = load_list("list4", offs4)
-        gates2 = load_gates(kept("gate2_0", [P, 1, S], F32), wg2, 0, 1)
-        war_raw = load_weight("war_raw", war, a_bytes(0))
-        gates2.extend(load_gates(kept("gate2_1", [P, 1, S], F32), wg2, 1, 1))
-        wai_raw = load_weight("wai_raw", wai, b_bytes(0))
-        wb = placed("wb", [P, 2 * H], U16, WA_CODES)
-        for i, words in enumerate((wbr_words, wbi_words)):
-            nc.sync.dma_start(wb[:, i * H : (i + 1) * H].bitcast(I32), words[0].bitcast(I32))
+        load_plane(tab2_plane, tab2_scales)
+        tab2 = load_e4m3_words(placed("tab2", [P, T], I32, page_bytes(0)), tab2_words)
+        wsp = load_e4m3_words(kept("wsp", [P, H], I32), wsp_words)
+        load_plane(wsp_plane, wsp_scales)
+        tab1 = load_e4m3_words(kept("tab1", [P, T], I32), tab_words)
+        gates2 = [load_gate("gate2_0", wg2, 0, gate2_bytes(0))]
+        load_plane(tab_plane, tab_scales)
+        war_raw = load_weight("war_raw", war, page_bytes(LAST), 0, H)
+        gates2.append(load_gate("gate2_1", wg2, 1, gate2_bytes(1)))
+        wai_raw = [load_weight("wai_raw%d" % i, wai, page_bytes(2) + 4 * KIB * i, i * H // 2, H // 2) for i in range(2)]
         for i, scales in enumerate((wbr_scales, wbi_scales)):
-            load_plane(wb_plane[:, i * H : (i + 1) * H], scales, nc.sync)
-        gates2.extend(load_gates(kept("gate2_2", [P, 1, S], F32), wg2, 2, 1))
-        gates2.extend(load_gates(placed("gate2_last", [P, 1, S], F32, GATE_LAST), wg2, LAST, 1))
+            load_plane(wb_plane[:, i * H : (i + 1) * H], scales)
+        wb = placed("wb", [P, 2, H // 2], I32, page_bytes(1))
+        for i, words in enumerate((wbr_words, wbi_words)):
+            nc.sync.dma_start(wb[:, i, :], words[0].bitcast(I32))
+        gates2.extend(load_gate("gate2_%d" % t, wg2, t, gate2_bytes(t)) for t in range(2, PACK))
         list3 = load_list("list3", offs3)
-        gates1 = load_gates(kept("gate1", [P, PACK, S], F32), wg1, 0, PACK)
-        wo_raw = load_weight("wo_raw", wo, Z)
-
-        gains = keep.tile([P, PACK], F32, name="gains")
-        nc.sync.dma_start(gains[:], gain.rearrange("(p t) -> p t", t=PACK))
+        gates1 = [load_gate("gate1_0", wg1, 0, gate1_bytes(0))]
+        wo_raw = kept("wo_raw", [P, PACK, N], F32)
+        for t in range(PACK):
+            nc.sync.dma_start(wo_raw[:, t, :], wo.rearrange("(a t b) n -> t a b n", t=PACK, b=RUN)[t])
+        gates1.append(load_gate("gate1_1", wg1, 1, gate1_bytes(1)))
+        gains = {t: load_gain(t, kept("gain%d" % t, [P, 1], F32)) for t in (0, LAST)}
+        gates1.extend(load_gate("gate1_%d" % t, wg1, t, gate1_bytes(t)) for t in range(2, PACK))
 
         banks = [psum.tile([P, BANK], F32, name="bank%d" % b) for b in range(8)]
-
-        scalar_banks, turn_banks = banks[:6], banks[6:]
+        sum_banks, turn_banks = banks[:6], banks[6:]
         ident = keep.tile([P, P], F32)
         make_identity(nc, ident[:])
 
@@ -162,204 +158,207 @@ def tile_list_woven_link_features_kernel(
             ring.append(bank)
             return bank
 
-        def gather_words(words, table, offsets):
-            nc.vector.tensor_copy(words[:], table[:].bitcast(U32).indirect(offsets[:]))
-            return words
-
-        def gather_scales(scale, plane, offsets, pieces):
-            n, c = S // pieces, LIST_COLS // pieces
-            for i in range(pieces):
-                nc.vector.tensor_copy(scale[:, i * n : (i + 1) * n], plane[:].indirect(offsets[:, i * c : (i + 1) * c]))
-            return scale
+        def gather(picked, table, offsets):
+            nc.vector.tensor_copy(picked[:], table.indirect(offsets[:]))
+            return picked
 
         halves = [slice(half * HALF, (half + 1) * HALF) for half in range(2)]
 
-        def first_sums(ring, weight, plane, picked, cols):
-            words, scale = picked
-            bank = take(ring)
-            nc.tensor.matmul_mx(
-                bank[:], lhsT=weight, lhsT_scale=plane,
-                rhs=words[:, cols].bitcast(FP8X4), rhs_scale=scale[:, cols], start=True, stop=True,
-            )
-            return bank
+        scale2 = gather(kept("scale2", [P, S], U8), tab2_plane[:], list2)
+        words2 = gather(kept("words2", [P, S], U32), tab2[:].bitcast(U32), list2)
+        wsp_dealt = kept("wsp_dealt", [P, H], I32)
+        nc.vector.tensor_copy(
+            wsp_dealt[:].rearrange("p (t a b) -> p t a b", t=PACK, b=RUN),
+            wsp[:].rearrange("p (a t b) -> p t a b", t=PACK, b=RUN),
+        )
+        wsp_plane_dealt = kept("wsp_plane_dealt", [P, H], U8)
+        nc.vector.tensor_copy(
+            wsp_plane_dealt[:].bitcast(I32).rearrange("p (t a) -> p t a", t=PACK),
+            wsp_plane[:].bitcast(I32).rearrange("p (a t) -> p t a", t=PACK),
+        )
+        words1 = gather(placed("words1", [P, S], U32, WORDS1), tab1[:].bitcast(U32), list1)
 
-        def first_product(dst, weight, plane, picked, cols):
-            nc.scalar.copy(dst[:, cols], first_sums(scalar_banks, weight, plane, picked, cols)[:])
-
-        def rows(t, first=0):
-            return slice(first + t * P, first + (t + 1) * P)
-
-        words2 = gather_words(kept("words2", [P, S], U32), tab2, list2)
-        wsp_d = deal(kept("wsp_d", [P, H], I32), wsp[:], 1)
-        wsp_plane_d = deal(kept("wsp_plane_d", [P, H], U8), wsp_plane[:], 1)
-        picked2 = words2, gather_scales(placed("scale2", [P, S], U8, PICKED1 + 4 * S), tab2_plane, list2, 2)
-        scale1 = gather_scales(placed("scale1", [P, S], U8, PICKED1 + 4 * S + S), tab_plane, list1, 1)
-        picked1 = gather_words(placed("words1", [P, S], U32, PICKED1), tab1, list1), scale1
-
-        h2 = [placed("h2_%d" % t, [P, S], F32, H2 + 4 * KIB * t) for t in range(PACK)]
-
-        def spatial_sums(t):
+        h2 = [placed("h2_%d" % t, [P, S], F32, STREAMS + 4 * KIB * t) for t in range(PACK)]
+        for t in range(PACK):
+            rows = slice(t * P, (t + 1) * P)
             for cols in halves:
-                first_product(h2[t], wsp_d[:, rows(t)].bitcast(FP8X4), wsp_plane_d[:, rows(t)], picked2, cols)
-
-        for t in range(LAST):
-            spatial_sums(t)
-
-        wa_bf = placed("wa_bf", [P, 2 * PACK * H], BF16, PAGES - 4 * KIB)[:]
-        wa_by_weight = wa_bf.rearrange("p (t w c) -> p w t c", t=PACK, w=2)
-        round_weight(wa_by_weight[:, 0], war_raw, 1.0)
-        round_weight(wa_by_weight[:, 1], wai_raw, -1.0)
-        spatial_sums(LAST)
-
-        def new_page(t):
-            return placed("page%d" % t, [P, T2], F32, PAGES + 8 * KIB * PAGE_ORDER.index(t))
-
-        def gate_and_scatter(page, offsets, gated, stream, gate, pieces):
-            n, c = S // pieces, LIST_COLS // pieces
-            for i in range(pieces):
-                cols = slice(i * n, (i + 1) * n)
-                nc.gpsimd.tensor_tensor(gated[:, cols], stream[:, cols], gate[:, cols], MULT)
-                nc.vector.tensor_copy(page[:].indirect(offsets[:, i * c : (i + 1) * c]), gated[:, cols])
-
-        pages = [new_page(0)]
-        gate_and_scatter(pages[0], list4, h2[0], h2[0], gates2[0], 1)
-        wb_d = deal(placed("wb_d", [P, 2 * H], U16, H2), wb[:], 2)
-        wb_plane_d = deal(placed("wb_plane_d", [P, 2 * H], U8, H2 + 4 * H), wb_plane[:], 2)
-        wa_codes = placed("wa_codes", [P, 2 * H], U32, WA_CODES)
-        wa_plane = keep.tile([P, 2 * H], U8, name="wa_plane", align_bytes=64)
-        nc.vector.quantize_mx(wa_codes[:].bitcast(FP8X4), wa_plane[:], wa_bf)
-        gated_rest = placed("gated_rest", [P, 2, S], F32, GATED)
-        for t in range(1, PACK):
-            pages.append(new_page(t))
-            gated = h2[t] if t == 1 else gated_rest[:, t - 2, :]
-            gate_and_scatter(pages[t], list4, gated, h2[t], gates2[t], 1)
-
-        def factors_by_link(dst, weights, plane, pair):
-            words, scale = picked1
-            bank = take(scalar_banks)
-            for lt in range(2):
-                links = slice((2 * pair + lt) * P, (2 * pair + lt + 1) * P)
+                bank = take(sum_banks)
                 nc.tensor.matmul_mx(
-                    bank[:, 2 * P * lt : 2 * P * (lt + 1)], lhsT=words[:, links].bitcast(FP8X4), lhsT_scale=scale[:, links],
-                    rhs=weights, rhs_scale=plane, start=True, stop=True,
+                    bank[:], lhsT=wsp_dealt[:, rows].bitcast(FP8X4), lhsT_scale=wsp_plane_dealt[:, rows],
+                    rhs=words2[:, cols].bitcast(FP8X4), rhs_scale=scale2[:, cols], start=True, stop=True,
                 )
-            places = dst[:, :, 2 * P * pair : 2 * P * (pair + 1)].rearrange("p i (lt m) -> p lt i m", lt=2)
-            nc.scalar.copy(places, bank[:].rearrange("p (lt i m) -> p lt i m", lt=2, i=2))
+                nc.scalar.copy(h2[t][:, cols], bank[:])
 
-        def factors(t):
-            a = placed("a_%d" % t, [P, 2, S], F32, a_bytes(t))
-            b = placed("b_%d" % t, [P, 2, S], F32, b_bytes(t))
-            for half in range(2):
-                for dst, codes, plane, dtype in ((b, wb_d, wb_plane_d, FP4X4), (a, wa_codes, wa_plane, FP8X4)):
-                    for i in range(2):
-                        if t == LAST:
-                            cols = rows(2 * t + i)
-                            first_product(dst[:, i, :], codes[:, cols].bitcast(dtype), plane[:, cols], picked1, halves[half])
-                        else:
-                            cols = slice(2 * P * t, 2 * P * (t + 1))
-                            factors_by_link(dst, codes[:, cols].bitcast(dtype), plane[:, cols], 2 * half + i)
+        pages = [placed("page%d" % t, [P, T2], F32, page_bytes(t)) for t in range(PACK)]
+
+        def gate_and_scatter(page, offsets, gated, stream, gate, cols):
+            nc.gpsimd.tensor_tensor(gated[:, cols], stream[:, cols], gate[:, cols], MULT)
+            nc.vector.tensor_copy(page[:].indirect(offsets[:, cols.start // 16 : cols.stop // 16]), gated[:, cols])
+
+        whole = slice(0, S)
+        nc.vector.tensor_tensor(pages[0][:].indirect(list4[:]), h2[0][:], gates2[0][:], MULT)
+        scale1 = gather(kept("scale1", [P, S], U8), tab_plane[:], list1)
+
+        wa_bf = placed("wa_bf", [P, 2 * PACK * H], BF16, WA_ROUNDED)[:]
+        wa_places = wa_bf.rearrange("p (t w a b i) -> p w t a i b", t=PACK, w=2, b=RUN, i=PACK)
+
+        def round_a_weight(w, raw, first, sign):
+            src = raw[:].rearrange("p i (a t b) -> p t a i b", t=PACK, b=RUN)
+            for t in range(PACK):
+                nc.scalar.activation(wa_places[:, w, t, first : first + src.shape[2]], src[:, t], COPY, scale=sign)
+
+        round_a_weight(0, war_raw, 0, 1.0)
+        for i in range(2):
+            round_a_weight(1, wai_raw[i], i * QUADRANT // 2, -1.0)
+        wa_codes = kept("wa_codes", [P, 2 * H], U32)
+        wa_plane = kept("wa_plane", [P, 2 * H], U8)
+        nc.vector.quantize_mx(wa_codes[:].bitcast(FP8X4), wa_plane[:], wa_bf)
+        wb_plane_dealt = kept("wb_plane_dealt", [P, 2 * H], U8)
+        nc.vector.tensor_copy(
+            wb_plane_dealt[:].bitcast(I32).rearrange("p (t w a) -> p t w a", t=PACK, w=2),
+            wb_plane[:].bitcast(I32).rearrange("p (w a t) -> p t w a", t=PACK, w=2),
+        )
+        wb_dealt = kept("wb_dealt", [P, H], I32)
+        nc.vector.tensor_copy(
+            wb_dealt[:].rearrange("p (t w a b) -> p t w a b", t=PACK, w=2, b=RUN // 2),
+            wb[:].rearrange("p w (a t b) -> p t w a b", t=PACK, b=RUN // 2),
+        )
+        for t in range(1, PACK):
+            gated = placed("gated2_last", [P, S], F32, B_FACTORS + 12 * KIB) if t == LAST else h2[t]
+            gate_and_scatter(pages[t], list4, gated, h2[t], gates2[t], whole)
+
+        def factors(name, offset, weights, plane, step):
+            t, half = divmod(step, 2)
+            tile = placed("%s_%d" % (name, step), [P, 2, HALF], F32, offset + 4 * KIB * FACTOR_PLACES[step])
+            for pair in range(LINK_TILES // 2):
+                bank = take(sum_banks)
+                for lt in range(2):
+                    first = HALF * half + P * (2 * pair + lt)
+                    nc.tensor.matmul_mx(
+                        bank[:, 2 * P * lt : 2 * P * (lt + 1)],
+                        lhsT=words1[:, first : first + P].bitcast(FP8X4), lhsT_scale=scale1[:, first : first + P],
+                        rhs=weights, rhs_scale=plane[:, 2 * P * t : 2 * P * (t + 1)], start=True, stop=True,
+                    )
+                places = tile[:, :, 2 * P * pair : 2 * P * (pair + 1)].rearrange("p i (lt m) -> p lt i m", lt=2)
+                nc.scalar.copy(places, bank[:].rearrange("p (lt i m) -> p lt i m", lt=2, i=2))
+            return tile
+
+        def both_factors(step):
+            t = step // 2
+            a = factors("a", A_FACTORS, wa_codes[:, 2 * P * t : 2 * P * (t + 1)].bitcast(FP8X4), wa_plane, step)
+            b = factors("b", B_FACTORS, wb_dealt[:, P * t : P * (t + 1)].bitcast(FP4X4), wb_plane_dealt, step)
             return a, b
 
-        def multiply(t, offset, pieces):
-            a, b = factor_tiles[t]
-            products = placed("products%d" % t, [P, 2, S], F32, offset)
-            for cols in pieces:
-                nc.gpsimd.tensor_tensor(products[:, :, cols], a[:, :, cols], b[:, :, cols], MULT)
-            return products
+        h1 = [placed("h1_%d" % t, [P, S], F32, gate2_bytes(2) if t == 1 else STREAMS + 4 * KIB * t) for t in range(PACK)]
+        gated1 = [placed("gated1_0", [P, S], F32, a_bytes(1, 1)), placed("gated1_1", [P, S], F32, STREAMS + 4 * KIB), h1[2]]
 
-        def turn(t, products, offset):
-            h1 = placed("h1_%d" % t, [P, S], F32, offset)
-            for half in range(2):
-                bank = take(turn_banks)
-                for lt in range(LINK_TILES):
-                    for i in range(2):
-                        nc.tensor.matmul(
-                            bank[:, lt * P : (lt + 1) * P], lhsT=products[:, i, half * HALF + lt * P : half * HALF + (lt + 1) * P], rhs=ident[:],
-                            start=(i == 0), stop=(i == 1), is_transpose=True,
-                        )
-                nc.scalar.copy(h1[:, halves[half]], bank[:])
-            return h1
+        def multiply_and_turn(step):
+            t, half = divmod(step, 2)
+            a, b = factor_tiles[step]
+            products = a
+            if t == 0:
+                products = placed("products_first%d" % half, [P, 2, HALF], F32, gate2_bytes(2 + half))
+            if half == 0 and t > 0:
+                products = placed("products_next%d" % t, [P, 2, HALF], F32, (STREAMS + 12 * KIB, STREAMS, gate2_bytes(2))[t - 1])
+            if half == 1 and t > 0:
+                products = placed("products%d" % t, [P, 2, HALF], F32, gate1_bytes(t - 1))
+            nc.gpsimd.tensor_tensor(
+                products[:].rearrange("p i c -> p (i c)"), a[:].rearrange("p i c -> p (i c)"),
+                b[:].rearrange("p i c -> p (i c)"), MULT,
+            )
+            bank = take(turn_banks)
+            for lt in range(LINK_TILES):
+                for i in range(2):
+                    nc.tensor.matmul(
+                        bank[:, lt * P : (lt + 1) * P], lhsT=products[:, i, lt * P : (lt + 1) * P], rhs=ident[:],
+                        start=(i == 0), stop=(i == 1), is_transpose=True,
+                    )
+            nc.scalar.copy(h1[t][:, halves[half]], bank[:])
 
-        def gate_h1(t, offset):
-            gated = placed("gated1_%d" % t, [P, S], F32, offset)
-            gate_and_scatter(pages[t], list3, gated, h1[t], gates1[t], 1)
+        steps = 2 * PACK
+        factor_tiles = [both_factors(step) for step in range(2)]
+        for step in range(steps):
+            if step + 2 < steps:
+                factor_tiles.append(both_factors(step + 2))
+            multiply_and_turn(step)
+            if step % 2 == 0 and step > 0:
+                t = step // 2 - 1
+                gate_and_scatter(pages[t], list3, gated1[t], h1[t], gates1[t], whole)
 
-        factor_tiles = [factors(0), factors(1)]
-        whole = [slice(0, S)]
-        h1 = [turn(0, multiply(0, GATE_LAST, halves), H1_FIRST)]
-        h1.append(turn(1, multiply(1, b_bytes(0), whole), a_bytes(1)))
-        gate_h1(0, PRODUCTS1)
-        factor_tiles.extend([factors(2), factors(3)])
+        for t in (1, 2):
+            gains[t] = load_gain(t, placed("gain%d" % t, [P, 1], F32, a_bytes(t + 1, 1) + 3 * KIB))
 
-        h1.append(turn(2, multiply(2, H1_FIRST - 4 * KIB, whole), a_bytes(2)))
-        wo_bf = placed("wo_bf", [P, PACK * N], BF16, b_bytes(0))
-        round_weight(wo_bf[:].rearrange("p (t c) -> p t c", t=PACK), wo_raw, 1.0)
+        wo_bf = placed("wo_bf", [P, PACK * N], BF16, WORDS1)
+        dst = wo_bf[:].rearrange("p (t m i) -> p m t i", t=PACK, i=PACK)
+        src = wo_raw[:].rearrange("p i (m t) -> p m t i", t=PACK)
+        for half in range(2):
+            ms = slice(half * P // 2, (half + 1) * P // 2)
+            nc.scalar.copy(dst[:, ms], src[:, ms])
 
         chunk_cols = [slice(sum(CHUNKS[:c]), sum(CHUNKS[: c + 1])) for c in range(len(CHUNKS))]
-        z_all = placed("z", [P, T2 * PACK], BF16, Z)
-        z_flat = [z_all[:, PACK * cols.start : PACK * cols.stop] for cols in chunk_cols]
+        last_chunk = len(CHUNKS) - 1
+        z_first = placed("z_first", [P, PACK * BANK], BF16, STREAMS)
+        z_main = placed("z_main", [P, 2 * PACK * BANK], BF16, gate2_bytes(LAST))
+        z_last = placed("z_last", [P, PACK * CHUNKS[last_chunk]], BF16, A_FACTORS - 4 * KIB)
+        z_flat = [z_first[:, PACK * cols.start : PACK * cols.stop] for cols in chunk_cols[:2]]
+        z_flat.extend(z_main[:, PACK * (cols.start - BANK) : PACK * (cols.stop - BANK)] for cols in chunk_cols[2:last_chunk])
+        z_flat.append(z_last[:])
         z = [flat.rearrange("p (m t) -> p m t", t=PACK) for flat in z_flat]
-        on_scalar = range(len(CHUNKS) - SCALAR_LAST_PAGE_CHUNKS, len(CHUNKS))
 
         def round_page(t, c):
-            page, factor = pages[t][:, chunk_cols[c]], gains[:, t : t + 1]
-            if t == LAST and c not in on_scalar:
-                nc.vector.tensor_scalar(z[c][:, :, t], page, factor, None, MULT)
-            elif t == LAST - 1 and c not in on_scalar:
+            page, factor = pages[t][:, chunk_cols[c]], gains[t][:]
+            if c == last_chunk and t < 2:
+                nc.gpsimd.tensor_scalar(z[c][:, :, t], page, factor, 0.0, MULT, ADD)
+            elif c == last_chunk or t < 2:
+                nc.scalar.activation(z[c][:, :, t], page, COPY, scale=factor)
+            elif t == 2:
                 twice = page.unsqueeze(2).to_broadcast([P, CHUNKS[c], 2])
                 nc.scalar.activation(z[c][:, :, t : t + 2], twice, COPY, scale=factor)
             else:
-                nc.scalar.activation(z[c][:, :, t], page, COPY, scale=factor)
+                nc.vector.tensor_scalar(z[c][:, :, t], page, factor, None, MULT)
 
-        def round_whole_page(t):
+        for t in range(LAST):
             for c in range(len(CHUNKS)):
                 round_page(t, c)
-
-        gate_h1(1, b_bytes(2))
-        gate_h1(2, H2 + 8 * KIB)
-        products = multiply(LAST, a_bytes(2), whole)
-        h1_last = placed("h1_last", [P, S], F32, a_bytes(1))
-        nc.gpsimd.tensor_tensor(h1_last[:], products[:, 0, :], products[:, 1, :], ADD)
-        for t in range(LAST):
-            round_whole_page(t)
-        wo_codes = placed("wo_codes", [P, N], U32, H2 + 8 * KIB)
-        wo_plane = placed("wo_plane", [P, N], U8, H2 + 8 * KIB + 4 * N)
+        wo_codes = placed("wo_codes", [P, N], U32, a_bytes(LAST, 1))
+        wo_plane = placed("wo_plane", [P, N], U8, a_bytes(LAST, 1) + 4 * N)
         nc.vector.quantize_mx(wo_codes[:].bitcast(FP8X4), wo_plane[:], wo_bf[:])
-        nc.vector.tensor_tensor(pages[LAST][:].indirect(list3[:]), h1_last[:], gates1[LAST], MULT)
-        for c in on_scalar:
-            round_page(LAST, c)
+        nc.vector.tensor_tensor(pages[LAST][:].indirect(list3[:]), h1[LAST][:], gates1[LAST][:], MULT)
+        round_page(LAST, last_chunk)
 
-        z_codes = keep.tile([P, T2], U32, align_bytes=64)
-        z_plane = keep.tile([P, T2], U8, align_bytes=64)
-        y_codes = keep.tile([P, T2], U32, align_bytes=64)
-        y_plane = keep.tile([P, T2], U8, align_bytes=64)
+        z_codes = kept("z_codes", [P, T2], U32)
+        z_plane = kept("z_plane", [P, T2], U8)
+        y_codes = kept("y_codes", [P, T2], U32)
+        y_plane = kept("y_plane", [P, T2], U8)
         out_rows = out_0.rearrange("(p t) m -> p t m", t=PACK)
         out_words = out_1[0].rearrange("p m t -> p (m t)").bitcast(I32)
 
         def last_product(c):
             w, cols = CHUNKS[c], chunk_cols[c]
-            if c not in on_scalar:
+            if c != last_chunk:
                 round_page(LAST, c)
             nc.vector.quantize_mx(z_codes[:, cols].bitcast(FP8X4), z_plane[:, cols], z_flat[c])
-            y = placed("y%d" % c, [P, PACK, w], F32, a_bytes(2) + 4 * PACK * cols.start)
+            place = 4 * PACK * cols.start
+            y = placed("y%d" % c, [P, PACK, w], F32, place if cols.start < T2 // 2 else A_FACTORS + place - 16 * KIB)
             per_bank = BANK // w
             for first in range(0, PACK, per_bank):
                 bank = take(banks)[:].rearrange("p (i m) -> p i m", m=w)
                 for i in range(per_bank):
+                    rows = slice((first + i) * P, (first + i + 1) * P)
                     nc.tensor.matmul_mx(
-                        bank[:, i, :], lhsT=wo_codes[:, rows(first + i)].bitcast(FP8X4), lhsT_scale=wo_plane[:, rows(first + i)],
+                        bank[:, i, :], lhsT=wo_codes[:, rows].bitcast(FP8X4), lhsT_scale=wo_plane[:, rows],
                         rhs=z_codes[:, cols].bitcast(FP8X4), rhs_scale=z_plane[:, cols], start=True, stop=True,
                     )
                 nc.scalar.copy(y[:, first : first + per_bank, :], bank)
                 done = first + per_bank
-                if done % STORE_ROWS[c] == 0:
-                    stored = slice(done - STORE_ROWS[c], done)
+                if done % STORE_ROWS == 0:
+                    stored = slice(done - STORE_ROWS, done)
                     nc.sync.dma_start(out_rows[:, stored, cols], y[:, stored, :])
             return y
 
         def store_codes(c, y, first, w, on_scalar):
             cols = slice(chunk_cols[c].start + first, chunk_cols[c].start + first + w)
-            grouped = placed("y_bf%d_%d" % (c, first), [P, w, PACK], BF16, a_bytes(0) + 2 * PACK * cols.start)
+            grouped = placed("y_bf%d_%d" % (c, first), [P, w, PACK], BF16, STREAMS + 2 * PACK * cols.start)
             dst = grouped[:].rearrange("p (c i) t -> p c t i", i=PACK)
             src = y[:, :, first : first + w].rearrange("p t (c i) -> p c t i", i=PACK)
             if on_scalar:
@@ -367,15 +366,15 @@ def tile_list_woven_link_features_kernel(
             else:
                 nc.vector.tensor_copy(dst, src)
             nc.vector.quantize_mx(y_codes[:, cols].bitcast(FP8X4), y_plane[:, cols], grouped[:].rearrange("p m t -> p (m t)"))
-            if cols.stop in CODE_STORES:
-                stored = slice(CODE_STORES[CODE_STORES.index(cols.stop) - 1], cols.stop)
+            if cols.stop % CODE_STORE == 0:
+                stored = slice(cols.stop - CODE_STORE, cols.stop)
                 nc.sync.dma_start(out_words[:, stored], y_codes[:, stored].bitcast(I32))
 
         ys = [last_product(c) for c in range(len(CHUNKS))]
-        for c, y in enumerate(ys[:-1]):
+        for c, y in enumerate(ys[:last_chunk]):
             store_codes(c, y, 0, CHUNKS[c], False)
-        half = CHUNKS[-1] // 2
-        store_codes(len(CHUNKS) - 1, ys[-1], 0, half, False)
-        store_codes(len(CHUNKS) - 1, ys[-1], half, half, True)
+        half_chunk = CHUNKS[last_chunk] // 2
+        store_codes(last_chunk, ys[last_chunk], 0, half_chunk, False)
+        store_codes(last_chunk, ys[last_chunk], half_chunk, half_chunk, True)
         for q in range(QUADRANTS):
             (nc.scalar, nc.sync)[q % 2].dma_start(scale_rows(out_2, q), plane_rows(y_plane, q))

@@ -232,25 +232,35 @@ def tile_list_woven_link_features_kernel(
             tile = placed("%s_%d" % (name, step), [P, 2, HALF], F32, offset + 4 * KIB * FACTOR_PLACES[step])
             for pair in range(LINK_TILES // 2):
                 bank = take(sum_banks)
+                if t == LAST:
+                    nc.tensor.matmul_mx(
+                        bank[:], lhsT=weights(2 * t + pair, 1), lhsT_scale=plane[:, P * (2 * t + pair) : P * (2 * t + pair + 1)],
+                        rhs=words1[:, halves[half]].bitcast(FP8X4), rhs_scale=scale1[:, halves[half]], start=True, stop=True,
+                    )
+                    nc.scalar.copy(tile[:, pair, :], bank[:])
+                    continue
                 for lt in range(2):
                     first = HALF * half + P * (2 * pair + lt)
                     nc.tensor.matmul_mx(
                         bank[:, 2 * P * lt : 2 * P * (lt + 1)],
                         lhsT=words1[:, first : first + P].bitcast(FP8X4), lhsT_scale=scale1[:, first : first + P],
-                        rhs=weights, rhs_scale=plane[:, 2 * P * t : 2 * P * (t + 1)], start=True, stop=True,
+                        rhs=weights(2 * t, 2), rhs_scale=plane[:, 2 * P * t : 2 * P * (t + 1)], start=True, stop=True,
                     )
                 places = tile[:, :, 2 * P * pair : 2 * P * (pair + 1)].rearrange("p i (lt m) -> p lt i m", lt=2)
                 nc.scalar.copy(places, bank[:].rearrange("p (lt i m) -> p lt i m", lt=2, i=2))
             return tile
 
-        def both_factors(step):
-            t = step // 2
-            a = factors("a", A_FACTORS, wa_codes[:, 2 * P * t : 2 * P * (t + 1)].bitcast(FP8X4), wa_plane, step)
-            b = factors("b", B_FACTORS, wb_dealt[:, P * t : P * (t + 1)].bitcast(FP4X4), wb_plane_dealt, step)
-            return a, b
+        def a_weights(first, count):
+            return wa_codes[:, P * first : P * (first + count)].bitcast(FP8X4)
 
-        h1 = [placed("h1_%d" % t, [P, S], F32, gate2_bytes(2) if t == 1 else STREAMS + 4 * KIB * t) for t in range(PACK)]
-        gated1 = [placed("gated1_0", [P, S], F32, a_bytes(1, 1)), placed("gated1_1", [P, S], F32, STREAMS + 4 * KIB), h1[2]]
+        def b_weights(first, count):
+            return wb_dealt[:, P // 2 * first : P // 2 * (first + count)].bitcast(FP4X4)
+
+        def both_factors(step):
+            return factors("a", A_FACTORS, a_weights, wa_plane, step), factors("b", B_FACTORS, b_weights, wb_plane_dealt, step)
+
+        h1 = [placed("h1_%d" % t, [P, S], F32, (STREAMS, gate2_bytes(2), STREAMS + 8 * KIB, STREAMS + 8 * KIB)[t]) for t in range(PACK)]
+        gated1 = [placed("gated1_%d" % t, [P, S], F32, (a_bytes(1, 1), STREAMS + 4 * KIB, a_bytes(2, 0))[t]) for t in range(LAST)]
 
         def multiply_and_turn(step):
             t, half = divmod(step, 2)
@@ -266,6 +276,8 @@ def tile_list_woven_link_features_kernel(
                 products[:].rearrange("p i c -> p (i c)"), a[:].rearrange("p i c -> p (i c)"),
                 b[:].rearrange("p i c -> p (i c)"), MULT,
             )
+            if t == LAST:
+                return products
             bank = take(turn_banks)
             for lt in range(LINK_TILES):
                 for i in range(2):
@@ -276,17 +288,21 @@ def tile_list_woven_link_features_kernel(
             nc.scalar.copy(h1[t][:, halves[half]], bank[:])
 
         steps = 2 * PACK
+        unturned = []
         factor_tiles = [both_factors(step) for step in range(2)]
         for step in range(steps):
             if step + 2 < steps:
                 factor_tiles.append(both_factors(step + 2))
-            multiply_and_turn(step)
+            unturned.append(multiply_and_turn(step))
             if step % 2 == 0 and step > 0:
                 t = step // 2 - 1
                 gate_and_scatter(pages[t], list3, gated1[t], h1[t], gates1[t], whole)
 
+        for half in range(2):
+            products = unturned[2 * LAST + half]
+            nc.gpsimd.tensor_tensor(h1[LAST][:, halves[half]], products[:, 0, :], products[:, 1, :], ADD)
         for t in (1, 2):
-            gains[t] = load_gain(t, placed("gain%d" % t, [P, 1], F32, a_bytes(t + 1, 1) + 3 * KIB))
+            gains[t] = load_gain(t, placed("gain%d" % t, [P, 1], F32, a_bytes(2, 1) + 64 * t))
 
         wo_bf = placed("wo_bf", [P, PACK * N], BF16, WORDS1)
         dst = wo_bf[:].rearrange("p (t m i) -> p m t i", t=PACK, i=PACK)
@@ -298,18 +314,14 @@ def tile_list_woven_link_features_kernel(
         chunk_cols = [slice(sum(CHUNKS[:c]), sum(CHUNKS[: c + 1])) for c in range(len(CHUNKS))]
         last_chunk = len(CHUNKS) - 1
         z_first = placed("z_first", [P, PACK * BANK], BF16, STREAMS)
-        z_main = placed("z_main", [P, 2 * PACK * BANK], BF16, gate2_bytes(LAST))
-        z_last = placed("z_last", [P, PACK * CHUNKS[last_chunk]], BF16, A_FACTORS - 4 * KIB)
+        z_main = placed("z_main", [P, 3 * PACK * BANK], BF16, gate2_bytes(LAST))
         z_flat = [z_first[:, PACK * cols.start : PACK * cols.stop] for cols in chunk_cols[:2]]
-        z_flat.extend(z_main[:, PACK * (cols.start - BANK) : PACK * (cols.stop - BANK)] for cols in chunk_cols[2:last_chunk])
-        z_flat.append(z_last[:])
+        z_flat.extend(z_main[:, PACK * (cols.start - BANK) : PACK * (cols.stop - BANK)] for cols in chunk_cols[2:])
         z = [flat.rearrange("p (m t) -> p m t", t=PACK) for flat in z_flat]
 
         def round_page(t, c):
             page, factor = pages[t][:, chunk_cols[c]], gains[t][:]
-            if c == last_chunk and t < 2:
-                nc.gpsimd.tensor_scalar(z[c][:, :, t], page, factor, 0.0, MULT, ADD)
-            elif c == last_chunk or t < 2:
+            if c == last_chunk or t < 2:
                 nc.scalar.activation(z[c][:, :, t], page, COPY, scale=factor)
             elif t == 2:
                 twice = page.unsqueeze(2).to_broadcast([P, CHUNKS[c], 2])

@@ -21,7 +21,7 @@ ADD = mybir.AluOpType.add
 P = 128
 PACK = 4
 LAST = PACK - 1
-RUN = 4
+RUN = 2
 QUADRANTS = 4
 QUADRANT = P // QUADRANTS
 QUADRANT_ORDER = (0, 2, 1, 3)
@@ -173,8 +173,8 @@ def tile_list_woven_link_features_kernel(
         )
         wsp_plane_dealt = kept("wsp_plane_dealt", [P, H], U8)
         nc.vector.tensor_copy(
-            wsp_plane_dealt[:].bitcast(I32).rearrange("p (t a) -> p t a", t=PACK),
-            wsp_plane[:].bitcast(I32).rearrange("p (a t) -> p t a", t=PACK),
+            wsp_plane_dealt[:].bitcast(U16).rearrange("p (t a) -> p t a", t=PACK),
+            wsp_plane[:].bitcast(U16).rearrange("p (a t) -> p t a", t=PACK),
         )
         words1 = gather(placed("words1", [P, S], U32, WORDS1), tab1[:].bitcast(U32), list1)
 
@@ -209,19 +209,19 @@ def tile_list_woven_link_features_kernel(
 
         round_a_weight(0, war_raw, 0, 1.0)
         for i in range(2):
-            round_a_weight(1, wai_raw[i], i * QUADRANT // 2, -1.0)
+            round_a_weight(1, wai_raw[i], i * P // RUN // 2, -1.0)
         wa_codes = kept("wa_codes", [P, 2 * H], U32)
         wa_plane = kept("wa_plane", [P, 2 * H], U8)
         nc.vector.quantize_mx(wa_codes[:].bitcast(FP8X4), wa_plane[:], wa_bf)
         wb_plane_dealt = kept("wb_plane_dealt", [P, 2 * H], U8)
         nc.vector.tensor_copy(
-            wb_plane_dealt[:].bitcast(I32).rearrange("p (t w a) -> p t w a", t=PACK, w=2),
-            wb_plane[:].bitcast(I32).rearrange("p (w a t) -> p t w a", t=PACK, w=2),
+            wb_plane_dealt[:].bitcast(U16).rearrange("p (t w a) -> p t w a", t=PACK, w=2),
+            wb_plane[:].bitcast(U16).rearrange("p (w a t) -> p t w a", t=PACK, w=2),
         )
         wb_dealt = kept("wb_dealt", [P, H], I32)
         nc.vector.tensor_copy(
-            wb_dealt[:].rearrange("p (t w a b) -> p t w a b", t=PACK, w=2, b=RUN // 2),
-            wb[:].rearrange("p w (a t b) -> p t w a b", t=PACK, b=RUN // 2),
+            wb_dealt[:].rearrange("p (t w a) -> p t w a", t=PACK, w=2),
+            wb[:].rearrange("p w (a t) -> p t w a", t=PACK),
         )
         for t in range(1, PACK):
             gated = placed("gated2_last", [P, S], F32, B_FACTORS + 12 * KIB) if t == LAST else h2[t]

@@ -91,9 +91,9 @@ def tile_list_woven_link_features_kernel(
         def scale_rows(scales, q):
             return scales[0, SCALE_ROWS * q : SCALE_ROWS * (q + 1), :].bitcast(I32)
 
-        def load_plane(plane, scales):
+        def load_plane(plane, scales, queue=nc.sync):
             for q in QUADRANT_ORDER:
-                nc.sync.dma_start(plane_rows(plane, q), scale_rows(scales, q))
+                queue.dma_start(plane_rows(plane, q), scale_rows(scales, q))
 
         def load_e4m3_words(tile, words):
             nc.sync.dma_start(tile[:], words[0].rearrange("p c i -> p (c i)").bitcast(I32))
@@ -118,24 +118,24 @@ def tile_list_woven_link_features_kernel(
         tab2_plane = zeroed_plane(kept("tab2_plane", [P, T], U8), nc.gpsimd)
         wsp_plane = zeroed_plane(kept("wsp_plane", [P, H], U8), nc.vector)
         tab_plane = zeroed_plane(kept("tab_plane", [P, T], U8), nc.vector)
-        wb_plane = zeroed_plane(placed("wb_plane", [P, 2 * H], U8, page_bytes(1) + 2 * KIB), nc.vector)
+        wb_plane = zeroed_plane(kept("wb_plane", [P, 2 * H], U8), nc.vector)
 
         list2 = load_list("list2", offs2)
-        list1 = load_list("list1", offs)
-        list4 = load_list("list4", offs4)
-        load_plane(tab2_plane, tab2_scales)
         tab2 = load_e4m3_words(placed("tab2", [P, T], I32, page_bytes(0)), tab2_words)
+        load_plane(tab2_plane, tab2_scales, nc.scalar)
         wsp = load_e4m3_words(kept("wsp", [P, H], I32), wsp_words)
-        load_plane(wsp_plane, wsp_scales)
         tab1 = load_e4m3_words(kept("tab1", [P, T], I32), tab_words)
+        load_plane(wsp_plane, wsp_scales)
+        list1 = load_list("list1", offs)
         gates2 = [load_gate("gate2_0", wg2, 0, gate2_bytes(0))]
+        list4 = load_list("list4", offs4)
         load_plane(tab_plane, tab_scales)
         war_raw = load_weight("war_raw", war, page_bytes(LAST), 0, H)
+        load_plane(wb_plane[:, :H], wbr_scales)
         gates2.append(load_gate("gate2_1", wg2, 1, gate2_bytes(1)))
-        wai_raw = [load_weight("wai_raw%d" % i, wai, page_bytes(2) + 4 * KIB * i, i * H // 2, H // 2) for i in range(2)]
-        for i, scales in enumerate((wbr_scales, wbi_scales)):
-            load_plane(wb_plane[:, i * H : (i + 1) * H], scales)
-        wb = placed("wb", [P, 2, H // 2], I32, page_bytes(1))
+        load_plane(wb_plane[:, H:], wbi_scales)
+        wai_raw = [load_weight("wai_raw%d" % i, wai, page_bytes(2 - i), i * H // 2, H // 2) for i in range(2)]
+        wb = kept("wb", [P, 2, H // 2], I32)
         for i, words in enumerate((wbr_words, wbi_words)):
             nc.sync.dma_start(wb[:, i, :], words[0].bitcast(I32))
         gates2.extend(load_gate("gate2_%d" % t, wg2, t, gate2_bytes(t)) for t in range(2, PACK))
@@ -210,9 +210,6 @@ def tile_list_woven_link_features_kernel(
         round_a_weight(0, war_raw, 0, 1.0)
         for i in range(2):
             round_a_weight(1, wai_raw[i], i * P // RUN // 2, -1.0)
-        wa_codes = kept("wa_codes", [P, 2 * H], U32)
-        wa_plane = kept("wa_plane", [P, 2 * H], U8)
-        nc.vector.quantize_mx(wa_codes[:].bitcast(FP8X4), wa_plane[:], wa_bf)
         wb_plane_dealt = kept("wb_plane_dealt", [P, 2 * H], U8)
         nc.vector.tensor_copy(
             wb_plane_dealt[:].bitcast(U16).rearrange("p (t w a) -> p t w a", t=PACK, w=2),
@@ -223,6 +220,9 @@ def tile_list_woven_link_features_kernel(
             wb_dealt[:].rearrange("p (t w a) -> p t w a", t=PACK, w=2),
             wb[:].rearrange("p w (a t) -> p t w a", t=PACK),
         )
+        wa_codes = kept("wa_codes", [P, 2 * H], U32)
+        wa_plane = kept("wa_plane", [P, 2 * H], U8)
+        nc.vector.quantize_mx(wa_codes[:].bitcast(FP8X4), wa_plane[:], wa_bf)
         for t in range(1, PACK):
             gated = placed("gated2_last", [P, S], F32, B_FACTORS + 12 * KIB) if t == LAST else h2[t]
             gate_and_scatter(pages[t], list4, gated, h2[t], gates2[t], whole)

@@ -30,13 +30,17 @@ BANK = 512
 LIST_COLS = S // 16
 HALF = S // 2
 LINK_TILES = HALF // P
+WAI_PIECES = ((0, 384), (384, 128))
 CHUNKS = (256, 256, 512, 512, 512)
+VECTOR_LAST_PAGE = 1536
+CODE_PIECES = ((0, 512, False), (512, 512, False), (1024, 512, False), (1536, 256, False), (1792, 256, True))
 STORE_ROWS = 2
 CODE_STORE = 512
 KIB = 1024
 B_FACTORS = 0
 A_FACTORS = 32 * KIB
 FACTOR_PLACES = (0, 1, 2, 0, 1, 5, 6, 7)
+RESULT_PLACES = (0, 8 * KIB, 32 * KIB, 40 * KIB)
 STREAMS = 64 * KIB
 PAGES = 80 * KIB
 GATES2 = 112 * KIB
@@ -91,9 +95,9 @@ def tile_list_woven_link_features_kernel(
         def scale_rows(scales, q):
             return scales[0, SCALE_ROWS * q : SCALE_ROWS * (q + 1), :].bitcast(I32)
 
-        def load_plane(plane, scales, queue=nc.sync):
+        def load_plane(plane, scales):
             for q in QUADRANT_ORDER:
-                queue.dma_start(plane_rows(plane, q), scale_rows(scales, q))
+                nc.sync.dma_start(plane_rows(plane, q), scale_rows(scales, q))
 
         def load_e4m3_words(tile, words):
             nc.sync.dma_start(tile[:], words[0].rearrange("p c i -> p (c i)").bitcast(I32))
@@ -120,10 +124,10 @@ def tile_list_woven_link_features_kernel(
         tab_plane = zeroed_plane(kept("tab_plane", [P, T], U8), nc.vector)
         wb_plane = zeroed_plane(kept("wb_plane", [P, 2 * H], U8), nc.vector)
 
-        list2 = load_list("list2", offs2)
-        tab2 = load_e4m3_words(placed("tab2", [P, T], I32, page_bytes(0)), tab2_words)
-        load_plane(tab2_plane, tab2_scales, nc.scalar)
         wsp = load_e4m3_words(kept("wsp", [P, H], I32), wsp_words)
+        list2 = load_list("list2", offs2)
+        load_plane(tab2_plane, tab2_scales)
+        tab2 = load_e4m3_words(placed("tab2", [P, T], I32, page_bytes(0)), tab2_words)
         tab1 = load_e4m3_words(kept("tab1", [P, T], I32), tab_words)
         load_plane(wsp_plane, wsp_scales)
         list1 = load_list("list1", offs)
@@ -134,7 +138,7 @@ def tile_list_woven_link_features_kernel(
         load_plane(wb_plane[:, :H], wbr_scales)
         gates2.append(load_gate("gate2_1", wg2, 1, gate2_bytes(1)))
         load_plane(wb_plane[:, H:], wbi_scales)
-        wai_raw = [load_weight("wai_raw%d" % i, wai, page_bytes(2 - i), i * H // 2, H // 2) for i in range(2)]
+        wai_raw = [load_weight("wai_raw%d" % i, wai, page_bytes(2 - i), *WAI_PIECES[i]) for i in range(2)]
         wb = kept("wb", [P, 2, H // 2], I32)
         for i, words in enumerate((wbr_words, wbi_words)):
             nc.sync.dma_start(wb[:, i, :], words[0].bitcast(I32))
@@ -164,13 +168,13 @@ def tile_list_woven_link_features_kernel(
 
         halves = [slice(half * HALF, (half + 1) * HALF) for half in range(2)]
 
-        scale2 = gather(kept("scale2", [P, S], U8), tab2_plane[:], list2)
-        words2 = gather(kept("words2", [P, S], U32), tab2[:].bitcast(U32), list2)
         wsp_dealt = kept("wsp_dealt", [P, H], I32)
         nc.vector.tensor_copy(
             wsp_dealt[:].rearrange("p (t a b) -> p t a b", t=PACK, b=RUN),
             wsp[:].rearrange("p (a t b) -> p t a b", t=PACK, b=RUN),
         )
+        scale2 = gather(kept("scale2", [P, S], U8), tab2_plane[:], list2)
+        words2 = gather(kept("words2", [P, S], U32), tab2[:].bitcast(U32), list2)
         wsp_plane_dealt = kept("wsp_plane_dealt", [P, H], U8)
         nc.vector.tensor_copy(
             wsp_plane_dealt[:].bitcast(U16).rearrange("p (t a) -> p t a", t=PACK),
@@ -209,7 +213,7 @@ def tile_list_woven_link_features_kernel(
 
         round_a_weight(0, war_raw, 0, 1.0)
         for i in range(2):
-            round_a_weight(1, wai_raw[i], i * P // RUN // 2, -1.0)
+            round_a_weight(1, wai_raw[i], WAI_PIECES[i][0] // (PACK * RUN), -1.0)
         wb_plane_dealt = kept("wb_plane_dealt", [P, 2 * H], U8)
         nc.vector.tensor_copy(
             wb_plane_dealt[:].bitcast(U16).rearrange("p (t w a) -> p t w a", t=PACK, w=2),
@@ -312,31 +316,33 @@ def tile_list_woven_link_features_kernel(
             nc.scalar.copy(dst[:, ms], src[:, ms])
 
         chunk_cols = [slice(sum(CHUNKS[:c]), sum(CHUNKS[: c + 1])) for c in range(len(CHUNKS))]
-        last_chunk = len(CHUNKS) - 1
         z_first = placed("z_first", [P, PACK * BANK], BF16, STREAMS)
         z_main = placed("z_main", [P, 3 * PACK * BANK], BF16, gate2_bytes(LAST))
-        z_flat = [z_first[:, PACK * cols.start : PACK * cols.stop] for cols in chunk_cols[:2]]
-        z_flat.extend(z_main[:, PACK * (cols.start - BANK) : PACK * (cols.stop - BANK)] for cols in chunk_cols[2:])
-        z = [flat.rearrange("p (m t) -> p m t", t=PACK) for flat in z_flat]
 
-        def round_page(t, c):
-            page, factor = pages[t][:, chunk_cols[c]], gains[t][:]
-            if c == last_chunk or t < 2:
-                nc.scalar.activation(z[c][:, :, t], page, COPY, scale=factor)
+        def z_cols(cols):
+            if cols.stop <= BANK:
+                return z_first[:, PACK * cols.start : PACK * cols.stop]
+            return z_main[:, PACK * (cols.start - BANK) : PACK * (cols.stop - BANK)]
+
+        def round_page(t, cols):
+            page, factor = pages[t][:, cols], gains[t][:]
+            z = z_cols(cols).rearrange("p (m t) -> p m t", t=PACK)
+            if cols.start >= VECTOR_LAST_PAGE or t < 2:
+                nc.scalar.activation(z[:, :, t], page, COPY, scale=factor)
             elif t == 2:
-                twice = page.unsqueeze(2).to_broadcast([P, CHUNKS[c], 2])
-                nc.scalar.activation(z[c][:, :, t : t + 2], twice, COPY, scale=factor)
+                twice = page.unsqueeze(2).to_broadcast([P, cols.stop - cols.start, 2])
+                nc.scalar.activation(z[:, :, t : t + 2], twice, COPY, scale=factor)
             else:
-                nc.vector.tensor_scalar(z[c][:, :, t], page, factor, None, MULT)
+                nc.vector.tensor_scalar(z[:, :, t], page, factor, None, MULT)
 
         for t in range(LAST):
-            for c in range(len(CHUNKS)):
-                round_page(t, c)
+            for cols in (slice(0, BANK), slice(BANK, VECTOR_LAST_PAGE), slice(VECTOR_LAST_PAGE, T2)):
+                round_page(t, cols)
         wo_codes = placed("wo_codes", [P, N], U32, a_bytes(LAST, 1))
         wo_plane = placed("wo_plane", [P, N], U8, a_bytes(LAST, 1) + 4 * N)
         nc.vector.quantize_mx(wo_codes[:].bitcast(FP8X4), wo_plane[:], wo_bf[:])
         nc.vector.tensor_tensor(pages[LAST][:].indirect(list3[:]), h1[LAST][:], gates1[LAST][:], MULT)
-        round_page(LAST, last_chunk)
+        round_page(LAST, slice(VECTOR_LAST_PAGE, T2))
 
         z_codes = kept("z_codes", [P, T2], U32)
         z_plane = kept("z_plane", [P, T2], U8)
@@ -345,13 +351,14 @@ def tile_list_woven_link_features_kernel(
         out_rows = out_0.rearrange("(p t) m -> p t m", t=PACK)
         out_words = out_1[0].rearrange("p m t -> p (m t)").bitcast(I32)
 
+        ys = [placed("y%d" % g, [P, PACK, BANK], F32, RESULT_PLACES[g]) for g in range(T2 // BANK)]
+
         def last_product(c):
             w, cols = CHUNKS[c], chunk_cols[c]
-            if c != last_chunk:
-                round_page(LAST, c)
-            nc.vector.quantize_mx(z_codes[:, cols].bitcast(FP8X4), z_plane[:, cols], z_flat[c])
-            place = 4 * PACK * cols.start
-            y = placed("y%d" % c, [P, PACK, w], F32, place if cols.start < T2 // 2 else A_FACTORS + place - 16 * KIB)
+            if cols.start < VECTOR_LAST_PAGE:
+                round_page(LAST, slice(cols.start, min(cols.stop, VECTOR_LAST_PAGE)))
+            nc.vector.quantize_mx(z_codes[:, cols].bitcast(FP8X4), z_plane[:, cols], z_cols(cols))
+            y = ys[cols.start // BANK][:, :, cols.start % BANK : cols.start % BANK + w]
             per_bank = BANK // w
             for first in range(0, PACK, per_bank):
                 bank = take(banks)[:].rearrange("p (i m) -> p i m", m=w)
@@ -366,13 +373,12 @@ def tile_list_woven_link_features_kernel(
                 if done % STORE_ROWS == 0:
                     stored = slice(done - STORE_ROWS, done)
                     nc.sync.dma_start(out_rows[:, stored, cols], y[:, stored, :])
-            return y
 
-        def store_codes(c, y, first, w, on_scalar):
-            cols = slice(chunk_cols[c].start + first, chunk_cols[c].start + first + w)
-            grouped = placed("y_bf%d_%d" % (c, first), [P, w, PACK], BF16, STREAMS + 2 * PACK * cols.start)
+        def store_codes(first, w, on_scalar):
+            cols = slice(first, first + w)
+            grouped = placed("y_bf%d" % first, [P, w, PACK], BF16, STREAMS + 2 * PACK * first)
             dst = grouped[:].rearrange("p (c i) t -> p c t i", i=PACK)
-            src = y[:, :, first : first + w].rearrange("p t (c i) -> p c t i", i=PACK)
+            src = ys[first // BANK][:, :, first % BANK : first % BANK + w].rearrange("p t (c i) -> p c t i", i=PACK)
             if on_scalar:
                 nc.scalar.copy(dst, src)
             else:
@@ -382,11 +388,9 @@ def tile_list_woven_link_features_kernel(
                 stored = slice(cols.stop - CODE_STORE, cols.stop)
                 nc.sync.dma_start(out_words[:, stored], y_codes[:, stored].bitcast(I32))
 
-        ys = [last_product(c) for c in range(len(CHUNKS))]
-        for c, y in enumerate(ys[:last_chunk]):
-            store_codes(c, y, 0, CHUNKS[c], False)
-        half_chunk = CHUNKS[last_chunk] // 2
-        store_codes(last_chunk, ys[last_chunk], 0, half_chunk, False)
-        store_codes(last_chunk, ys[last_chunk], half_chunk, half_chunk, True)
+        for c in range(len(CHUNKS)):
+            last_product(c)
+        for piece in CODE_PIECES:
+            store_codes(*piece)
         for q in range(QUADRANTS):
             (nc.scalar, nc.sync)[q % 2].dma_start(scale_rows(out_2, q), plane_rows(y_plane, q))

@@ -34,7 +34,7 @@ WAI_PIECES = ((0, 384), (384, 128))
 CHUNKS = (256, 256, 512, 512, 512)
 VECTOR_LAST_PAGE = 1536
 CODE_PIECES = ((0, 512, False), (512, 512, False), (1024, 512, False), (1536, 256, False), (1792, 256, True))
-STORE_ROWS = 2
+STORE_ROWS = (2, 2, 1, 2, 2)
 CODE_STORE = 512
 KIB = 1024
 B_FACTORS = 0
@@ -120,9 +120,9 @@ def tile_list_woven_link_features_kernel(
             return raw
 
         tab2_plane = zeroed_plane(kept("tab2_plane", [P, T], U8), nc.gpsimd)
-        wsp_plane = zeroed_plane(kept("wsp_plane", [P, H], U8), nc.vector)
-        tab_plane = zeroed_plane(kept("tab_plane", [P, T], U8), nc.vector)
-        wb_plane = zeroed_plane(kept("wb_plane", [P, 2 * H], U8), nc.vector)
+        wsp_plane = zeroed_plane(kept("wsp_plane", [P, H], U8), nc.gpsimd)
+        tab_plane = zeroed_plane(kept("tab_plane", [P, T], U8), nc.gpsimd)
+        wb_plane = zeroed_plane(kept("wb_plane", [P, 2 * H], U8), nc.gpsimd)
 
         wsp = load_e4m3_words(kept("wsp", [P, H], I32), wsp_words)
         list2 = load_list("list2", offs2)
@@ -370,9 +370,10 @@ def tile_list_woven_link_features_kernel(
                     )
                 nc.scalar.copy(y[:, first : first + per_bank, :], bank)
                 done = first + per_bank
-                if done % STORE_ROWS == 0:
-                    stored = slice(done - STORE_ROWS, done)
-                    nc.sync.dma_start(out_rows[:, stored, cols], y[:, stored, :])
+                if done % STORE_ROWS[c] == 0:
+                    stored = slice(done - STORE_ROWS[c], done)
+                    queue = nc.scalar if cols.start >= T2 // 2 else nc.sync
+                    queue.dma_start(out_rows[:, stored, cols], y[:, stored, :])
 
         def store_codes(first, w, on_scalar):
             cols = slice(first, first + w)

@@ -32,15 +32,18 @@ HALF = S // 2
 LINK_TILES = HALF // P
 WAI_PIECES = ((0, 384), (384, 128))
 CHUNKS = (256, 256, 512, 512, 512)
-VECTOR_LAST_PAGE = 1536
-CODE_PIECES = ((0, 512, False), (512, 512, False), (1024, 512, False), (1536, 256, False), (1792, 256, True))
-STORE_ROWS = (2, 2, 1, 2, 2)
-CODE_STORE = 512
+Z_FIRST = 768
+SCALAR_LAST_PAGE = slice(1664, 2048)
+Z_PIECES = (((0, 256),), ((256, 512),), ((512, 768), (768, 1024)), ((1024, 1536),), ((1536, 2048),))
+PAGE_PIECES = ((0, 768, 2048), (0, 768, 2048), (0, 512, 768, 1024, 1664, 2048))
+BANK_ROWS = (1, 2, 1, 1, 1)
+STORE_ROWS = (1, 2, 1, 2, 2)
+VECTOR_LAST_RESULT = 256
+CODE_STORES = (512, 1536, 2048)
 KIB = 1024
 B_FACTORS = 0
 A_FACTORS = 32 * KIB
 FACTOR_PLACES = (0, 1, 2, 0, 1, 5, 6, 7)
-RESULT_PLACES = (0, 8 * KIB, 32 * KIB, 40 * KIB)
 STREAMS = 64 * KIB
 PAGES = 80 * KIB
 GATES2 = 112 * KIB
@@ -264,7 +267,7 @@ def tile_list_woven_link_features_kernel(
             return factors("a", A_FACTORS, a_weights, wa_plane, step), factors("b", B_FACTORS, b_weights, wb_plane_dealt, step)
 
         h1 = [placed("h1_%d" % t, [P, S], F32, (STREAMS, gate2_bytes(2), STREAMS + 8 * KIB, STREAMS + 8 * KIB)[t]) for t in range(PACK)]
-        gated1 = [placed("gated1_%d" % t, [P, S], F32, (a_bytes(1, 1), STREAMS + 4 * KIB, a_bytes(2, 0))[t]) for t in range(LAST)]
+        gated1 = [placed("gated1_%d" % t, [P, S], F32, (a_bytes(1, 1), a_bytes(1, 0), a_bytes(2, 0))[t]) for t in range(LAST)]
 
         def multiply_and_turn(step):
             t, half = divmod(step, 2)
@@ -316,18 +319,18 @@ def tile_list_woven_link_features_kernel(
             nc.scalar.copy(dst[:, ms], src[:, ms])
 
         chunk_cols = [slice(sum(CHUNKS[:c]), sum(CHUNKS[: c + 1])) for c in range(len(CHUNKS))]
-        z_first = placed("z_first", [P, PACK * BANK], BF16, STREAMS)
-        z_main = placed("z_main", [P, 3 * PACK * BANK], BF16, gate2_bytes(LAST))
+        z_first = placed("z_first", [P, PACK * Z_FIRST], BF16, STREAMS)
+        z_main = placed("z_main", [P, PACK * (T2 - Z_FIRST)], BF16, gate1_bytes(2) - 2 * PACK * (T2 - Z_FIRST))
 
         def z_cols(cols):
-            if cols.stop <= BANK:
+            if cols.stop <= Z_FIRST:
                 return z_first[:, PACK * cols.start : PACK * cols.stop]
-            return z_main[:, PACK * (cols.start - BANK) : PACK * (cols.stop - BANK)]
+            return z_main[:, PACK * (cols.start - Z_FIRST) : PACK * (cols.stop - Z_FIRST)]
 
         def round_page(t, cols):
             page, factor = pages[t][:, cols], gains[t][:]
             z = z_cols(cols).rearrange("p (m t) -> p m t", t=PACK)
-            if cols.start >= VECTOR_LAST_PAGE or t < 2:
+            if cols.start >= SCALAR_LAST_PAGE.start or t < 2:
                 nc.scalar.activation(z[:, :, t], page, COPY, scale=factor)
             elif t == 2:
                 twice = page.unsqueeze(2).to_broadcast([P, cols.stop - cols.start, 2])
@@ -336,62 +339,70 @@ def tile_list_woven_link_features_kernel(
                 nc.vector.tensor_scalar(z[:, :, t], page, factor, None, MULT)
 
         for t in range(LAST):
-            for cols in (slice(0, BANK), slice(BANK, VECTOR_LAST_PAGE), slice(VECTOR_LAST_PAGE, T2)):
-                round_page(t, cols)
+            for first, end in zip(PAGE_PIECES[t], PAGE_PIECES[t][1:]):
+                round_page(t, slice(first, end))
         wo_codes = placed("wo_codes", [P, N], U32, a_bytes(LAST, 1))
         wo_plane = placed("wo_plane", [P, N], U8, a_bytes(LAST, 1) + 4 * N)
         nc.vector.quantize_mx(wo_codes[:].bitcast(FP8X4), wo_plane[:], wo_bf[:])
         nc.vector.tensor_tensor(pages[LAST][:].indirect(list3[:]), h1[LAST][:], gates1[LAST][:], MULT)
-        round_page(LAST, slice(VECTOR_LAST_PAGE, T2))
+        round_page(LAST, SCALAR_LAST_PAGE)
 
         z_codes = kept("z_codes", [P, T2], U32)
         z_plane = kept("z_plane", [P, T2], U8)
         y_codes = kept("y_codes", [P, T2], U32)
-        y_plane = kept("y_plane", [P, T2], U8)
+        y_plane = kept("y_plane", [P, BANK], U8)
         out_rows = out_0.rearrange("(p t) m -> p t m", t=PACK)
         out_words = out_1[0].rearrange("p m t -> p (m t)").bitcast(I32)
 
-        ys = [placed("y%d" % g, [P, PACK, BANK], F32, RESULT_PLACES[g]) for g in range(T2 // BANK)]
+        groups = T2 // BANK
+        ys = [placed("y%d" % g, [P, PACK, BANK], F32, 4 * PACK * BANK * g) for g in range(groups)]
+        y_bf = placed("y_bf", [P, PACK * T2], BF16, STREAMS)
 
         def last_product(c):
             w, cols = CHUNKS[c], chunk_cols[c]
-            if cols.start < VECTOR_LAST_PAGE:
-                round_page(LAST, slice(cols.start, min(cols.stop, VECTOR_LAST_PAGE)))
-            nc.vector.quantize_mx(z_codes[:, cols].bitcast(FP8X4), z_plane[:, cols], z_cols(cols))
+            pieces = [slice(first, end) for first, end in Z_PIECES[c]]
+            for piece in pieces:
+                round_page(LAST, slice(piece.start, min(piece.stop, SCALAR_LAST_PAGE.start)))
+            for piece in pieces:
+                nc.vector.quantize_mx(z_codes[:, piece].bitcast(FP8X4), z_plane[:, piece], z_cols(piece))
             y = ys[cols.start // BANK][:, :, cols.start % BANK : cols.start % BANK + w]
-            per_bank = BANK // w
-            for first in range(0, PACK, per_bank):
-                bank = take(banks)[:].rearrange("p (i m) -> p i m", m=w)
-                for i in range(per_bank):
-                    rows = slice((first + i) * P, (first + i + 1) * P)
-                    nc.tensor.matmul_mx(
-                        bank[:, i, :], lhsT=wo_codes[:, rows].bitcast(FP8X4), lhsT_scale=wo_plane[:, rows],
-                        rhs=z_codes[:, cols].bitcast(FP8X4), rhs_scale=z_plane[:, cols], start=True, stop=True,
-                    )
-                nc.scalar.copy(y[:, first : first + per_bank, :], bank)
-                done = first + per_bank
+            for first in range(0, PACK, BANK_ROWS[c]):
+                done = first + BANK_ROWS[c]
+                bank = take(banks)[:, : BANK_ROWS[c] * w].rearrange("p (i m) -> p i m", m=w)
+                for t in range(first, done):
+                    rows = slice(t * P, (t + 1) * P)
+                    for piece in pieces:
+                        nc.tensor.matmul_mx(
+                            bank[:, t - first, piece.start - cols.start : piece.stop - cols.start],
+                            lhsT=wo_codes[:, rows].bitcast(FP8X4), lhsT_scale=wo_plane[:, rows],
+                            rhs=z_codes[:, piece].bitcast(FP8X4), rhs_scale=z_plane[:, piece], start=True, stop=True,
+                        )
+                nc.scalar.copy(y[:, first:done, :], bank)
                 if done % STORE_ROWS[c] == 0:
                     stored = slice(done - STORE_ROWS[c], done)
                     queue = nc.scalar if cols.start >= T2 // 2 else nc.sync
                     queue.dma_start(out_rows[:, stored, cols], y[:, stored, :])
 
-        def store_codes(first, w, on_scalar):
-            cols = slice(first, first + w)
-            grouped = placed("y_bf%d" % first, [P, w, PACK], BF16, STREAMS + 2 * PACK * first)
-            dst = grouped[:].rearrange("p (c i) t -> p c t i", i=PACK)
-            src = ys[first // BANK][:, :, first % BANK : first % BANK + w].rearrange("p t (c i) -> p c t i", i=PACK)
-            if on_scalar:
-                nc.scalar.copy(dst, src)
-            else:
-                nc.vector.tensor_copy(dst, src)
-            nc.vector.quantize_mx(y_codes[:, cols].bitcast(FP8X4), y_plane[:, cols], grouped[:].rearrange("p m t -> p (m t)"))
-            if cols.stop % CODE_STORE == 0:
-                stored = slice(cols.stop - CODE_STORE, cols.stop)
-                nc.sync.dma_start(out_words[:, stored], y_codes[:, stored].bitcast(I32))
+        def round_result(copy, g, first, end):
+            dst = y_bf[:, PACK * (BANK * g + first) : PACK * (BANK * g + end)].rearrange("p (c i t) -> p c t i", i=PACK, t=PACK)
+            copy(dst, ys[g][:, :, first:end].rearrange("p t (c i) -> p c t i", i=PACK))
+            nc.vector.quantize_mx(
+                y_codes[:, BANK * g + first : BANK * g + end].bitcast(FP8X4), y_plane[SCALE_ROWS * g :, first:end],
+                y_bf[:, PACK * (BANK * g + first) : PACK * (BANK * g + end)],
+            )
 
         for c in range(len(CHUNKS)):
             last_product(c)
-        for piece in CODE_PIECES:
-            store_codes(*piece)
+        for g in range(groups):
+            cols = slice(BANK * g, BANK * (g + 1))
+            if g < groups - 1:
+                round_result(nc.vector.tensor_copy, g, 0, BANK)
+            else:
+                round_result(nc.vector.tensor_copy, g, 0, VECTOR_LAST_RESULT)
+                round_result(nc.scalar.copy, g, VECTOR_LAST_RESULT, BANK)
+            if cols.stop in CODE_STORES:
+                stored = slice(((0,) + CODE_STORES)[CODE_STORES.index(cols.stop)], cols.stop)
+                nc.sync.dma_start(out_words[:, stored], y_codes[:, stored].bitcast(I32))
         for q in range(QUADRANTS):
-            (nc.scalar, nc.sync)[q % 2].dma_start(scale_rows(out_2, q), plane_rows(y_plane, q))
+            packed = y_plane[QUADRANT * q : QUADRANT * q + SCALE_ROWS * groups, :].bitcast(I32)
+            (nc.scalar, nc.sync)[q % 2].dma_start(scale_rows(out_2, q).rearrange("r (g c) -> g r c", g=groups), packed)

@@ -31,26 +31,32 @@ LIST_COLS = S // 16
 HALF = S // 2
 LINK_TILES = HALF // P
 WAI_PIECES = ((0, 384), (384, 128))
-CHUNKS = (256, 256, 512, 512, 512)
+
+STORE_EDGES = (0, 256, 512, 1024, 2048)
+Z_EDGES = (0, 256, 512, 1024, 1536, 2048)
 Z_FIRST = 768
-SCALAR_LAST_PAGE = slice(1664, 2048)
-Z_PIECES = (((0, 256),), ((256, 512),), ((512, 768), (768, 1024)), ((1024, 1536),), ((1536, 2048),))
-PAGE_PIECES = ((0, 768, 2048), (0, 768, 2048), (0, 512, 768, 1024, 1664, 2048))
-BANK_ROWS = (1, 2, 1, 1, 1)
-STORE_ROWS = (1, 2, 1, 2, 2)
+VECTOR_PAGE_EDGES = (0, 256, 384, 512, 1024, 1536)
+PAGE_EDGES = ((0, 768, 2048), (0, 768, 2048), (0, 384, 768, 1024, 1536, 2048))
 VECTOR_LAST_RESULT = 256
-CODE_STORES = (512, 1536, 2048)
+CODE_EDGES = (0, 512, 1536, 2048)
+
 KIB = 1024
 B_FACTORS = 0
 A_FACTORS = 32 * KIB
 FACTOR_PLACES = (0, 1, 2, 0, 1, 5, 6, 7)
 STREAMS = 64 * KIB
 PAGES = 80 * KIB
-GATES2 = 112 * KIB
+PAGE_ORDER = (0, 3, 2, 1)
+WB_DEALT = 112 * KIB
+GATES2 = (156 * KIB, 116 * KIB, 120 * KIB, 124 * KIB)
 GATES1 = 128 * KIB
 GATE1_ORDER = (1, 0, 2, 3)
 WA_ROUNDED = 144 * KIB
 WORDS1 = 152 * KIB
+
+
+def pieces(edges):
+    return [slice(first, end) for first, end in zip(edges, edges[1:])]
 
 
 def tile_list_woven_link_features_kernel(
@@ -72,13 +78,13 @@ def tile_list_woven_link_features_kernel(
             return keep.tile(shape, dtype, name=name, align_bytes=64)
 
         def page_bytes(t):
-            return PAGES + 8 * KIB * t
+            return PAGES + 8 * KIB * PAGE_ORDER.index(t)
 
         def a_bytes(t, half):
             return A_FACTORS + 8 * KIB * t + 4 * KIB * half
 
         def gate2_bytes(t):
-            return GATES2 + 4 * KIB * t
+            return GATES2[t]
 
         def gate1_bytes(t):
             return GATES1 + 4 * KIB * GATE1_ORDER.index(t)
@@ -88,29 +94,29 @@ def tile_list_woven_link_features_kernel(
             nc.sync.dma_start(tile[:], offsets)
             return tile
 
-        def zeroed_plane(plane, engine):
+        def zeroed_plane(name, width, engine):
+            plane = kept(name, [P, width], U8)
             engine.memset(plane[:].bitcast(I32), 0)
             return plane
-
-        def plane_rows(plane, q):
-            return plane[QUADRANT * q : QUADRANT * q + SCALE_ROWS, :].bitcast(I32)
 
         def scale_rows(scales, q):
             return scales[0, SCALE_ROWS * q : SCALE_ROWS * (q + 1), :].bitcast(I32)
 
         def load_plane(plane, scales):
             for q in QUADRANT_ORDER:
-                nc.sync.dma_start(plane_rows(plane, q), scale_rows(scales, q))
+                nc.sync.dma_start(plane[QUADRANT * q : QUADRANT * q + SCALE_ROWS, :].bitcast(I32), scale_rows(scales, q))
 
         def load_e4m3_words(tile, words):
             nc.sync.dma_start(tile[:], words[0].rearrange("p c i -> p (c i)").bitcast(I32))
             return tile
 
+        def dealt_rows(w, t):
+            return w.rearrange("(a t b) j -> t a b j", t=PACK, b=RUN)[t]
+
         def load_gate(name, wg, t, offset):
             tile = placed(name, [P, S], F32, offset)
-            rows = wg.rearrange("(a t b) j -> t a b j", t=PACK, b=RUN)[t]
             for q in QUADRANT_ORDER:
-                nc.sync.dma_start(tile[QUADRANT * q : QUADRANT * (q + 1)], rows)
+                nc.sync.dma_start(tile[QUADRANT * q : QUADRANT * (q + 1)], dealt_rows(wg, t))
             return tile
 
         def load_gain(t, tile):
@@ -122,17 +128,17 @@ def tile_list_woven_link_features_kernel(
             nc.sync.dma_start(raw[:], w.rearrange("(p i) c -> p i c", i=PACK)[:, :, first : first + width])
             return raw
 
-        tab2_plane = zeroed_plane(kept("tab2_plane", [P, T], U8), nc.gpsimd)
-        wsp_plane = zeroed_plane(kept("wsp_plane", [P, H], U8), nc.gpsimd)
-        tab_plane = zeroed_plane(kept("tab_plane", [P, T], U8), nc.gpsimd)
-        wb_plane = zeroed_plane(kept("wb_plane", [P, 2 * H], U8), nc.gpsimd)
+        tab2_plane = zeroed_plane("tab2_plane", T, nc.gpsimd)
+        wsp_plane = zeroed_plane("wsp_plane", H, nc.gpsimd)
+        tab_plane = zeroed_plane("tab_plane", T, nc.gpsimd)
+        wb_plane = zeroed_plane("wb_plane", 2 * H, nc.gpsimd)
 
         wsp = load_e4m3_words(kept("wsp", [P, H], I32), wsp_words)
         list2 = load_list("list2", offs2)
         load_plane(tab2_plane, tab2_scales)
         tab2 = load_e4m3_words(placed("tab2", [P, T], I32, page_bytes(0)), tab2_words)
-        tab1 = load_e4m3_words(kept("tab1", [P, T], I32), tab_words)
         load_plane(wsp_plane, wsp_scales)
+        tab1 = load_e4m3_words(kept("tab1", [P, T], I32), tab_words)
         list1 = load_list("list1", offs)
         gates2 = [load_gate("gate2_0", wg2, 0, gate2_bytes(0))]
         list4 = load_list("list4", offs4)
@@ -141,7 +147,7 @@ def tile_list_woven_link_features_kernel(
         load_plane(wb_plane[:, :H], wbr_scales)
         gates2.append(load_gate("gate2_1", wg2, 1, gate2_bytes(1)))
         load_plane(wb_plane[:, H:], wbi_scales)
-        wai_raw = [load_weight("wai_raw%d" % i, wai, page_bytes(2 - i), *WAI_PIECES[i]) for i in range(2)]
+        wai_raw = [load_weight("wai_raw%d" % i, wai, (page_bytes(2), WB_DEALT - KIB // 2)[i], *WAI_PIECES[i]) for i in range(2)]
         wb = kept("wb", [P, 2, H // 2], I32)
         for i, words in enumerate((wbr_words, wbi_words)):
             nc.sync.dma_start(wb[:, i, :], words[0].bitcast(I32))
@@ -150,7 +156,7 @@ def tile_list_woven_link_features_kernel(
         gates1 = [load_gate("gate1_0", wg1, 0, gate1_bytes(0))]
         wo_raw = kept("wo_raw", [P, PACK, N], F32)
         for t in range(PACK):
-            nc.sync.dma_start(wo_raw[:, t, :], wo.rearrange("(a t b) n -> t a b n", t=PACK, b=RUN)[t])
+            nc.sync.dma_start(wo_raw[:, t, :], dealt_rows(wo, t))
         gates1.append(load_gate("gate1_1", wg1, 1, gate1_bytes(1)))
         gains = {t: load_gain(t, kept("gain%d" % t, [P, 1], F32)) for t in (0, LAST)}
         gates1.extend(load_gate("gate1_%d" % t, wg1, t, gate1_bytes(t)) for t in range(2, PACK))
@@ -166,45 +172,41 @@ def tile_list_woven_link_features_kernel(
             return bank
 
         def gather(picked, table, offsets):
-            nc.vector.tensor_copy(picked[:], table.indirect(offsets[:]))
+            nc.vector.tensor_copy(picked[:], table[:].bitcast(picked.dtype).indirect(offsets[:]))
             return picked
 
-        halves = [slice(half * HALF, (half + 1) * HALF) for half in range(2)]
+        def product(out, still, still_plane, moving, moving_plane):
+            nc.tensor.matmul_mx(out, lhsT=still, lhsT_scale=still_plane, rhs=moving, rhs_scale=moving_plane, start=True, stop=True)
 
-        wsp_dealt = kept("wsp_dealt", [P, H], I32)
-        nc.vector.tensor_copy(
-            wsp_dealt[:].rearrange("p (t a b) -> p t a b", t=PACK, b=RUN),
-            wsp[:].rearrange("p (a t b) -> p t a b", t=PACK, b=RUN),
-        )
-        scale2 = gather(kept("scale2", [P, S], U8), tab2_plane[:], list2)
-        words2 = gather(kept("words2", [P, S], U32), tab2[:].bitcast(U32), list2)
-        wsp_plane_dealt = kept("wsp_plane_dealt", [P, H], U8)
-        nc.vector.tensor_copy(
-            wsp_plane_dealt[:].bitcast(U16).rearrange("p (t a) -> p t a", t=PACK),
-            wsp_plane[:].bitcast(U16).rearrange("p (a t) -> p t a", t=PACK),
-        )
-        words1 = gather(placed("words1", [P, S], U32, WORDS1), tab1[:].bitcast(U32), list1)
+        def deal(dealt, raw, unit, dealt_form, raw_form, **sizes):
+            nc.scalar.copy(dealt[:].bitcast(unit).rearrange(dealt_form, **sizes), raw.bitcast(unit).rearrange(raw_form, **sizes))
+            return dealt
+
+        halves = pieces((0, HALF, S))
+        whole = slice(0, S)
+
+        wsp_dealt = deal(kept("wsp_dealt", [P, H], I32), wsp[:], U32, "p (t a b) -> p t a b", "p (a t b) -> p t a b", t=PACK, b=RUN)
+        wsp_plane_dealt = deal(kept("wsp_plane_dealt", [P, H], U8), wsp_plane[:], U16, "p (t a) -> p t a", "p (a t) -> p t a", t=PACK)
+        scale2 = gather(kept("scale2", [P, S], U8), tab2_plane, list2)
+        words2 = gather(kept("words2", [P, S], U32), tab2, list2)
+        words1 = gather(placed("words1", [P, S], U32, WORDS1), tab1, list1)
 
         h2 = [placed("h2_%d" % t, [P, S], F32, STREAMS + 4 * KIB * t) for t in range(PACK)]
         for t in range(PACK):
             rows = slice(t * P, (t + 1) * P)
             for cols in halves:
                 bank = take(sum_banks)
-                nc.tensor.matmul_mx(
-                    bank[:], lhsT=wsp_dealt[:, rows].bitcast(FP8X4), lhsT_scale=wsp_plane_dealt[:, rows],
-                    rhs=words2[:, cols].bitcast(FP8X4), rhs_scale=scale2[:, cols], start=True, stop=True,
-                )
+                product(bank[:], wsp_dealt[:, rows].bitcast(FP8X4), wsp_plane_dealt[:, rows], words2[:, cols].bitcast(FP8X4), scale2[:, cols])
                 nc.scalar.copy(h2[t][:, cols], bank[:])
 
         pages = [placed("page%d" % t, [P, T2], F32, page_bytes(t)) for t in range(PACK)]
 
-        def gate_and_scatter(page, offsets, gated, stream, gate, cols):
-            nc.gpsimd.tensor_tensor(gated[:, cols], stream[:, cols], gate[:, cols], MULT)
-            nc.vector.tensor_copy(page[:].indirect(offsets[:, cols.start // 16 : cols.stop // 16]), gated[:, cols])
+        def gate_and_scatter(page, offsets, gated, stream, gate):
+            nc.gpsimd.tensor_tensor(gated[:], stream[:], gate[:], MULT)
+            nc.vector.tensor_copy(page[:].indirect(offsets[:]), gated[:])
 
-        whole = slice(0, S)
         nc.vector.tensor_tensor(pages[0][:].indirect(list4[:]), h2[0][:], gates2[0][:], MULT)
-        scale1 = gather(kept("scale1", [P, S], U8), tab_plane[:], list1)
+        scale1 = gather(kept("scale1", [P, S], U8), tab_plane, list1)
 
         wa_bf = placed("wa_bf", [P, 2 * PACK * H], BF16, WA_ROUNDED)[:]
         wa_places = wa_bf.rearrange("p (t w a b i) -> p w t a i b", t=PACK, w=2, b=RUN, i=PACK)
@@ -217,22 +219,14 @@ def tile_list_woven_link_features_kernel(
         round_a_weight(0, war_raw, 0, 1.0)
         for i in range(2):
             round_a_weight(1, wai_raw[i], WAI_PIECES[i][0] // (PACK * RUN), -1.0)
-        wb_plane_dealt = kept("wb_plane_dealt", [P, 2 * H], U8)
-        nc.vector.tensor_copy(
-            wb_plane_dealt[:].bitcast(U16).rearrange("p (t w a) -> p t w a", t=PACK, w=2),
-            wb_plane[:].bitcast(U16).rearrange("p (w a t) -> p t w a", t=PACK, w=2),
-        )
-        wb_dealt = kept("wb_dealt", [P, H], I32)
-        nc.vector.tensor_copy(
-            wb_dealt[:].rearrange("p (t w a) -> p t w a", t=PACK, w=2),
-            wb[:].rearrange("p w (a t) -> p t w a", t=PACK),
-        )
         wa_codes = kept("wa_codes", [P, 2 * H], U32)
         wa_plane = kept("wa_plane", [P, 2 * H], U8)
         nc.vector.quantize_mx(wa_codes[:].bitcast(FP8X4), wa_plane[:], wa_bf)
+        wb_plane_dealt = deal(placed("wb_plane_dealt", [P, 2 * H], U8, WB_DEALT), wb_plane[:], U16, "p (t w a) -> p t w a", "p (w a t) -> p t w a", t=PACK, w=2)
+        wb_dealt = deal(placed("wb_dealt", [P, H], I32, WB_DEALT + KIB), wb[:].rearrange("p w c -> p (w c)"), U32, "p (t w a) -> p t w a", "p (w a t) -> p t w a", t=PACK, w=2)
         for t in range(1, PACK):
             gated = placed("gated2_last", [P, S], F32, B_FACTORS + 12 * KIB) if t == LAST else h2[t]
-            gate_and_scatter(pages[t], list4, gated, h2[t], gates2[t], whole)
+            gate_and_scatter(pages[t], list4, gated, h2[t], gates2[t])
 
         def factors(name, offset, weights, plane, step):
             t, half = divmod(step, 2)
@@ -240,18 +234,15 @@ def tile_list_woven_link_features_kernel(
             for pair in range(LINK_TILES // 2):
                 bank = take(sum_banks)
                 if t == LAST:
-                    nc.tensor.matmul_mx(
-                        bank[:], lhsT=weights(2 * t + pair, 1), lhsT_scale=plane[:, P * (2 * t + pair) : P * (2 * t + pair + 1)],
-                        rhs=words1[:, halves[half]].bitcast(FP8X4), rhs_scale=scale1[:, halves[half]], start=True, stop=True,
-                    )
+                    w = 2 * t + pair
+                    product(bank[:], weights(w, 1), plane[:, P * w : P * (w + 1)], words1[:, halves[half]].bitcast(FP8X4), scale1[:, halves[half]])
                     nc.scalar.copy(tile[:, pair, :], bank[:])
                     continue
                 for lt in range(2):
-                    first = HALF * half + P * (2 * pair + lt)
-                    nc.tensor.matmul_mx(
-                        bank[:, 2 * P * lt : 2 * P * (lt + 1)],
-                        lhsT=words1[:, first : first + P].bitcast(FP8X4), lhsT_scale=scale1[:, first : first + P],
-                        rhs=weights(2 * t, 2), rhs_scale=plane[:, 2 * P * t : 2 * P * (t + 1)], start=True, stop=True,
+                    links = slice(HALF * half + P * (2 * pair + lt), HALF * half + P * (2 * pair + lt + 1))
+                    product(
+                        bank[:, 2 * P * lt : 2 * P * (lt + 1)], words1[:, links].bitcast(FP8X4), scale1[:, links],
+                        weights(2 * t, 2), plane[:, 2 * P * t : 2 * P * (t + 1)],
                     )
                 places = tile[:, :, 2 * P * pair : 2 * P * (pair + 1)].rearrange("p i (lt m) -> p lt i m", lt=2)
                 nc.scalar.copy(places, bank[:].rearrange("p (lt i m) -> p lt i m", lt=2, i=2))
@@ -268,23 +259,18 @@ def tile_list_woven_link_features_kernel(
 
         h1 = [placed("h1_%d" % t, [P, S], F32, (STREAMS, gate2_bytes(2), STREAMS + 8 * KIB, STREAMS + 8 * KIB)[t]) for t in range(PACK)]
         gated1 = [placed("gated1_%d" % t, [P, S], F32, (a_bytes(1, 1), a_bytes(1, 0), a_bytes(2, 0))[t]) for t in range(LAST)]
+        product_bytes = (
+            gate2_bytes(2), gate2_bytes(3), STREAMS + 12 * KIB, gate1_bytes(0), STREAMS, gate1_bytes(1), gate2_bytes(2), gate1_bytes(2),
+        )
 
-        def multiply_and_turn(step):
-            t, half = divmod(step, 2)
+        def multiply(step):
             a, b = factor_tiles[step]
-            products = a
-            if t == 0:
-                products = placed("products_first%d" % half, [P, 2, HALF], F32, gate2_bytes(2 + half))
-            if half == 0 and t > 0:
-                products = placed("products_next%d" % t, [P, 2, HALF], F32, (STREAMS + 12 * KIB, STREAMS, gate2_bytes(2))[t - 1])
-            if half == 1 and t > 0:
-                products = placed("products%d" % t, [P, 2, HALF], F32, gate1_bytes(t - 1))
-            nc.gpsimd.tensor_tensor(
-                products[:].rearrange("p i c -> p (i c)"), a[:].rearrange("p i c -> p (i c)"),
-                b[:].rearrange("p i c -> p (i c)"), MULT,
-            )
-            if t == LAST:
-                return products
+            products = placed("products%d" % step, [P, 2, HALF], F32, product_bytes[step])
+            nc.gpsimd.tensor_tensor(*(x[:].rearrange("p i c -> p (i c)") for x in (products, a, b)), MULT)
+            return products
+
+        def turn(step, products):
+            t, half = divmod(step, 2)
             bank = take(turn_banks)
             for lt in range(LINK_TILES):
                 for i in range(2):
@@ -300,52 +286,53 @@ def tile_list_woven_link_features_kernel(
         for step in range(steps):
             if step + 2 < steps:
                 factor_tiles.append(both_factors(step + 2))
-            unturned.append(multiply_and_turn(step))
+            products = multiply(step)
+            if step // 2 < LAST:
+                turn(step, products)
+            else:
+                unturned.append(products)
             if step % 2 == 0 and step > 0:
                 t = step // 2 - 1
-                gate_and_scatter(pages[t], list3, gated1[t], h1[t], gates1[t], whole)
+                gate_and_scatter(pages[t], list3, gated1[t], h1[t], gates1[t])
 
-        for half in range(2):
-            products = unturned[2 * LAST + half]
-            nc.gpsimd.tensor_tensor(h1[LAST][:, halves[half]], products[:, 0, :], products[:, 1, :], ADD)
+        for cols, products in zip(halves, unturned):
+            nc.gpsimd.tensor_tensor(h1[LAST][:, cols], products[:, 0, :], products[:, 1, :], ADD)
         for t in (1, 2):
             gains[t] = load_gain(t, placed("gain%d" % t, [P, 1], F32, a_bytes(2, 1) + 64 * t))
 
         wo_bf = placed("wo_bf", [P, PACK * N], BF16, WORDS1)
         dst = wo_bf[:].rearrange("p (t m i) -> p m t i", t=PACK, i=PACK)
         src = wo_raw[:].rearrange("p i (m t) -> p m t i", t=PACK)
-        for half in range(2):
-            ms = slice(half * P // 2, (half + 1) * P // 2)
+        for ms in pieces((0, P // 2, P)):
             nc.scalar.copy(dst[:, ms], src[:, ms])
 
-        chunk_cols = [slice(sum(CHUNKS[:c]), sum(CHUNKS[: c + 1])) for c in range(len(CHUNKS))]
         z_first = placed("z_first", [P, PACK * Z_FIRST], BF16, STREAMS)
         z_main = placed("z_main", [P, PACK * (T2 - Z_FIRST)], BF16, gate1_bytes(2) - 2 * PACK * (T2 - Z_FIRST))
 
-        def z_cols(cols):
+        def z_places(cols):
             if cols.stop <= Z_FIRST:
                 return z_first[:, PACK * cols.start : PACK * cols.stop]
             return z_main[:, PACK * (cols.start - Z_FIRST) : PACK * (cols.stop - Z_FIRST)]
 
-        def round_page(t, cols):
+        def round_page(engine, t, cols):
             page, factor = pages[t][:, cols], gains[t][:]
-            z = z_cols(cols).rearrange("p (m t) -> p m t", t=PACK)
-            if cols.start >= SCALAR_LAST_PAGE.start or t < 2:
-                nc.scalar.activation(z[:, :, t], page, COPY, scale=factor)
-            elif t == 2:
+            z = z_places(cols).rearrange("p (m t) -> p m t", t=PACK)
+            if engine is nc.vector:
+                nc.vector.tensor_scalar(z[:, :, t], page, factor, None, MULT)
+            elif t == 2 and cols.start < VECTOR_PAGE_EDGES[-1]:
                 twice = page.unsqueeze(2).to_broadcast([P, cols.stop - cols.start, 2])
                 nc.scalar.activation(z[:, :, t : t + 2], twice, COPY, scale=factor)
             else:
-                nc.vector.tensor_scalar(z[:, :, t], page, factor, None, MULT)
+                nc.scalar.activation(z[:, :, t], page, COPY, scale=factor)
 
         for t in range(LAST):
-            for first, end in zip(PAGE_PIECES[t], PAGE_PIECES[t][1:]):
-                round_page(t, slice(first, end))
+            for cols in pieces(PAGE_EDGES[t]):
+                round_page(nc.scalar, t, cols)
         wo_codes = placed("wo_codes", [P, N], U32, a_bytes(LAST, 1))
         wo_plane = placed("wo_plane", [P, N], U8, a_bytes(LAST, 1) + 4 * N)
         nc.vector.quantize_mx(wo_codes[:].bitcast(FP8X4), wo_plane[:], wo_bf[:])
         nc.vector.tensor_tensor(pages[LAST][:].indirect(list3[:]), h1[LAST][:], gates1[LAST][:], MULT)
-        round_page(LAST, SCALAR_LAST_PAGE)
+        round_page(nc.scalar, LAST, slice(VECTOR_PAGE_EDGES[-1], T2))
 
         z_codes = kept("z_codes", [P, T2], U32)
         z_plane = kept("z_plane", [P, T2], U8)
@@ -353,55 +340,73 @@ def tile_list_woven_link_features_kernel(
         y_plane = kept("y_plane", [P, BANK], U8)
         out_rows = out_0.rearrange("(p t) m -> p t m", t=PACK)
         out_words = out_1[0].rearrange("p m t -> p (m t)").bitcast(I32)
-
-        groups = T2 // BANK
-        ys = [placed("y%d" % g, [P, PACK, BANK], F32, 4 * PACK * BANK * g) for g in range(groups)]
+        y_edges = (0, BANK, 2 * BANK, T2)
+        ys = [placed("y%d" % i, [P, PACK, cols.stop - cols.start], F32, 4 * PACK * cols.start) for i, cols in enumerate(pieces(y_edges))]
         y_bf = placed("y_bf", [P, PACK * T2], BF16, STREAMS)
 
-        def last_product(c):
-            w, cols = CHUNKS[c], chunk_cols[c]
-            pieces = [slice(first, end) for first, end in Z_PIECES[c]]
-            for piece in pieces:
-                round_page(LAST, slice(piece.start, min(piece.stop, SCALAR_LAST_PAGE.start)))
-            for piece in pieces:
-                nc.vector.quantize_mx(z_codes[:, piece].bitcast(FP8X4), z_plane[:, piece], z_cols(piece))
-            y = ys[cols.start // BANK][:, :, cols.start % BANK : cols.start % BANK + w]
-            for first in range(0, PACK, BANK_ROWS[c]):
-                done = first + BANK_ROWS[c]
-                bank = take(banks)[:, : BANK_ROWS[c] * w].rearrange("p (i m) -> p i m", m=w)
-                for t in range(first, done):
-                    rows = slice(t * P, (t + 1) * P)
-                    for piece in pieces:
-                        nc.tensor.matmul_mx(
-                            bank[:, t - first, piece.start - cols.start : piece.stop - cols.start],
-                            lhsT=wo_codes[:, rows].bitcast(FP8X4), lhsT_scale=wo_plane[:, rows],
-                            rhs=z_codes[:, piece].bitcast(FP8X4), rhs_scale=z_plane[:, piece], start=True, stop=True,
-                        )
-                nc.scalar.copy(y[:, first:done, :], bank)
-                if done % STORE_ROWS[c] == 0:
-                    stored = slice(done - STORE_ROWS[c], done)
-                    queue = nc.scalar if cols.start >= T2 // 2 else nc.sync
-                    queue.dma_start(out_rows[:, stored, cols], y[:, stored, :])
+        def y_places(cols):
+            i = min(cols.start // BANK, len(ys) - 1)
+            return ys[i][:, :, cols.start - y_edges[i] : cols.stop - y_edges[i]]
 
-        def round_result(copy, g, first, end):
-            dst = y_bf[:, PACK * (BANK * g + first) : PACK * (BANK * g + end)].rearrange("p (c i t) -> p c t i", i=PACK, t=PACK)
-            copy(dst, ys[g][:, :, first:end].rearrange("p t (c i) -> p c t i", i=PACK))
-            nc.vector.quantize_mx(
-                y_codes[:, BANK * g + first : BANK * g + end].bitcast(FP8X4), y_plane[SCALE_ROWS * g :, first:end],
-                y_bf[:, PACK * (BANK * g + first) : PACK * (BANK * g + end)],
-            )
+        vector_rounds = pieces(sorted(VECTOR_PAGE_EDGES + (Z_FIRST,)))
 
-        for c in range(len(CHUNKS)):
-            last_product(c)
-        for g in range(groups):
-            cols = slice(BANK * g, BANK * (g + 1))
-            if g < groups - 1:
-                round_result(nc.vector.tensor_copy, g, 0, BANK)
+        def quantise_z(cols, ahead):
+            while vector_rounds and vector_rounds[0].start < ahead:
+                round_page(nc.vector, LAST, vector_rounds.pop(0))
+            for piece in pieces(sorted({cols.start, cols.stop} | ({Z_FIRST} if cols.start < Z_FIRST < cols.stop else set()))):
+                nc.vector.quantize_mx(z_codes[:, piece].bitcast(FP8X4), z_plane[:, piece], z_places(piece))
+
+        def last_product(rows, cols, empty):
+            bank = take(banks)[:, : len(rows) * (cols.stop - cols.start)].rearrange("p (i m) -> p i m", i=len(rows))
+            for i, t in enumerate(rows):
+                channels = slice(t * P, (t + 1) * P)
+                product(bank[:, i, :], wo_codes[:, channels].bitcast(FP8X4), wo_plane[:, channels], z_codes[:, cols].bitcast(FP8X4), z_plane[:, cols])
+            empty(y_places(cols)[:, rows.start : rows.stop, :], bank)
+
+        def store(queue, rows, cols):
+            queue.dma_start(out_rows[:, rows.start : rows.stop, cols], y_places(cols)[:, rows.start : rows.stop, :])
+
+        z_cols = pieces(Z_EDGES)
+        stores = pieces(STORE_EDGES)
+        single_rows = [range(t, t + 1) for t in range(PACK)]
+        row_pairs = [range(t, t + 2) for t in range(0, PACK, 2)]
+        quantise_z(z_cols[0], VECTOR_PAGE_EDGES[2])
+        for c, row_sets in enumerate((single_rows, row_pairs, single_rows)):
+            if c > 0:
+                quantise_z(z_cols[c], z_cols[c].stop)
+            for rows in row_sets:
+                last_product(rows, z_cols[c], nc.scalar.copy)
+                store(nc.sync, rows, stores[c])
+        for cols in z_cols[3:]:
+            quantise_z(cols, cols.stop)
+        left, right = z_cols[3:]
+        for rows in single_rows[:2]:
+            last_product(rows, left, nc.scalar.copy)
+            last_product(rows, right, nc.scalar.copy)
+            store(nc.scalar, rows, stores[3])
+        last_product(single_rows[2], left, nc.scalar.copy)
+        last_product(single_rows[3], left, nc.vector.tensor_copy)
+        for rows in single_rows[2:]:
+            last_product(rows, right, nc.scalar.copy)
+            store(nc.scalar, rows, stores[3])
+
+        groups = T2 // BANK
+
+        def quantise_result(copy, cols):
+            g, first = divmod(cols.start, BANK)
+            rounded = y_bf[:, PACK * cols.start : PACK * cols.stop]
+            copy(rounded.rearrange("p (c i t) -> p c t i", i=PACK, t=PACK), y_places(cols).rearrange("p t (c i) -> p c t i", i=PACK))
+            nc.vector.quantize_mx(y_codes[:, cols].bitcast(FP8X4), y_plane[SCALE_ROWS * g :, first : first + cols.stop - cols.start], rounded)
+
+        code_stores = pieces(CODE_EDGES)
+        for cols in pieces(range(0, T2 + 1, BANK)):
+            if cols.stop < T2:
+                quantise_result(nc.vector.tensor_copy, cols)
             else:
-                round_result(nc.vector.tensor_copy, g, 0, VECTOR_LAST_RESULT)
-                round_result(nc.scalar.copy, g, VECTOR_LAST_RESULT, BANK)
-            if cols.stop in CODE_STORES:
-                stored = slice(((0,) + CODE_STORES)[CODE_STORES.index(cols.stop)], cols.stop)
+                quantise_result(nc.vector.tensor_copy, slice(cols.start, cols.start + VECTOR_LAST_RESULT))
+                quantise_result(nc.scalar.copy, slice(cols.start + VECTOR_LAST_RESULT, T2))
+            if cols.stop == code_stores[0].stop:
+                stored = code_stores.pop(0)
                 nc.sync.dma_start(out_words[:, stored], y_codes[:, stored].bitcast(I32))
         for q in range(QUADRANTS):
             packed = y_plane[QUADRANT * q : QUADRANT * q + SCALE_ROWS * groups, :].bitcast(I32)

@@ -46,9 +46,7 @@ A_FACTORS = 32 * KIB
 FACTOR_PLACES = (0, 1, 2, 0, 1, 5, 6, 7)
 STREAMS = 64 * KIB
 PAGES = 80 * KIB
-PAGE_ORDER = (0, 3, 2, 1)
-WB_DEALT = 112 * KIB
-GATES2 = (156 * KIB, 116 * KIB, 120 * KIB, 124 * KIB)
+GATES2 = 112 * KIB
 GATES1 = 128 * KIB
 GATE1_ORDER = (1, 0, 2, 3)
 WA_ROUNDED = 144 * KIB
@@ -78,13 +76,13 @@ def tile_list_woven_link_features_kernel(
             return keep.tile(shape, dtype, name=name, align_bytes=64)
 
         def page_bytes(t):
-            return PAGES + 8 * KIB * PAGE_ORDER.index(t)
+            return PAGES + 8 * KIB * t
 
         def a_bytes(t, half):
             return A_FACTORS + 8 * KIB * t + 4 * KIB * half
 
         def gate2_bytes(t):
-            return GATES2[t]
+            return GATES2 + 4 * KIB * t
 
         def gate1_bytes(t):
             return GATES1 + 4 * KIB * GATE1_ORDER.index(t)
@@ -137,8 +135,8 @@ def tile_list_woven_link_features_kernel(
         list2 = load_list("list2", offs2)
         load_plane(tab2_plane, tab2_scales)
         tab2 = load_e4m3_words(placed("tab2", [P, T], I32, page_bytes(0)), tab2_words)
-        load_plane(wsp_plane, wsp_scales)
         tab1 = load_e4m3_words(kept("tab1", [P, T], I32), tab_words)
+        load_plane(wsp_plane, wsp_scales)
         list1 = load_list("list1", offs)
         gates2 = [load_gate("gate2_0", wg2, 0, gate2_bytes(0))]
         list4 = load_list("list4", offs4)
@@ -147,7 +145,7 @@ def tile_list_woven_link_features_kernel(
         load_plane(wb_plane[:, :H], wbr_scales)
         gates2.append(load_gate("gate2_1", wg2, 1, gate2_bytes(1)))
         load_plane(wb_plane[:, H:], wbi_scales)
-        wai_raw = [load_weight("wai_raw%d" % i, wai, (page_bytes(2), WB_DEALT - KIB // 2)[i], *WAI_PIECES[i]) for i in range(2)]
+        wai_raw = [load_weight("wai_raw%d" % i, wai, page_bytes(2 - i), *WAI_PIECES[i]) for i in range(2)]
         wb = kept("wb", [P, 2, H // 2], I32)
         for i, words in enumerate((wbr_words, wbi_words)):
             nc.sync.dma_start(wb[:, i, :], words[0].bitcast(I32))
@@ -179,16 +177,16 @@ def tile_list_woven_link_features_kernel(
             nc.tensor.matmul_mx(out, lhsT=still, lhsT_scale=still_plane, rhs=moving, rhs_scale=moving_plane, start=True, stop=True)
 
         def deal(dealt, raw, unit, dealt_form, raw_form, **sizes):
-            nc.scalar.copy(dealt[:].bitcast(unit).rearrange(dealt_form, **sizes), raw.bitcast(unit).rearrange(raw_form, **sizes))
+            nc.vector.tensor_copy(dealt[:].bitcast(unit).rearrange(dealt_form, **sizes), raw.bitcast(unit).rearrange(raw_form, **sizes))
             return dealt
 
         halves = pieces((0, HALF, S))
         whole = slice(0, S)
 
-        wsp_dealt = deal(kept("wsp_dealt", [P, H], I32), wsp[:], U32, "p (t a b) -> p t a b", "p (a t b) -> p t a b", t=PACK, b=RUN)
-        wsp_plane_dealt = deal(kept("wsp_plane_dealt", [P, H], U8), wsp_plane[:], U16, "p (t a) -> p t a", "p (a t) -> p t a", t=PACK)
+        wsp_dealt = deal(kept("wsp_dealt", [P, H], I32), wsp[:], I32, "p (t a b) -> p t a b", "p (a t b) -> p t a b", t=PACK, b=RUN)
         scale2 = gather(kept("scale2", [P, S], U8), tab2_plane, list2)
         words2 = gather(kept("words2", [P, S], U32), tab2, list2)
+        wsp_plane_dealt = deal(kept("wsp_plane_dealt", [P, H], U8), wsp_plane[:], U16, "p (t a) -> p t a", "p (a t) -> p t a", t=PACK)
         words1 = gather(placed("words1", [P, S], U32, WORDS1), tab1, list1)
 
         h2 = [placed("h2_%d" % t, [P, S], F32, STREAMS + 4 * KIB * t) for t in range(PACK)]
@@ -219,11 +217,11 @@ def tile_list_woven_link_features_kernel(
         round_a_weight(0, war_raw, 0, 1.0)
         for i in range(2):
             round_a_weight(1, wai_raw[i], WAI_PIECES[i][0] // (PACK * RUN), -1.0)
+        wb_plane_dealt = deal(kept("wb_plane_dealt", [P, 2 * H], U8), wb_plane[:], U16, "p (t w a) -> p t w a", "p (w a t) -> p t w a", t=PACK, w=2)
+        wb_dealt = deal(kept("wb_dealt", [P, H], I32), wb[:].rearrange("p w c -> p (w c)"), I32, "p (t w a) -> p t w a", "p (w a t) -> p t w a", t=PACK, w=2)
         wa_codes = kept("wa_codes", [P, 2 * H], U32)
         wa_plane = kept("wa_plane", [P, 2 * H], U8)
         nc.vector.quantize_mx(wa_codes[:].bitcast(FP8X4), wa_plane[:], wa_bf)
-        wb_plane_dealt = deal(placed("wb_plane_dealt", [P, 2 * H], U8, WB_DEALT), wb_plane[:], U16, "p (t w a) -> p t w a", "p (w a t) -> p t w a", t=PACK, w=2)
-        wb_dealt = deal(placed("wb_dealt", [P, H], I32, WB_DEALT + KIB), wb[:].rearrange("p w c -> p (w c)"), U32, "p (t w a) -> p t w a", "p (w a t) -> p t w a", t=PACK, w=2)
         for t in range(1, PACK):
             gated = placed("gated2_last", [P, S], F32, B_FACTORS + 12 * KIB) if t == LAST else h2[t]
             gate_and_scatter(pages[t], list4, gated, h2[t], gates2[t])

@@ -145,10 +145,11 @@ def tile_list_woven_link_features_kernel(
         load_plane(wb_plane[:, :H], wbr_scales)
         gates2.append(load_gate("gate2_1", wg2, 1, gate2_bytes(1)))
         load_plane(wb_plane[:, H:], wbi_scales)
-        wai_raw = [load_weight("wai_raw%d" % i, wai, page_bytes(2 - i), *WAI_PIECES[i]) for i in range(2)]
+        wai_raw = [load_weight("wai_raw0", wai, page_bytes(2), *WAI_PIECES[0])]
         wb = kept("wb", [P, 2, H // 2], I32)
         for i, words in enumerate((wbr_words, wbi_words)):
             nc.sync.dma_start(wb[:, i, :], words[0].bitcast(I32))
+        wai_raw.append(load_weight("wai_raw1", wai, page_bytes(1), *WAI_PIECES[1]))
         gates2.extend(load_gate("gate2_%d" % t, wg2, t, gate2_bytes(t)) for t in range(2, PACK))
         list3 = load_list("list3", offs3)
         gates1 = [load_gate("gate1_0", wg1, 0, gate1_bytes(0))]
@@ -253,7 +254,8 @@ def tile_list_woven_link_features_kernel(
             return wb_dealt[:, P // 2 * first : P // 2 * (first + count)].bitcast(FP4X4)
 
         def both_factors(step):
-            return factors("a", A_FACTORS, a_weights, wa_plane, step), factors("b", B_FACTORS, b_weights, wb_plane_dealt, step)
+            b = factors("b", B_FACTORS, b_weights, wb_plane_dealt, step)
+            return factors("a", A_FACTORS, a_weights, wa_plane, step), b
 
         h1 = [placed("h1_%d" % t, [P, S], F32, (STREAMS, gate2_bytes(2), STREAMS + 8 * KIB, STREAMS + 8 * KIB)[t]) for t in range(PACK)]
         gated1 = [placed("gated1_%d" % t, [P, S], F32, (a_bytes(1, 1), a_bytes(1, 0), a_bytes(2, 0))[t]) for t in range(LAST)]

@@ -30,7 +30,7 @@ BANK = 512
 LIST_COLS = S // 16
 HALF = S // 2
 LINK_TILES = HALF // P
-WAI_PIECES = ((0, 384), (384, 128))
+WAI_PIECES = ((0, 256), (256, 256))
 
 STORE_EDGES = (0, 256, 512, 1024, 2048)
 Z_EDGES = (0, 256, 512, 1024, 1536, 2048)
@@ -46,7 +46,9 @@ A_FACTORS = 32 * KIB
 FACTOR_PLACES = (0, 1, 2, 0, 1, 5, 6, 7)
 STREAMS = 64 * KIB
 PAGES = 80 * KIB
-GATES2 = 112 * KIB
+PAGE_ORDER = (0, 3, 2, 1)
+H2_LAST = 112 * KIB
+GATES2 = (156 * KIB, 116 * KIB, 120 * KIB, 124 * KIB)
 GATES1 = 128 * KIB
 GATE1_ORDER = (1, 0, 2, 3)
 WA_ROUNDED = 144 * KIB
@@ -76,13 +78,13 @@ def tile_list_woven_link_features_kernel(
             return keep.tile(shape, dtype, name=name, align_bytes=64)
 
         def page_bytes(t):
-            return PAGES + 8 * KIB * t
+            return PAGES + 8 * KIB * PAGE_ORDER.index(t)
 
         def a_bytes(t, half):
             return A_FACTORS + 8 * KIB * t + 4 * KIB * half
 
         def gate2_bytes(t):
-            return GATES2 + 4 * KIB * t
+            return GATES2[t]
 
         def gate1_bytes(t):
             return GATES1 + 4 * KIB * GATE1_ORDER.index(t)
@@ -145,11 +147,11 @@ def tile_list_woven_link_features_kernel(
         load_plane(wb_plane[:, :H], wbr_scales)
         gates2.append(load_gate("gate2_1", wg2, 1, gate2_bytes(1)))
         load_plane(wb_plane[:, H:], wbi_scales)
-        wai_raw = [load_weight("wai_raw0", wai, page_bytes(2), *WAI_PIECES[0])]
         wb = kept("wb", [P, 2, H // 2], I32)
         for i, words in enumerate((wbr_words, wbi_words)):
             nc.sync.dma_start(wb[:, i, :], words[0].bitcast(I32))
-        wai_raw.append(load_weight("wai_raw1", wai, page_bytes(1), *WAI_PIECES[1]))
+        wai_raw = [load_weight("wai_raw0", wai, page_bytes(2), *WAI_PIECES[0])]
+        wai_raw.append(load_weight("wai_raw1", wai, H2_LAST - KIB, *WAI_PIECES[1]))
         gates2.extend(load_gate("gate2_%d" % t, wg2, t, gate2_bytes(t)) for t in range(2, PACK))
         list3 = load_list("list3", offs3)
         gates1 = [load_gate("gate1_0", wg1, 0, gate1_bytes(0))]
@@ -177,26 +179,28 @@ def tile_list_woven_link_features_kernel(
         def product(out, still, still_plane, moving, moving_plane):
             nc.tensor.matmul_mx(out, lhsT=still, lhsT_scale=still_plane, rhs=moving, rhs_scale=moving_plane, start=True, stop=True)
 
-        def deal(dealt, raw, unit, dealt_form, raw_form, **sizes):
-            nc.vector.tensor_copy(dealt[:].bitcast(unit).rearrange(dealt_form, **sizes), raw.bitcast(unit).rearrange(raw_form, **sizes))
+        def deal(copy, dealt, raw, unit, dealt_form, raw_form, **sizes):
+            copy(dealt[:].bitcast(unit).rearrange(dealt_form, **sizes), raw.bitcast(unit).rearrange(raw_form, **sizes))
             return dealt
 
         halves = pieces((0, HALF, S))
         whole = slice(0, S)
 
-        wsp_dealt = deal(kept("wsp_dealt", [P, H], I32), wsp[:], I32, "p (t a b) -> p t a b", "p (a t b) -> p t a b", t=PACK, b=RUN)
+        wsp_dealt = deal(nc.vector.tensor_copy, kept("wsp_dealt", [P, H], I32), wsp[:], I32, "p (t a b) -> p t a b", "p (a t b) -> p t a b", t=PACK, b=RUN)
         scale2 = gather(kept("scale2", [P, S], U8), tab2_plane, list2)
         words2 = gather(kept("words2", [P, S], U32), tab2, list2)
-        wsp_plane_dealt = deal(kept("wsp_plane_dealt", [P, H], U8), wsp_plane[:], U16, "p (t a) -> p t a", "p (a t) -> p t a", t=PACK)
+        wsp_plane_dealt = deal(nc.vector.tensor_copy, kept("wsp_plane_dealt", [P, H], U8), wsp_plane[:], U16, "p (t a) -> p t a", "p (a t) -> p t a", t=PACK)
         words1 = gather(placed("words1", [P, S], U32, WORDS1), tab1, list1)
 
-        h2 = [placed("h2_%d" % t, [P, S], F32, STREAMS + 4 * KIB * t) for t in range(PACK)]
+        h2 = [placed("h2_%d" % t, [P, S], F32, STREAMS + 4 * KIB * t if t < LAST else H2_LAST) for t in range(PACK)]
         for t in range(PACK):
             rows = slice(t * P, (t + 1) * P)
             for cols in halves:
                 bank = take(sum_banks)
                 product(bank[:], wsp_dealt[:, rows].bitcast(FP8X4), wsp_plane_dealt[:, rows], words2[:, cols].bitcast(FP8X4), scale2[:, cols])
                 nc.scalar.copy(h2[t][:, cols], bank[:])
+
+        b_banks, a_banks = sum_banks[-2:], sum_banks[:-2]
 
         pages = [placed("page%d" % t, [P, T2], F32, page_bytes(t)) for t in range(PACK)]
 
@@ -218,8 +222,8 @@ def tile_list_woven_link_features_kernel(
         round_a_weight(0, war_raw, 0, 1.0)
         for i in range(2):
             round_a_weight(1, wai_raw[i], WAI_PIECES[i][0] // (PACK * RUN), -1.0)
-        wb_plane_dealt = deal(kept("wb_plane_dealt", [P, 2 * H], U8), wb_plane[:], U16, "p (t w a) -> p t w a", "p (w a t) -> p t w a", t=PACK, w=2)
-        wb_dealt = deal(kept("wb_dealt", [P, H], I32), wb[:].rearrange("p w c -> p (w c)"), I32, "p (t w a) -> p t w a", "p (w a t) -> p t w a", t=PACK, w=2)
+        wb_plane_dealt = deal(nc.scalar.copy, kept("wb_plane_dealt", [P, 2 * H], U8), wb_plane[:], U16, "p (t g a) -> p g t a", "p (g a t) -> p g t a", t=PACK, a=8)
+        wb_dealt = deal(nc.scalar.copy, kept("wb_dealt", [P, H], I32), wb[:].rearrange("p w c -> p (w c)"), U32, "p (t g a) -> p g t a", "p (g a t) -> p g t a", t=PACK, a=4)
         wa_codes = kept("wa_codes", [P, 2 * H], U32)
         wa_plane = kept("wa_plane", [P, 2 * H], U8)
         nc.vector.quantize_mx(wa_codes[:].bitcast(FP8X4), wa_plane[:], wa_bf)
@@ -227,11 +231,11 @@ def tile_list_woven_link_features_kernel(
             gated = placed("gated2_last", [P, S], F32, B_FACTORS + 12 * KIB) if t == LAST else h2[t]
             gate_and_scatter(pages[t], list4, gated, h2[t], gates2[t])
 
-        def factors(name, offset, weights, plane, step):
+        def factors(name, offset, ring, weights, plane, step):
             t, half = divmod(step, 2)
             tile = placed("%s_%d" % (name, step), [P, 2, HALF], F32, offset + 4 * KIB * FACTOR_PLACES[step])
             for pair in range(LINK_TILES // 2):
-                bank = take(sum_banks)
+                bank = take(ring)
                 if t == LAST:
                     w = 2 * t + pair
                     product(bank[:], weights(w, 1), plane[:, P * w : P * (w + 1)], words1[:, halves[half]].bitcast(FP8X4), scale1[:, halves[half]])
@@ -254,13 +258,13 @@ def tile_list_woven_link_features_kernel(
             return wb_dealt[:, P // 2 * first : P // 2 * (first + count)].bitcast(FP4X4)
 
         def both_factors(step):
-            b = factors("b", B_FACTORS, b_weights, wb_plane_dealt, step)
-            return factors("a", A_FACTORS, a_weights, wa_plane, step), b
+            b = factors("b", B_FACTORS, b_banks, b_weights, wb_plane_dealt, step)
+            return factors("a", A_FACTORS, a_banks, a_weights, wa_plane, step), b
 
         h1 = [placed("h1_%d" % t, [P, S], F32, (STREAMS, gate2_bytes(2), STREAMS + 8 * KIB, STREAMS + 8 * KIB)[t]) for t in range(PACK)]
         gated1 = [placed("gated1_%d" % t, [P, S], F32, (a_bytes(1, 1), a_bytes(1, 0), a_bytes(2, 0))[t]) for t in range(LAST)]
         product_bytes = (
-            gate2_bytes(2), gate2_bytes(3), STREAMS + 12 * KIB, gate1_bytes(0), STREAMS, gate1_bytes(1), gate2_bytes(2), gate1_bytes(2),
+            gate2_bytes(2), gate2_bytes(3), H2_LAST, gate1_bytes(0), STREAMS, gate1_bytes(1), gate2_bytes(2), gate1_bytes(2),
         )
 
         def multiply(step):

@@ -37,8 +37,8 @@ Z_EDGES = (0, 256, 512, 1024, 1536, 2048)
 Z_FIRST = 768
 VECTOR_PAGE_EDGES = (0, 256, 384, 512, 1024, 1536)
 PAGE_EDGES = ((0, 768, 2048), (0, 768, 2048), (0, 384, 768, 1024, 1536, 2048))
-VECTOR_LAST_RESULT = 256
-CODE_EDGES = (0, 512, 1536, 2048)
+RESULT_EDGES = (0, 512, 1024, 1536, 1792, 2048)
+CODE_EDGES = (0, 512, 1536, 1792, 2048)
 
 KIB = 1024
 B_FACTORS = 0
@@ -147,10 +147,10 @@ def tile_list_woven_link_features_kernel(
         load_plane(wb_plane[:, :H], wbr_scales)
         gates2.append(load_gate("gate2_1", wg2, 1, gate2_bytes(1)))
         load_plane(wb_plane[:, H:], wbi_scales)
+        wai_raw = [load_weight("wai_raw0", wai, page_bytes(2), *WAI_PIECES[0])]
         wb = kept("wb", [P, 2, H // 2], I32)
         for i, words in enumerate((wbr_words, wbi_words)):
             nc.sync.dma_start(wb[:, i, :], words[0].bitcast(I32))
-        wai_raw = [load_weight("wai_raw0", wai, page_bytes(2), *WAI_PIECES[0])]
         wai_raw.append(load_weight("wai_raw1", wai, H2_LAST - KIB, *WAI_PIECES[1]))
         gates2.extend(load_gate("gate2_%d" % t, wg2, t, gate2_bytes(t)) for t in range(2, PACK))
         list3 = load_list("list3", offs3)
@@ -189,7 +189,7 @@ def tile_list_woven_link_features_kernel(
         wsp_dealt = deal(nc.vector.tensor_copy, kept("wsp_dealt", [P, H], I32), wsp[:], I32, "p (t a b) -> p t a b", "p (a t b) -> p t a b", t=PACK, b=RUN)
         scale2 = gather(kept("scale2", [P, S], U8), tab2_plane, list2)
         words2 = gather(kept("words2", [P, S], U32), tab2, list2)
-        wsp_plane_dealt = deal(nc.vector.tensor_copy, kept("wsp_plane_dealt", [P, H], U8), wsp_plane[:], U16, "p (t a) -> p t a", "p (a t) -> p t a", t=PACK)
+        wsp_plane_dealt = deal(nc.vector.tensor_copy, kept("wsp_plane_dealt", [P, H], U8), wsp_plane[:], U16, "p (t g a) -> p g t a", "p (g a t) -> p g t a", t=PACK, a=8)
         words1 = gather(placed("words1", [P, S], U32, WORDS1), tab1, list1)
 
         h2 = [placed("h2_%d" % t, [P, S], F32, STREAMS + 4 * KIB * t if t < LAST else H2_LAST) for t in range(PACK)]
@@ -223,7 +223,7 @@ def tile_list_woven_link_features_kernel(
         for i in range(2):
             round_a_weight(1, wai_raw[i], WAI_PIECES[i][0] // (PACK * RUN), -1.0)
         wb_plane_dealt = deal(nc.scalar.copy, kept("wb_plane_dealt", [P, 2 * H], U8), wb_plane[:], U16, "p (t g a) -> p g t a", "p (g a t) -> p g t a", t=PACK, a=8)
-        wb_dealt = deal(nc.scalar.copy, kept("wb_dealt", [P, H], I32), wb[:].rearrange("p w c -> p (w c)"), U32, "p (t g a) -> p g t a", "p (g a t) -> p g t a", t=PACK, a=4)
+        wb_dealt = deal(nc.vector.tensor_copy, kept("wb_dealt", [P, H], I32), wb[:].rearrange("p w c -> p (w c)"), I32, "p (t g a) -> p g t a", "p (g a t) -> p g t a", t=PACK, a=4)
         wa_codes = kept("wa_codes", [P, 2 * H], U32)
         wa_plane = kept("wa_plane", [P, 2 * H], U8)
         nc.vector.quantize_mx(wa_codes[:].bitcast(FP8X4), wa_plane[:], wa_bf)
@@ -403,12 +403,8 @@ def tile_list_woven_link_features_kernel(
             nc.vector.quantize_mx(y_codes[:, cols].bitcast(FP8X4), y_plane[SCALE_ROWS * g :, first : first + cols.stop - cols.start], rounded)
 
         code_stores = pieces(CODE_EDGES)
-        for cols in pieces(range(0, T2 + 1, BANK)):
-            if cols.stop < T2:
-                quantise_result(nc.vector.tensor_copy, cols)
-            else:
-                quantise_result(nc.vector.tensor_copy, slice(cols.start, cols.start + VECTOR_LAST_RESULT))
-                quantise_result(nc.scalar.copy, slice(cols.start + VECTOR_LAST_RESULT, T2))
+        for cols in pieces(RESULT_EDGES):
+            quantise_result(nc.scalar.copy if cols.stop == T2 else nc.vector.tensor_copy, cols)
             if cols.stop == code_stores[0].stop:
                 stored = code_stores.pop(0)
                 nc.sync.dma_start(out_words[:, stored], y_codes[:, stored].bitcast(I32))

@@ -148,10 +148,10 @@ def tile_list_woven_link_features_kernel(
         gates2.append(load_gate("gate2_1", wg2, 1, gate2_bytes(1)))
         load_plane(wb_plane[:, H:], wbi_scales)
         wai_raw = [load_weight("wai_raw0", wai, page_bytes(2), *WAI_PIECES[0])]
+        wai_raw.append(load_weight("wai_raw1", wai, H2_LAST - KIB, *WAI_PIECES[1]))
         wb = kept("wb", [P, 2, H // 2], I32)
         for i, words in enumerate((wbr_words, wbi_words)):
             nc.sync.dma_start(wb[:, i, :], words[0].bitcast(I32))
-        wai_raw.append(load_weight("wai_raw1", wai, H2_LAST - KIB, *WAI_PIECES[1]))
         gates2.extend(load_gate("gate2_%d" % t, wg2, t, gate2_bytes(t)) for t in range(2, PACK))
         list3 = load_list("list3", offs3)
         gates1 = [load_gate("gate1_0", wg1, 0, gate1_bytes(0))]
@@ -258,8 +258,8 @@ def tile_list_woven_link_features_kernel(
             return wb_dealt[:, P // 2 * first : P // 2 * (first + count)].bitcast(FP4X4)
 
         def both_factors(step):
-            b = factors("b", B_FACTORS, b_banks, b_weights, wb_plane_dealt, step)
-            return factors("a", A_FACTORS, a_banks, a_weights, wa_plane, step), b
+            a = factors("a", A_FACTORS, a_banks, a_weights, wa_plane, step)
+            return a, factors("b", B_FACTORS, b_banks, b_weights, wb_plane_dealt, step)
 
         h1 = [placed("h1_%d" % t, [P, S], F32, (STREAMS, gate2_bytes(2), STREAMS + 8 * KIB, STREAMS + 8 * KIB)[t]) for t in range(PACK)]
         gated1 = [placed("gated1_%d" % t, [P, S], F32, (a_bytes(1, 1), a_bytes(1, 0), a_bytes(2, 0))[t]) for t in range(LAST)]

@@ -38,7 +38,7 @@ Z_FIRST = 768
 VECTOR_PAGE_EDGES = (0, 256, 384, 512, 1024, 1536)
 PAGE_EDGES = ((0, 768, 2048), (0, 768, 2048), (0, 384, 768, 1024, 1536, 2048))
 RESULT_EDGES = (0, 512, 1024, 1536, 1792, 2048)
-CODE_EDGES = (0, 512, 1536, 1792, 2048)
+CODE_EDGES = (0, 512, 1536, 2048)
 
 KIB = 1024
 B_FACTORS = 0
@@ -137,17 +137,17 @@ def tile_list_woven_link_features_kernel(
         list2 = load_list("list2", offs2)
         load_plane(tab2_plane, tab2_scales)
         tab2 = load_e4m3_words(placed("tab2", [P, T], I32, page_bytes(0)), tab2_words)
-        tab1 = load_e4m3_words(kept("tab1", [P, T], I32), tab_words)
         load_plane(wsp_plane, wsp_scales)
+        tab1 = load_e4m3_words(kept("tab1", [P, T], I32), tab_words)
         list1 = load_list("list1", offs)
-        gates2 = [load_gate("gate2_0", wg2, 0, gate2_bytes(0))]
         list4 = load_list("list4", offs4)
-        load_plane(tab_plane, tab_scales)
+        gates2 = [load_gate("gate2_0", wg2, 0, gate2_bytes(0))]
         war_raw = load_weight("war_raw", war, page_bytes(LAST), 0, H)
-        load_plane(wb_plane[:, :H], wbr_scales)
+        load_plane(tab_plane, tab_scales)
         gates2.append(load_gate("gate2_1", wg2, 1, gate2_bytes(1)))
-        load_plane(wb_plane[:, H:], wbi_scales)
+        load_plane(wb_plane[:, :H], wbr_scales)
         wai_raw = [load_weight("wai_raw0", wai, page_bytes(2), *WAI_PIECES[0])]
+        load_plane(wb_plane[:, H:], wbi_scales)
         wai_raw.append(load_weight("wai_raw1", wai, H2_LAST - KIB, *WAI_PIECES[1]))
         wb = kept("wb", [P, 2, H // 2], I32)
         for i, words in enumerate((wbr_words, wbi_words)):
@@ -200,8 +200,6 @@ def tile_list_woven_link_features_kernel(
                 product(bank[:], wsp_dealt[:, rows].bitcast(FP8X4), wsp_plane_dealt[:, rows], words2[:, cols].bitcast(FP8X4), scale2[:, cols])
                 nc.scalar.copy(h2[t][:, cols], bank[:])
 
-        b_banks, a_banks = sum_banks[-2:], sum_banks[:-2]
-
         pages = [placed("page%d" % t, [P, T2], F32, page_bytes(t)) for t in range(PACK)]
 
         def gate_and_scatter(page, offsets, gated, stream, gate):
@@ -231,11 +229,11 @@ def tile_list_woven_link_features_kernel(
             gated = placed("gated2_last", [P, S], F32, B_FACTORS + 12 * KIB) if t == LAST else h2[t]
             gate_and_scatter(pages[t], list4, gated, h2[t], gates2[t])
 
-        def factors(name, offset, ring, weights, plane, step):
+        def factors(name, offset, weights, plane, step):
             t, half = divmod(step, 2)
             tile = placed("%s_%d" % (name, step), [P, 2, HALF], F32, offset + 4 * KIB * FACTOR_PLACES[step])
             for pair in range(LINK_TILES // 2):
-                bank = take(ring)
+                bank = take(sum_banks)
                 if t == LAST:
                     w = 2 * t + pair
                     product(bank[:], weights(w, 1), plane[:, P * w : P * (w + 1)], words1[:, halves[half]].bitcast(FP8X4), scale1[:, halves[half]])
@@ -258,8 +256,7 @@ def tile_list_woven_link_features_kernel(
             return wb_dealt[:, P // 2 * first : P // 2 * (first + count)].bitcast(FP4X4)
 
         def both_factors(step):
-            a = factors("a", A_FACTORS, a_banks, a_weights, wa_plane, step)
-            return a, factors("b", B_FACTORS, b_banks, b_weights, wb_plane_dealt, step)
+            return factors("a", A_FACTORS, a_weights, wa_plane, step), factors("b", B_FACTORS, b_weights, wb_plane_dealt, step)
 
         h1 = [placed("h1_%d" % t, [P, S], F32, (STREAMS, gate2_bytes(2), STREAMS + 8 * KIB, STREAMS + 8 * KIB)[t]) for t in range(PACK)]
         gated1 = [placed("gated1_%d" % t, [P, S], F32, (a_bytes(1, 1), a_bytes(1, 0), a_bytes(2, 0))[t]) for t in range(LAST)]

@@ -35,8 +35,8 @@ WAI_PIECES = ((0, 256), (256, 256))
 STORE_EDGES = (0, 256, 512, 1024, 2048)
 Z_EDGES = (0, 256, 512, 1024, 1536, 2048)
 Z_FIRST = 768
-VECTOR_PAGE_EDGES = (0, 256, 384, 512, 1024, 1536)
-PAGE_EDGES = ((0, 768, 2048), (0, 768, 2048), (0, 384, 768, 1024, 1536, 2048))
+VECTOR_PAGE_EDGES = (0, 256, 512, 1024, 1536)
+PAGE_EDGES = ((0, 768, 2048), (0, 768, 2048), (0, 256, 768, 1024, 1536, 2048))
 RESULT_EDGES = (0, 512, 1024, 1536, 1792, 2048)
 CODE_EDGES = (0, 512, 1536, 2048)
 
@@ -329,9 +329,6 @@ def tile_list_woven_link_features_kernel(
         for t in range(LAST):
             for cols in pieces(PAGE_EDGES[t]):
                 round_page(nc.scalar, t, cols)
-        wo_codes = placed("wo_codes", [P, N], U32, a_bytes(LAST, 1))
-        wo_plane = placed("wo_plane", [P, N], U8, a_bytes(LAST, 1) + 4 * N)
-        nc.vector.quantize_mx(wo_codes[:].bitcast(FP8X4), wo_plane[:], wo_bf[:])
         nc.vector.tensor_tensor(pages[LAST][:].indirect(list3[:]), h1[LAST][:], gates1[LAST][:], MULT)
         round_page(nc.scalar, LAST, slice(VECTOR_PAGE_EDGES[-1], T2))
 
@@ -371,7 +368,11 @@ def tile_list_woven_link_features_kernel(
         stores = pieces(STORE_EDGES)
         single_rows = [range(t, t + 1) for t in range(PACK)]
         row_pairs = [range(t, t + 2) for t in range(0, PACK, 2)]
-        quantise_z(z_cols[0], VECTOR_PAGE_EDGES[2])
+        round_page(nc.vector, LAST, vector_rounds.pop(0))
+        wo_codes = placed("wo_codes", [P, N], U32, gate1_bytes(LAST))
+        wo_plane = placed("wo_plane", [P, N], U8, gate1_bytes(LAST) + 4 * N)
+        nc.vector.quantize_mx(wo_codes[:].bitcast(FP8X4), wo_plane[:], wo_bf[:])
+        quantise_z(z_cols[0], z_cols[0].stop)
         for c, row_sets in enumerate((single_rows, row_pairs, single_rows)):
             if c > 0:
                 quantise_z(z_cols[c], z_cols[c].stop)

from contextlib import ExitStack

import concourse.mybir as mybir
from concourse.masks import make_identity

K, T, S, H, T2, N = 512, 2048, 1024, 512, 2048, 512
FLOPS = 2 * K * H * S * 5 + 2 * H * N * T2

F32 = mybir.dt.float32
BF16 = mybir.dt.bfloat16
I32 = mybir.dt.int32
U32 = mybir.dt.uint32
U16 = mybir.dt.uint16
U8 = mybir.dt.uint8
FP8X4 = mybir.dt.float8_e4m3fn_x4
FP4X4 = mybir.dt.float4_e2m1fn_x4
COPY = mybir.ActivationFunctionType.Copy
MULT = mybir.AluOpType.mult
ADD = mybir.AluOpType.add

P = 128
PACK = 4
LAST = PACK - 1
RUN = 2
QUADRANTS = 4
QUADRANT = P // QUADRANTS
QUADRANT_ORDER = (0, 2, 1, 3)
SCALE_ROWS = 4
BANK = 512
LIST_COLS = S // 16
HALF = S // 2
LINK_TILES = HALF // P
WAI_PIECES = ((0, 256), (256, 256))

STORE_EDGES = (0, 256, 512, 1024, 2048)
Z_EDGES = (0, 256, 512, 1024, 1536, 2048)
Z_FIRST = 768
VECTOR_PAGE_EDGES = (0, 256, 512, 1024, 1536)
PAGE_EDGES = ((0, 768, 2048), (0, 768, 2048), (0, 256, 768, 1024, 1536, 2048))
RESULT_EDGES = (0, 512, 1024, 1536, 1792, 2048)
CODE_EDGES = (0, 512, 1536, 2048)

KIB = 1024
B_FACTORS = 0
A_FACTORS = 32 * KIB
FACTOR_PLACES = (0, 1, 2, 0, 1, 5, 6, 7)
STREAMS = 64 * KIB
PAGES = 80 * KIB
PAGE_ORDER = (0, 3, 2, 1)
H2_LAST = 112 * KIB
GATES2 = (156 * KIB, 116 * KIB, 120 * KIB, 124 * KIB)
GATES1 = 128 * KIB
GATE1_ORDER = (1, 0, 2, 3)
WA_ROUNDED = 144 * KIB
WORDS1 = 152 * KIB


def pieces(edges):
    return [slice(first, end) for first, end in zip(edges, edges[1:])]


def tile_list_woven_link_features_kernel(
    tc, tab_words, tab_scales, tab2_words, tab2_scales, offs, offs2, offs3, offs4, war, wai,
    wbr_words, wbr_scales, wbi_words, wbi_scales, wsp_words, wsp_scales, wg1, wg2, gain, wo,
    out_0, out_1, out_2,
):
    nc = tc.nc
    with ExitStack() as ctx:
        lists = ctx.enter_context(tc.tile_pool(name="lists", bufs=1))
        keep = ctx.enter_context(tc.tile_pool(name="keep", bufs=1))
        shared = ctx.enter_context(tc.tile_pool(name="shared", bufs=1))
        psum = ctx.enter_context(tc.psum_pool(name="psum", bufs=1))

        def placed(name, shape, dtype, offset):
            return shared.tile(shape, dtype, name=name, align_bytes=64, offset=offset)

        def kept(name, shape, dtype):
            return keep.tile(shape, dtype, name=name, align_bytes=64)

        def page_bytes(t):
            return PAGES + 8 * KIB * PAGE_ORDER.index(t)

        def a_bytes(t, half):
            return A_FACTORS + 8 * KIB * t + 4 * KIB * half

        def gate2_bytes(t):
            return GATES2[t]

        def gate1_bytes(t):
            return GATES1 + 4 * KIB * GATE1_ORDER.index(t)

        def load_list(name, offsets):
            tile = lists.tile([P, LIST_COLS], U16, name=name)
            nc.sync.dma_start(tile[:], offsets)
            return tile

        def zeroed_plane(name, width, engine):
            plane = kept(name, [P, width], U8)
            engine.memset(plane[:].bitcast(I32), 0)
            return plane

        def scale_rows(scales, q):
            return scales[0, SCALE_ROWS * q : SCALE_ROWS * (q + 1), :].bitcast(I32)

        def load_plane(plane, scales):
            for q in QUADRANT_ORDER:
                nc.sync.dma_start(plane[QUADRANT * q : QUADRANT * q + SCALE_ROWS, :].bitcast(I32), scale_rows(scales, q))

        def load_e4m3_words(tile, words):
            nc.sync.dma_start(tile[:], words[0].rearrange("p c i -> p (c i)").bitcast(I32))
            return tile

        def dealt_rows(w, t):
            return w.rearrange("(a t b) j -> t a b j", t=PACK, b=RUN)[t]

        def load_gate(name, wg, t, offset):
            tile = placed(name, [P, S], F32, offset)
            for q in QUADRANT_ORDER:
                nc.sync.dma_start(tile[QUADRANT * q : QUADRANT * (q + 1)], dealt_rows(wg, t))
            return tile

        def load_gain(t, tile):
            nc.sync.dma_start(tile[:], gain.rearrange("(a t b o) -> t a b o", t=PACK, b=RUN, o=1)[t])
            return tile

        def load_weight(name, w, offset, first, width):
            raw = placed(name, [P, PACK, width], F32, offset)
            nc.sync.dma_start(raw[:], w.rearrange("(p i) c -> p i c", i=PACK)[:, :, first : first + width])
            return raw

        tab2_plane = zeroed_plane("tab2_plane", T, nc.gpsimd)
        wsp_plane = zeroed_plane("wsp_plane", H, nc.gpsimd)
        tab_plane = zeroed_plane("tab_plane", T, nc.gpsimd)
        wb_plane = zeroed_plane("wb_plane", 2 * H, nc.gpsimd)

        wsp = load_e4m3_words(kept("wsp", [P, H], I32), wsp_words)
        list2 = load_list("list2", offs2)
        load_plane(tab2_plane, tab2_scales)
        tab2 = load_e4m3_words(placed("tab2", [P, T], I32, page_bytes(0)), tab2_words)
        load_plane(wsp_plane, wsp_scales)
        tab1 = load_e4m3_words(kept("tab1", [P, T], I32), tab_words)
        list1 = load_list("list1", offs)
        list4 = load_list("list4", offs4)
        gates2 = [load_gate("gate2_0", wg2, 0, gate2_bytes(0))]
        war_raw = load_weight("war_raw", war, page_bytes(LAST), 0, H)
        load_plane(tab_plane, tab_scales)
        gates2.append(load_gate("gate2_1", wg2, 1, gate2_bytes(1)))
        load_plane(wb_plane[:, :H], wbr_scales)
        wai_raw = [load_weight("wai_raw0", wai, page_bytes(2), *WAI_PIECES[0])]
        load_plane(wb_plane[:, H:], wbi_scales)
        wai_raw.append(load_weight("wai_raw1", wai, H2_LAST - KIB, *WAI_PIECES[1]))
        wb = kept("wb", [P, 2, H // 2], I32)
        for i, words in enumerate((wbr_words, wbi_words)):
            nc.sync.dma_start(wb[:, i, :], words[0].bitcast(I32))
        gates2.extend(load_gate("gate2_%d" % t, wg2, t, gate2_bytes(t)) for t in range(2, PACK))
        list3 = load_list("list3", offs3)
        gates1 = [load_gate("gate1_0", wg1, 0, gate1_bytes(0))]
        wo_raw = kept("wo_raw", [P, PACK, N], F32)
        for t in range(PACK):
            nc.sync.dma_start(wo_raw[:, t, :], dealt_rows(wo, t))
        gates1.append(load_gate("gate1_1", wg1, 1, gate1_bytes(1)))
        gains = {t: load_gain(t, kept("gain%d" % t, [P, 1], F32)) for t in (0, LAST)}
        gates1.extend(load_gate("gate1_%d" % t, wg1, t, gate1_bytes(t)) for t in range(2, PACK))

        banks = [psum.tile([P, BANK], F32, name="bank%d" % b) for b in range(8)]
        sum_banks, turn_banks = banks[:6], banks[6:]
        ident = keep.tile([P, P], F32)
        make_identity(nc, ident[:])

        def take(ring):
            bank = ring.pop(0)
            ring.append(bank)
            return bank

        def gather(picked, table, offsets):
            nc.vector.tensor_copy(picked[:], table[:].bitcast(picked.dtype).indirect(offsets[:]))
            return picked

        def product(out, still, still_plane, moving, moving_plane):
            nc.tensor.matmul_mx(out, lhsT=still, lhsT_scale=still_plane, rhs=moving, rhs_scale=moving_plane, start=True, stop=True)

        def deal(copy, dealt, raw, unit, dealt_form, raw_form, **sizes):
            copy(dealt[:].bitcast(unit).rearrange(dealt_form, **sizes), raw.bitcast(unit).rearrange(raw_form, **sizes))
            return dealt

        halves = pieces((0, HALF, S))
        whole = slice(0, S)

        wsp_dealt = deal(nc.vector.tensor_copy, kept("wsp_dealt", [P, H], I32), wsp[:], I32, "p (t a b) -> p t a b", "p (a t b) -> p t a b", t=PACK, b=RUN)
        scale2 = gather(kept("scale2", [P, S], U8), tab2_plane, list2)
        words2 = gather(kept("words2", [P, S], U32), tab2, list2)
        wsp_plane_dealt = deal(nc.vector.tensor_copy, kept("wsp_plane_dealt", [P, H], U8), wsp_plane[:], U16, "p (t g a) -> p g t a", "p (g a t) -> p g t a", t=PACK, a=8)
        words1 = gather(placed("words1", [P, S], U32, WORDS1), tab1, list1)

        h2 = [placed("h2_%d" % t, [P, S], F32, STREAMS + 4 * KIB * t if t < LAST else H2_LAST) for t in range(PACK)]
        for t in range(PACK):
            rows = slice(t * P, (t + 1) * P)
            for cols in halves:
                bank = take(sum_banks)
                product(bank[:], wsp_dealt[:, rows].bitcast(FP8X4), wsp_plane_dealt[:, rows], words2[:, cols].bitcast(FP8X4), scale2[:, cols])
                nc.scalar.copy(h2[t][:, cols], bank[:])

        pages = [placed("page%d" % t, [P, T2], F32, page_bytes(t)) for t in range(PACK)]

        def gate_and_scatter(page, offsets, gated, stream, gate):
            nc.gpsimd.tensor_tensor(gated[:], stream[:], gate[:], MULT)
            nc.vector.tensor_copy(page[:].indirect(offsets[:]), gated[:])

        nc.vector.tensor_tensor(pages[0][:].indirect(list4[:]), h2[0][:], gates2[0][:], MULT)
        scale1 = gather(kept("scale1", [P, S], U8), tab_plane, list1)

        wa_bf = placed("wa_bf", [P, 2 * PACK * H], BF16, WA_ROUNDED)[:]
        wa_places = wa_bf.rearrange("p (t w a b i) -> p w t a i b", t=PACK, w=2, b=RUN, i=PACK)

        def round_a_weight(w, raw, first, sign):
            src = raw[:].rearrange("p i (a t b) -> p t a i b", t=PACK, b=RUN)
            for t in range(PACK):
                nc.scalar.activation(wa_places[:, w, t, first : first + src.shape[2]], src[:, t], COPY, scale=sign)

        round_a_weight(0, war_raw, 0, 1.0)
        for i in range(2):
            round_a_weight(1, wai_raw[i], WAI_PIECES[i][0] // (PACK * RUN), -1.0)
        wb_plane_dealt = deal(nc.scalar.copy, kept("wb_plane_dealt", [P, 2 * H], U8), wb_plane[:], U16, "p (t g a) -> p g t a", "p (g a t) -> p g t a", t=PACK, a=8)
        wb_dealt = deal(nc.vector.tensor_copy, kept("wb_dealt", [P, H], I32), wb[:].rearrange("p w c -> p (w c)"), I32, "p (t g a) -> p g t a", "p (g a t) -> p g t a", t=PACK, a=4)
        wa_codes = kept("wa_codes", [P, 2 * H], U32)
        wa_plane = kept("wa_plane", [P, 2 * H], U8)
        nc.vector.quantize_mx(wa_codes[:].bitcast(FP8X4), wa_plane[:], wa_bf)
        for t in range(1, PACK):
            gated = placed("gated2_last", [P, S], F32, B_FACTORS + 12 * KIB) if t == LAST else h2[t]
            gate_and_scatter(pages[t], list4, gated, h2[t], gates2[t])

        def factors(name, offset, weights, plane, step):
            t, half = divmod(step, 2)
            tile = placed("%s_%d" % (name, step), [P, 2, HALF], F32, offset + 4 * KIB * FACTOR_PLACES[step])
            for pair in range(LINK_TILES // 2):
                bank = take(sum_banks)
                if t == LAST:
                    w = 2 * t + pair
                    product(bank[:], weights(w, 1), plane[:, P * w : P * (w + 1)], words1[:, halves[half]].bitcast(FP8X4), scale1[:, halves[half]])
                    nc.scalar.copy(tile[:, pair, :], bank[:])
                    continue
                for lt in range(2):
                    links = slice(HALF * half + P * (2 * pair + lt), HALF * half + P * (2 * pair + lt + 1))
                    product(
                        bank[:, 2 * P * lt : 2 * P * (lt + 1)], words1[:, links].bitcast(FP8X4), scale1[:, links],
                        weights(2 * t, 2), plane[:, 2 * P * t : 2 * P * (t + 1)],
                    )
                places = tile[:, :, 2 * P * pair : 2 * P * (pair + 1)].rearrange("p i (lt m) -> p lt i m", lt=2)
                nc.scalar.copy(places, bank[:].rearrange("p (lt i m) -> p lt i m", lt=2, i=2))
            return tile

        def a_weights(first, count):
            return wa_codes[:, P * first : P * (first + count)].bitcast(FP8X4)

        def b_weights(first, count):
            return wb_dealt[:, P // 2 * first : P // 2 * (first + count)].bitcast(FP4X4)

        def both_factors(step):
            return factors("a", A_FACTORS, a_weights, wa_plane, step), factors("b", B_FACTORS, b_weights, wb_plane_dealt, step)

        h1 = [placed("h1_%d" % t, [P, S], F32, (STREAMS, gate2_bytes(2), STREAMS + 8 * KIB, STREAMS + 8 * KIB)[t]) for t in range(PACK)]
        gated1 = [placed("gated1_%d" % t, [P, S], F32, (a_bytes(1, 1), a_bytes(1, 0), a_bytes(2, 0))[t]) for t in range(LAST)]
        product_bytes = (
            gate2_bytes(2), gate2_bytes(3), H2_LAST, gate1_bytes(0), STREAMS, gate1_bytes(1), gate2_bytes(2), gate1_bytes(2),
        )

        def multiply(step):
            a, b = factor_tiles[step]
            products = placed("products%d" % step, [P, 2, HALF], F32, product_bytes[step])
            nc.gpsimd.tensor_tensor(*(x[:].rearrange("p i c -> p (i c)") for x in (products, a, b)), MULT)
            return products

        def turn(step, products):
            t, half = divmod(step, 2)
            bank = take(turn_banks)
            for lt in range(LINK_TILES):
                for i in range(2):
                    nc.tensor.matmul(
                        bank[:, lt * P : (lt + 1) * P], lhsT=products[:, i, lt * P : (lt + 1) * P], rhs=ident[:],
                        start=(i == 0), stop=(i == 1), is_transpose=True,
                    )
            nc.scalar.copy(h1[t][:, halves[half]], bank[:])

        steps = 2 * PACK
        unturned = []
        factor_tiles = [both_factors(step) for step in range(2)]
        for step in range(steps):
            if step + 2 < steps:
                factor_tiles.append(both_factors(step + 2))
            products = multiply(step)
            if step // 2 < LAST:
                turn(step, products)
            else:
                unturned.append(products)
            if step % 2 == 0 and step > 0:
                t = step // 2 - 1
                gate_and_scatter(pages[t], list3, gated1[t], h1[t], gates1[t])

        for cols, products in zip(halves, unturned):
            nc.gpsimd.tensor_tensor(h1[LAST][:, cols], products[:, 0, :], products[:, 1, :], ADD)
        for t in (1, 2):
            gains[t] = load_gain(t, placed("gain%d" % t, [P, 1], F32, a_bytes(2, 1) + 64 * t))

        wo_bf = placed("wo_bf", [P, PACK * N], BF16, WORDS1)
        dst = wo_bf[:].rearrange("p (t m i) -> p m t i", t=PACK, i=PACK)
        src = wo_raw[:].rearrange("p i (m t) -> p m t i", t=PACK)
        for ms in pieces((0, P // 2, P)):
            nc.scalar.copy(dst[:, ms], src[:, ms])

        z_first = placed("z_first", [P, PACK * Z_FIRST], BF16, STREAMS)
        z_main = placed("z_main", [P, PACK * (T2 - Z_FIRST)], BF16, gate1_bytes(2) - 2 * PACK * (T2 - Z_FIRST))

        def z_places(cols):
            if cols.stop <= Z_FIRST:
                return z_first[:, PACK * cols.start : PACK * cols.stop]
            return z_main[:, PACK * (cols.start - Z_FIRST) : PACK * (cols.stop - Z_FIRST)]

        def round_page(engine, t, cols):
            page, factor = pages[t][:, cols], gains[t][:]
            z = z_places(cols).rearrange("p (m t) -> p m t", t=PACK)
            if engine is nc.vector:
                nc.vector.tensor_scalar(z[:, :, t], page, factor, None, MULT)
            elif t == 2 and cols.start < VECTOR_PAGE_EDGES[-1]:
                twice = page.unsqueeze(2).to_broadcast([P, cols.stop - cols.start, 2])
                nc.scalar.activation(z[:, :, t : t + 2], twice, COPY, scale=factor)
            else:
                nc.scalar.activation(z[:, :, t], page, COPY, scale=factor)

        for t in range(LAST):
            for cols in pieces(PAGE_EDGES[t]):
                round_page(nc.scalar, t, cols)
        nc.vector.tensor_tensor(pages[LAST][:].indirect(list3[:]), h1[LAST][:], gates1[LAST][:], MULT)
        round_page(nc.scalar, LAST, slice(VECTOR_PAGE_EDGES[-1], T2))

        z_codes = kept("z_codes", [P, T2], U32)
        z_plane = kept("z_plane", [P, T2], U8)
        y_codes = kept("y_codes", [P, T2], U32)
        y_plane = kept("y_plane", [P, BANK], U8)
        out_rows = out_0.rearrange("(p t) m -> p t m", t=PACK)
        out_words = out_1[0].rearrange("p m t -> p (m t)").bitcast(I32)
        y_edges = (0, BANK, 2 * BANK, T2)
        ys = [placed("y%d" % i, [P, PACK, cols.stop - cols.start], F32, 4 * PACK * cols.start) for i, cols in enumerate(pieces(y_edges))]
        y_bf = placed("y_bf", [P, PACK * T2], BF16, STREAMS)

        def y_places(cols):
            i = min(cols.start // BANK, len(ys) - 1)
            return ys[i][:, :, cols.start - y_edges[i] : cols.stop - y_edges[i]]

        vector_rounds = pieces(sorted(VECTOR_PAGE_EDGES + (Z_FIRST,)))

        def quantise_z(cols, ahead):
            while vector_rounds and vector_rounds[0].start < ahead:
                round_page(nc.vector, LAST, vector_rounds.pop(0))
            for piece in pieces(sorted({cols.start, cols.stop} | ({Z_FIRST} if cols.start < Z_FIRST < cols.stop else set()))):
                nc.vector.quantize_mx(z_codes[:, piece].bitcast(FP8X4), z_plane[:, piece], z_places(piece))

        def last_product(rows, cols, empty):
            bank = take(banks)[:, : len(rows) * (cols.stop - cols.start)].rearrange("p (i m) -> p i m", i=len(rows))
            for i, t in enumerate(rows):
                channels = slice(t * P, (t + 1) * P)
                product(bank[:, i, :], wo_codes[:, channels].bitcast(FP8X4), wo_plane[:, channels], z_codes[:, cols].bitcast(FP8X4), z_plane[:, cols])
            empty(y_places(cols)[:, rows.start : rows.stop, :], bank)

        def store(queue, rows, cols):
            queue.dma_start(out_rows[:, rows.start : rows.stop, cols], y_places(cols)[:, rows.start : rows.stop, :])

        z_cols = pieces(Z_EDGES)
        stores = pieces(STORE_EDGES)
        single_rows = [range(t, t + 1) for t in range(PACK)]
        row_pairs = [range(t, t + 2) for t in range(0, PACK, 2)]
        round_page(nc.vector, LAST, vector_rounds.pop(0))
        wo_codes = placed("wo_codes", [P, N], U32, gate1_bytes(LAST))
        wo_plane = placed("wo_plane", [P, N], U8, gate1_bytes(LAST) + 4 * N)
        nc.vector.quantize_mx(wo_codes[:].bitcast(FP8X4), wo_plane[:], wo_bf[:])
        quantise_z(z_cols[0], z_cols[0].stop)
        for c, row_sets in enumerate((single_rows, row_pairs, single_rows)):
            if c > 0:
                quantise_z(z_cols[c], z_cols[c].stop)
            for rows in row_sets:
                last_product(rows, z_cols[c], nc.scalar.copy)
                store(nc.sync, rows, stores[c])
        for cols in z_cols[3:]:
            quantise_z(cols, cols.stop)
        left, right = z_cols[3:]
        for rows in single_rows[:2]:
            last_product(rows, left, nc.scalar.copy)
            last_product(rows, right, nc.scalar.copy)
            store(nc.scalar, rows, stores[3])
        last_product(single_rows[2], left, nc.scalar.copy)
        last_product(single_rows[3], left, nc.vector.tensor_copy)
        for rows in single_rows[2:]:
            last_product(rows, right, nc.scalar.copy)
            store(nc.scalar, rows, stores[3])

        groups = T2 // BANK

        def quantise_result(copy, cols):
            g, first = divmod(cols.start, BANK)
            rounded = y_bf[:, PACK * cols.start : PACK * cols.stop]
            copy(rounded.rearrange("p (c i t) -> p c t i", i=PACK, t=PACK), y_places(cols).rearrange("p t (c i) -> p c t i", i=PACK))
            nc.vector.quantize_mx(y_codes[:, cols].bitcast(FP8X4), y_plane[SCALE_ROWS * g :, first : first + cols.stop - cols.start], rounded)

        code_stores = pieces(CODE_EDGES)
        for cols in pieces(RESULT_EDGES):
            quantise_result(nc.scalar.copy if cols.stop == T2 else nc.vector.tensor_copy, cols)
            if cols.stop == code_stores[0].stop:
                stored = code_stores.pop(0)
                nc.sync.dma_start(out_words[:, stored], y_codes[:, stored].bitcast(I32))
        for q in range(QUADRANTS):
            packed = y_plane[QUADRANT * q : QUADRANT * q + SCALE_ROWS * groups, :].bitcast(I32)
            (nc.scalar, nc.sync)[q % 2].dma_start(scale_rows(out_2, q).rearrange("r (g c) -> g r c", g=groups), packed)
